import numpy as np, ml_dtypes
CORES = [5,29,101,125,133,157,229,253]
N = 8
BF = ml_dtypes.bfloat16
def gentries(a):
    return np.ascontiguousarray(a.reshape(8, 16, -1).transpose(0, 2, 1)).reshape(8, -1)
def gtable(e):
    e = np.asarray(e); return np.ascontiguousarray(e.reshape(8, -1, 16).transpose(0, 2, 1)).reshape(128, -1).astype(np.int32)
W, Q, L, C, S, ST, RO, TH = 2048, 16, 128, 64, 256, 2, 2, 9
K = Q * C
GM = (W - L) // (C - 1)
def val(rng, shape, even):
    if even: return rng.integers(0, 256, shape)
    return np.minimum(np.exp2(8.01 * rng.random(shape)).astype(np.int64) - 1, 255)
def items(rng, B, z, share, even):
    v = np.ascontiguousarray(B[np.arange(8)[None, :, None], z].transpose(0, 2 - 1, 3, 2))
    return np.where(rng.random(v.shape, dtype=np.float32) < share, val(rng, v.shape, even), v)
def parts(rng, even):
    per = rng.integers(7, 41, 8); V = rng.integers(0, 4, (8, 40)); ph = rng.integers(0, 40, (N, 8)); e = rng.integers(0, 40, (N, 8, Q)); G8 = np.arange(8)[None, :, None]
    B = np.repeat(val(rng, (8, 1, 16), even), 4, axis=1); B = np.where(rng.random(B.shape) < (0.6 if even else 0.75), val(rng, B.shape, even), B)
    z = V[G8, (np.arange(W) + ph[..., None]) % per[None, :, None]]
    z = np.where(rng.random(z.shape) < rng.choice(np.array([0.01, 0.02, 0.04, 0.06]), (N, 8, 1)), rng.integers(0, 4, z.shape), z)
    u = V[G8[..., None], (np.arange(L) + e[..., None]) % per[None, :, None, None]]
    u = np.where(rng.random(u.shape) < 0.015, rng.integers(0, 4, u.shape), u).reshape(N, 8, Q * L)
    T = items(rng, B, z, 0.08, even); P = items(rng, B, u, 0.08, even)
    eb = e[(np.arange(N)[:, None] + np.arange(RO)[None, :]) % N].transpose(0, 2, 1, 3)
    h = (ph[:, :, None, None] - eb).astype(np.int32)[..., None] + np.arange(W - L + 1, dtype=np.int32)
    hit = h % per.astype(np.int32)[None, :, None, None, None] == 0
    sc = rng.random(hit.shape, dtype=np.float32); f = rng.choice(np.array([0.02, 0.05, 0.15, 0.4], np.float32), (N, 8, 1, 1, 1))
    st = np.sort(np.argpartition(np.where(hit, sc * f, sc), C, axis=-1)[..., :C], axis=-1)
    x = rng.random((N, 8, Q, L)); y = rng.random((N, 8, 16, Q))
    if not even: x = x ** rng.choice(np.array([0.2, 1.0, 5.0]), (N, 8, Q, 1)); y = y ** rng.choice(np.array([0.3, 1.0, 4.0]), (N, 8, 1, Q))
    d = np.arange(L); wt = np.minimum(d + (x * (L - d)).astype(np.int64), L - 1)
    wt = np.where(rng.random(wt.shape) < 0.4, 0, wt)
    return T, P, wt, np.minimum((L * y).astype(np.int64), L - 1), np.ascontiguousarray(st).astype(np.int64)
def pack(T, P, wt, O, st):
    return {"txt": np.ascontiguousarray(T.reshape(N, 128, W)).astype(np.float32).astype(BF), "pat": np.ascontiguousarray(P.reshape(N, 128, Q * L)).astype(np.float32).astype(BF),
            "wit": np.ascontiguousarray(wt.reshape(N, 8, Q * L)).astype(np.int32), "prb": np.ascontiguousarray(O.reshape(N, 128, Q)).astype(np.int32),
            "cd": np.stack([gtable(a.reshape(8, RO * K)) for a in st])}
def runs(rng, n):
    gap = np.ones(C, np.int64); gap[0] = 0
    gap[1 + rng.permutation(C - 1)[:n - 1]] = 2 + rng.integers(0, GM - 1, n - 1)
    a = np.add.accumulate(gap); return a + int(rng.integers(0, W - L - int(a[-1]) + 1))
def still(rng, T, P, wt, O, g):
    X = rng.integers(0, 256, (1, 16, 1)); T[:, g] = X; P[:, g] = X; P[:, g, :, L - 1::L] = 255 - X
    wt[:, g] = 0; wt[:, g, :, 1] = L - 1; O[:, g] = rng.integers(0, L - 2, (N, 16, Q)); return X
def shares(rng, n):
    if rng.random() < 0.5:
        c = np.full(Q, n // Q); c[rng.permutation(Q)[:n - Q * (n // Q)]] += 1; return c
    c = np.ones(Q, np.int64); left = n - Q
    for p in rng.permutation(Q):
        k = min(C - 1, left); c[p] += k; left -= k
    return c
def setup_inputs(rng):
    return pack(*parts(rng, True))
def setup_inputs_spread(rng):
    return pack(*parts(rng, False))
def setup_inputs_ends(rng):
    cut = np.array([0, TH - 1, TH, 16]); row = np.arange(16)[:, None]
    def rec(n):
        v = 255 * (row < cut[rng.choice(4, (N, 8, 1, n), p=np.array([0.45, 0.3, 0.1, 0.15]))])
        return np.where(rng.random((N, 8, 1, n)) < 0.06, 255 * rng.integers(0, 2, (N, 8, 16, n)), v)
    T = rec(W); P = rec(Q * L); wt = (L - 1) * rng.integers(0, 2, (N, 8, Q, L)); O = (L - 1) * rng.integers(0, 2, (N, 8, 16, Q))
    O = np.where(rng.random(O.shape) < 0.1, rng.choice(np.array([1, L - 2]), O.shape), O)
    st = np.zeros((N, 8, RO, Q, C), np.int64); lo = np.arange(C); hi = W - L - lo[::-1]; last = np.concatenate([lo[:C - 2], np.array([W - 2 * L + 1, W - L])])
    for q in range(N):
        for g in range(8):
            for t in range(RO):
                for p in range(Q):
                    k = int(rng.integers(0, 4)); h = int(rng.integers(1, C))
                    if g == 7 or k == 2: st[q, g, t, p] = last
                    elif k == 0: st[q, g, t, p] = np.concatenate([lo[:h], hi[h:]])
                    elif k == 1: st[q, g, t, p] = np.concatenate([np.array([0, L - 1]), hi[2:]])
                    else: st[q, g, t, p] = np.concatenate([2 * lo[:h], W - L - 2 * lo[:C - h][::-1]])
    T[:, 7, :, :C + L] = 0; T[:, 7, :, W - 2 * L + 1] = 0; T[:, 7, :, W - L] = 255; T[:, 7, :, W - 1] = 255
    P[:, 7, :, 0::L] = 0; P[:, 7, :, L - 2::L] = 0; P[:, 7, :, L - 1::L] = 255
    wt[:, 7, :, 1] = L - 1; wt[:, 7, :, L - 1] = 0
    O[:, 7] = (L - 1) * rng.integers(0, 2, (N, 16, Q)); O[:, 7, 5] = 0; O[:, 7, 6] = L - 1
    return pack(T, P, wt, O, st)
def setup_inputs_corners(rng):
    T, P, wt, O, st = parts(rng, True); goal = (S, S + 1, S - 1, K, Q)
    for g in range(6):
        X = still(rng, T, P, wt, O, g)[0, :, 0]
        for q in range(N):
            for p in range(Q):
                if (g < 5 and rng.random() < 0.3) or (g == 5 and q % 2 == 0):
                    P[q, g, :, p * L + int(O[q, g, int(rng.choice(np.array([0, 7, 15]))), p])] = 255 - X
            for t in range(RO):
                c = shares(rng, S if g == 5 else goal[(g + q + t) % 5])
                for p in range(Q): st[q, g, t, p] = runs(rng, int(c[p]))
    X = still(rng, T, P, wt, O, 6); P[::2, 6, :, L - 2::L] = 255 - X; H = W // 2
    for q in range(N):
        for t in range(RO):
            for p in range(Q):
                s0 = int(rng.integers(0, H - L - C + 2)) if (q + t) % 2 == 0 else int(rng.integers(H, W - L - C + 2))
                st[q, 6, t, p] = s0 + np.arange(C)
    k = rng.integers(0, 3, (N, Q, L)); wt[:, 7] = np.where(k == 0, 0, np.where(k == 1, np.arange(L), L - 1))
    v = rng.choice(np.array([0, L - 1, L // 2, 3]), (2, N, 1, Q)); O[:, 7] = np.where(rng.random((N, 16, Q)) < 0.5, v[0], v[1])
    for q in range(N):
        for t in range(0, RO, 2):
            s0 = int(rng.integers(0, W - L - K + 2)); st[q, 7, t] = s0 + np.arange(K).reshape(Q, C)
    wt[0, 7, 0, 1] = L - 1; wt[0, 7, 1, 1] = 0; wt[0, 7, 2, 1] = L - 1; O[0, 7, :, 1] = 3 * rng.integers(0, 2, 16)
    tx, pt = T[0, 7], P[0, 7]; a, b = int(st[0, 7, 0, 1, 0]), int(st[0, 7, 0, 1, C - 1])
    for s in (a, b):
        for o in (0, 3): tx[:, s + o] = pt[:, L + o]
    pt[:, 2 * L - 2] = 255 - tx[:, a + L - 2]; pt[:, 2 * L - 1] = 255 - tx[:, b + L - 1]
    return pack(T, P, wt, O, st)
def setup_inputs_crowd(rng):
    T, P, wt, O, st = parts(rng, True)
    for g in range(8):
        if g % 2 == 0:
            still(rng, T, P, wt, O, g); o = int(rng.integers(0, L - 2)); O[:, g, 0] = o
            for q in range(N):
                if g % 4 == 2: O[q, g, 0, int(rng.integers(0, Q))] = (o + 1) % (L - 2)
                for t in range(RO): st[q, g, t] = runs(rng, S // Q)[None, :]
        else:
            D = int(rng.integers(8, min(28, GM) + 1)); z = int(rng.integers(0, D))
            X = rng.integers(0, 256, 16); Y = X.copy(); i = rng.permutation(16)[:TH]; Y[i] = 255 - Y[i]; XY = np.stack([X, Y], axis=1)
            h = rng.integers(0, 2, D); v = np.concatenate([h, h]); v[z] = 0; v[z + D] = 1
            P[:, g] = XY[:, v[np.arange(Q * L) % L % (2 * D)]]; wt[:, g] = 0
            o = rng.integers(0, L - 1, (N, 16, Q)); o = o + (o % D == z); o[:, 15] = z + D * rng.integers(0, 2, (N, Q)); O[:, g] = o
            for q in range(N):
                s0 = int(rng.integers(0, W - L - (C - 1) * D + 1)); st[q, g] = s0 + D * np.arange(C)
                u = v[(np.arange(W) - s0) % (2 * D)]
                if g % 4 == 3: u = np.where(rng.random(W) < 0.01, 1 - u, u)
                T[q, g] = XY[:, u]
    return pack(T, P, wt, O, st)
def check_inputs(d):
    bad = []
    for k, lo, hi in (("txt", 0, 255), ("pat", 0, 255), ("wit", 0, L - 1), ("prb", 0, L - 1), ("cd", 0, W - L)):
        v = np.asarray(d[k]).astype(np.float64)
        if not (np.min(v) >= lo and np.max(v) <= hi): bad.append("range of " + k)
        if np.any(v != np.floor(v)): bad.append("whole numbers of " + k)
    w = np.asarray(d["wit"]).astype(np.int64).reshape(N, 8, Q, L)
    if np.any((w != 0) & (w < np.arange(L))): bad.append("a witness of wit is 0 or at least its distance")
    s = np.stack([gentries(a) for a in d["cd"]]).astype(np.int64).reshape(N, 8, RO, Q, C)
    if np.any(s[..., 1:] <= s[..., :-1]): bad.append("rising starts of cd")
    return bad
def unlike(x, y):
    return np.add.reduce((x != y).astype(np.int64), axis=0) >= TH
def reference(txt, pat, wit, prb, cd):
    T = txt.astype(np.float32).astype(np.int64).reshape(N, 8, 16, W); P = pat.astype(np.float32).astype(np.int64).reshape(N, 8, 16, Q * L)
    wt = wit.astype(np.int64).reshape(N, 8, Q * L); O = prb.astype(np.int64).reshape(N, 8, 16, Q)
    st = np.stack([gentries(a) for a in cd]).astype(np.int64).reshape(N, 8, RO, K); pl = np.arange(K) // C
    for t in range(RO):
        for r in range(N):
            b = (r + t) % N
            for g in range(8):
                tx, pt, wv, ov, a = T[r, g], P[b, g], wt[b, g], O[b, g], st[r, g, t]
                live = np.arange(K)
                for stage in range(ST):
                    i, j = live[:-1], live[1:]; d = a[j] - a[i]
                    ok = (pl[i] == pl[j]) & (d < L); i, j, d = i[ok], j[ok], d[ok]
                    w = wv[pl[i] * L + d]; ok = w > 0; i, j, d, w = i[ok], j[ok], d[ok], w[ok]
                    y = tx[:, a[i] + w]; dead = np.zeros(K, bool)
                    dead[i[unlike(pt[:, pl[i] * L + w], y)]] = True
                    dead[j[unlike(pt[:, pl[j] * L + w - d], y)]] = True
                    live = live[~dead[live]]
                s = live[:S]
                if len(s) == 0: continue
                p = pl[s]; o = ov[:, p]
                bad = unlike(tx[:, a[s] + o], pt[:, p * L + o])
                fail = np.any(bad, axis=0); m = np.argmax(bad, axis=0); of = o[m, np.arange(len(s))]
                x = np.unique((a[s] + o[0])[~fail]); tx[:, x] = 255 - tx[:, x]
                d = a[s][1:] - a[s][:-1]; c = (p[1:] == p[:-1]) & fail[1:] & ~fail[:-1] & (of[1:] + d < L)
                place, first = np.unique((p[1:] * L + d)[c], return_index=True); wv[place] = (of[1:] + d)[c][first]
                who, first = np.unique(p[fail], return_index=True); mf = m[fail][first]
                for q, k in zip(who, mf): ov[:, q] = np.concatenate([ov[k:k + 1, q], ov[:k, q], ov[k + 1:, q]])
    return {"yt": T.reshape(N, 128, W).astype(np.float32).astype(BF), "yw": wt.astype(np.float32), "yo": O.reshape(N, 128, Q).astype(np.float32)}

@@ -1,0 +1,727 @@
+from concourse.bass import DstId, RemoteDMATransfer, IndirectOffsetOnAxis
+from concourse.mybir import AluOpType as AL, AxisListType, ActivationFunctionType as AF
+
+F, B, U, I = "float32", "bfloat16", "uint16", "int32"
+SIZE = {F: 4, B: 2, U: 2, I: 4}
+
+OWN = {"TX": (2080, B), "P0": (2048, B), "P1": (2048, B), "WP": (136, F), "WL": (128, F), "WR0": (2192, F), "WR1": (2192, F),
+       "DG": (2048, B), "GW": (1024, B), "Y": (1024, B), "NJ": (1024, B), "NI": (1024, B), "WN": (8800, B), "PX": (4096, B),
+       "NQ": (4096, B), "MO0": (160, U), "MO1": (160, U), "MI0": (160, U), "MI1": (160, U), "CD": (128, I), "WI": (128, I),
+       "OI": (16, I), "AR0": (512, B), "AR1": (512, B), "HL0": (128, B), "HL1": (128, B), "OO": (16, F)}
+SMALL = {
+    F: {"W0": 16, "O0": 32, "O1": 32, "KC": 32, "NR": 256, "N16": 128, "NM": 128, "ID32": 128,
+        "DUMP": 32, "NDU": 32, "RMK": 16, "C128": 16, "BT0": 128, "ZT0": 128, "BT1": 128, "ZT1": 128, "A0": 64, "A1": 64, "ND0": 64, "ND1": 64,
+        "NA0": 72, "NA1": 72, "DT": 64, "TP": 64, "LF": 72, "NN": 64, "ND2": 32, "AL1": 64, "T1": 64, "T2": 64, "KL": 64,
+        "TH": 64, "TM": 32, "ANY": 32, "XD": 32, "SE": 8, "TO": 16, "LS": 8, "RS": 384, "SC": 384, "FL": 384, "LM": 8, "TQ": 64, "RM": 8, "LX": 16, "L2": 16,
+        "RA": 128, "RB": 256},
+    B: {"OB0": 16, "OB1": 16, "ID": 128, "NID": 128, "IDB": 128, "ID4": 128, "NID4": 128, "BLK": 128, "BLM8": 128, "BL4": 128, "M2": 128, "TRI": 128,
+        "TRI2": 128, "M1": 128, "M3": 128, "K4": 128, "K5": 128, "HE": 128, "HO": 128, "HX": 128, "BD": 128, "NBD": 128, "BP": 128, "Z2": 144, "ZE": 144, "ZH": 144, "XS": 264, "BE": 128, "BO": 128, "X1": 128, "X2": 128, "X3": 128, "X4": 128, "X5": 128,
+        "Z": 144, "ZQ": 144, "ZP": 144, "MB": 128, "IX": 256, "C0": 64, "KJ": 72, "AL2": 64, "CUM": 64, "V0": 512, "V1": 512, "PO0": 272, "PO1": 272,
+        "SGE": 256, "SGS": 256, "OG": 256, "PR": 264, "DB": 256, "PEN": 256, "XX": 256, "BAD": 264, "UU": 256, "UT": 128,
+        "UD": 128, "EQ": 384, "MW": 384, "YY": 256, "LE": 264, "G0": 16, "G1": 16, "HH": 16, "E1": 256, "E2": 128, "FV": 256},
+    U: {"LB": 16, "L3": 24, "LV": 32, "OW0": 64, "OW1": 64, "OY": 64, "OJ": 64, "OP": 64, "OW2": 32, "OS": 32, "OTU": 256, "OPO": 256, "OPT": 16,
+        "PL": 16, "SX": 2, "OX": 16, "OA": 16},
+    I: {"KI": 8, "AI0": 64, "AI1": 64, "LO0": 64, "LO1": 64},
+}
+SCRATCH = {"AD0": ("dram", [32, 512], B), "AD1": ("dram", [32, 512], B)}
+PLACE = {}
+for _k, (_n, _d) in OWN.items():
+    SCRATCH[_k] = ("sbuf", [128, _n], _d)
+    PLACE[_k] = (_k, 0, _n, SIZE[_d])
+for _d, _t in SMALL.items():
+    _o = 0
+    for _k, _n in _t.items():
+        PLACE[_k] = ("pool_" + _d, _o, _n, SIZE[_d])
+        _o += (_n + 15) // 16 * 16
+    SCRATCH["pool_" + _d] = ("sbuf", [128, _o], _d)
+for _k in range(8):
+    SCRATCH["B%d" % _k] = ("psum", [128, 512], F)
+    PLACE["B%d" % _k] = ("B%d" % _k, 0, 512, 4)
+
+NDMA = 24
+SEMAPHORES = ["sv", "sa", "st", "sg", "ls", "rp", "rw", "rm0", "rm1", "ap", "aw", "am0", "am1"] + ["d%d" % k for k in range(NDMA)]
+BIG = 1.0e6
+CY, PE, WAKE, HOP = 1.04e-3, 0.55e-3, 0.1, 5.5
+
+
+def relays(topo, src, dst):
+    c = [x for x in topo.cores_of(src) if x != src and topo.may_write(x, dst)]
+    return [x for x in c if topo.die(x) == topo.die(src)] + [x for x in c if topo.die(x) != topo.die(src)]
+
+
+def relay_program(g, core, T, topo):
+    n = len(T.cores)
+    own = [c for c in topo.cores_of(core) if T.rank_of(c) is not None]
+    if not own:
+        return
+    src = own[0]
+    r = T.rank_of(src)
+    prv, nxt = T.cores[(r - 1) % n], T.cores[(r + 1) % n]
+    rl = relays(topo, src, prv)
+    if core not in rl:
+        return
+    k = rl.index(core)
+    wd = 2048 // len(rl)
+    ne = len(topo.engines(src, core))
+    tot = [0]
+
+    def hand(buf, sem, cnt, dst, rsem):
+        g.wait_ge(T.sem[sem], cnt)
+        rid, pid = topo.addr(dst, core)
+        g.remote_dma(buf, buf, T.sem[rsem], T.sem.ls, pid, rid, topo.mask(core, dst))
+        tot[0] += len(topo.engines(core, dst))
+
+    hand(T.P1[:, k * wd:(k + 1) * wd], "rp", ne // len(rl), prv, "ap")
+    if k == 1:
+        hand(T.WL[:], "rw", ne, prv, "aw")
+    if k == 0:
+        hand(T.MI0[:], "rm0", ne, prv, "am0")
+    if core == relays(topo, src, nxt)[0]:
+        hand(T.MI1[:], "rm1", ne, nxt, "am1")
+    g.wait_ge(T.sem.ls, tot[0])
+
+
+def rank_program(g, core, T, topo):
+    rank = T.rank_of(core)
+    if rank is None:
+        relay_program(g, core, T, topo)
+        return
+    n = len(T.cores)
+    prv, nxt = T.cores[(rank - 1) % n], T.cores[(rank + 1) % n]
+    ops = []
+    Q = {"v": g.vector, "a": g.scalar, "t": g.tensor, "g": g, "s": g.sync}
+
+    def R(name, a=None, b=None, s=1):
+        name, o, w, sz = PLACE[name]
+        a = o if a is None else a + o
+        b = o + w if b is None else b + o
+        if s == -1:
+            ap = T[name][:, b - 1::-1] if a == 0 else T[name][:, b - 1:a - 1:-1]
+        elif s == 1:
+            ap = T[name][:, a:b]
+        else:
+            return {"ap": T[name][:, a:b:s], "reg": [(name, a, b, s)], "n": (b - a + s - 1) // s, "sz": sz}
+        return {"ap": ap, "reg": [(name, a, b)], "n": b - a, "sz": sz}
+
+    def IND(win, off):
+        return {"ap": win["ap"].indirect(off["ap"]), "reg": win["reg"], "off": off["reg"], "n": 16 * off["n"], "sz": win["sz"]}
+
+    def val(x):
+        return x["ap"] if isinstance(x, dict) else x
+
+    def add(e, fn, rd, wr, kind="c", ext=None, hold=None, lat=0.0, after=None):
+        r_, w_ = [], []
+        rd = [x for x in rd if isinstance(x, dict)]
+        for x in rd:
+            r_ += x["reg"] + x.get("off", [])
+        for x in wr:
+            w_ += x["reg"]
+            r_ += x.get("off", [])
+        if hold is None:
+            m = max(x["n"] for x in rd + wr)
+            if "off" in wr[0]:
+                hold = 0.05 + 3.8 * m * CY
+            elif any("off" in x for x in rd):
+                hold = 0.06 + 1.56 * m * CY
+            elif e == "a":
+                hold = 0.05 + max(64, m) * CY
+            else:
+                hold = max(64, m * (0.5 if all(x["sz"] == 2 for x in rd + wr if x["n"] > 1) else 1)) * CY
+        ops.append({"e": e, "fn": fn, "r": r_, "w": w_, "k": kind, "ext": ext, "hold": hold, "lat": lat, "after": after})
+        return len(ops) - 1
+
+    chain = [None]
+
+    def tt(o, a, b, op):
+        two = "off" not in a and a["reg"][0][0][0] != "B" and b["reg"][0][0][0] != "B"
+        k = add("v", lambda: g.vector.tensor_tensor(val(o), val(a), val(b), op), [a, b], [o])
+        if two and o["n"] > 32:
+            ops[k]["hold"] *= 2
+        if op == AL.not_equal:
+            ops[k]["after"] = chain[0]
+            chain[0] = k
+
+    def ts(o, a, s1, op0, s2=None, op1=None):
+        if op1 is None:
+            return add("v", lambda: g.vector.tensor_scalar(val(o), val(a), val(s1), None, op0), [a, s1], [o])
+        return add("v", lambda: g.vector.tensor_scalar(val(o), val(a), val(s1), val(s2), op0, op1), [a, s1, s2], [o])
+
+    hints = []
+
+    def cp(o, a):
+        return add("v", lambda: g.vector.tensor_copy(val(o), val(a)), [a], [o])
+
+    def ms(o, c, eng="g"):
+        if eng == "g":
+            iota(o, [[0, o["n"]]], int(c), 0)
+        else:
+            add("v", lambda: g.vector.memset(val(o), c), [], [o])
+
+    def scan(o, d0, d1, init, op0, op1):
+        add("v", lambda: g.vector.tensor_tensor_scan(val(o), val(d0), val(d1), init, op0, op1), [d0, d1], [o])
+
+    def act(o, a, f=AF.Identity, bias=0.0, scale=1.0):
+        return add("a", lambda: g.scalar.activation(val(o), val(a), f, bias=val(bias), scale=val(scale)), [a, bias, scale], [o])
+
+    def mm(o, l, r_, st, sp):
+        add("t", lambda: g.tensor.matmul(val(o), val(l), val(r_), st, sp), [l, r_], [o],
+            hold=max(64, r_["n"]) * PE * (4 if r_["sz"] == 4 else 1), lat=0.1)
+
+    def iota(o, pat, base, cm, fl=True):
+        if fl:
+            add("g", lambda: g.iota(val(o), pat, base, cm, allow_small_or_imprecise_dtypes=True), [], [o], hold=0.13 + 2 * o["n"] * CY)
+        else:
+            add("g", lambda: g.iota(val(o), pat, base, cm), [], [o], hold=0.13 + 2 * o["n"] * CY)
+
+    def dma(e, o, a, lat=2.2):
+        add(e, lambda: Q[e].dma_start(val(o), val(a)), [a], [o], "d", hold=0.1, lat=lat)
+
+    def X(ap, name):
+        return {"ap": ap, "reg": [(name, 0, 1 << 20)], "n": 1, "sz": 4}
+
+    def arrive(bufs, sem, cnt, after, lat):
+        add("x", None, [], bufs, "x", (sem, cnt), hold=0.0, lat=lat, after=after)
+
+    sent = [0]
+
+    def send(o_name, a, dst, sem):
+        rid, pid = topo.addr(dst, core)
+        sent[0] += len(topo.engines(core, dst))
+        return add("g", lambda: g.remote_dma(T[o_name][:], val(a), T.sem[sem], T.sem.ls, pid, rid, topo.mask(core, dst)), [a], [], "r", hold=0.5)
+
+    def S(p, z="Z"):
+        return R(z, 15 - p, 143 - p)
+
+    def D(p):
+        return R("DG", 128 * p, 128 * p + 128)
+
+    (cK, cR, cG16, cM0, cM1, c128, c128b, c256, cZ, cE, cE0, cK1, cRN, cMM, cDU, cD2, cD3, cD4, cBE, cBO, cB0, cB2, cR0, c32, cBD) = [R("KC", k, k + 1) for k in range(25)]
+    kK, kR, kG, kH, kV, kW = [R("KI", k, k + 1) for k in range(6)]
+    add_, sub, mul, mx, mn = AL.add, AL.subtract, AL.mult, AL.max, AL.min
+    N128 = R("NR", 0, 128)
+
+    dma("s", R("CD"), X(T.cd[:], "cd"))
+    dma("a", R("WI"), X(T.wit[:], "wit"))
+    dma("s", R("TX", 0, 2048), X(T.txt[:], "txt"), 5.0)
+    dma("a", R("P0"), X(T.pat[:], "pat"), 5.0)
+    dma("s", R("OI"), X(T.prb[:], "prb"))
+    hints.extend([[0, 2, 4], [1, 3]])
+
+    iota(kK, [[0, 1]], 0, 1, False)
+    iota(R("NR"), [[1, 256]], 0, 0)
+    iota(R("N16"), [[16, 8], [0, 16]], 0, 0)
+    iota(R("NM"), [[0, 8], [1, 16]], 0, 0)
+    ms(R("WP", 128, 136), 0.0)
+    ts(kR, kK, 15, AL.bitwise_and)
+    ts(kG, kK, 4, AL.arith_shift_right)
+    ts(kH, kK, 4, AL.arith_shift_right, 1, AL.bitwise_and)
+    cp(cK, kK)
+    cp(cR, kR)
+    ts(cG16, kG, 16.0, mul)
+    cp(cM1, kH)
+    ts(cM0, kH, -1.0, mul, 1.0, add_)
+    ts(c128, kR, 128.0, mul)
+    ts(R("ID"), N128, cK, AL.is_equal)
+    ts(R("RMK"), R("NR", 0, 16), cR, AL.is_equal)
+    for p in range(7):
+        act(D(p), R("ID"), AF.Identity, 0.0, R("RMK", p, p + 1))
+    for p in range(7, 16):
+        ts(D(p), R("ID"), R("RMK", p, p + 1), mul)
+    ts(c128b, kR, 128.0, mul, 128.0, add_)
+    ts(c256, kR, 256.0, mul)
+    ts(cZ, cG16, 15.0, add_)
+    act(R("IDB"), R("ID"), AF.Identity, 0.0, 262144.0)
+    act(R("NID"), R("ID"), AF.Identity, 0.0, -1.0)
+    ts(R("Z"), R("NR", 0, 144), cZ, AL.is_equal)
+    act(R("ZQ"), R("Z"), AF.Identity, 0.0, -16384.0)
+    act(R("ZP"), R("Z"), AF.Identity, 0.0, 4096.0)
+    ms(R("KJ", 0, 1), 0.0)
+    ms(R("LF", 0, 1), -2048.0)
+    ts(R("BLK"), R("N16"), cG16, AL.is_equal)
+    ts(R("X1"), N128, cK, AL.is_gt)
+    ts(cDU, kR, 32.0, mul, 6201.0, add_)
+    ts(cMM, kR, 128.0, add_)
+    ts(c32, kR, 32.0, mul)
+    tt(R("TRI"), R("X1"), R("BLK"), mul)
+    ts(R("DUMP"), R("NR", 0, 32), cDU, add_)
+    ts(R("NDU"), R("DUMP"), -1.0, mul, 1.0, add_)
+    ts(R("LV"), R("NR", 0, 32), c32, add_)
+    act(R("IX"), R("NR"), AF.Identity, 0.5, -1.0 / 512)
+    tt(R("TRI2"), R("TRI"), R("ID"), add_)
+    for t in range(2):
+        ms(R("O%d" % t, 16, 32), 200.0)
+        ms(R("PO%d" % t, 256, 272), 999.0)
+        ms(R("MO%d" % t, 8, 16), 0, "v")
+    act(R("BLM8"), R("BLK"), AF.Identity, 0.0, -8.0)
+    act(R("BL4"), R("BLK"), AF.Identity, 0.0, 4096.0)
+    act(R("M2"), R("BLK"), AF.Identity, 0.0, -256.0)
+    act(R("ID32"), R("ID"))
+    act(R("ID4"), R("ID"), AF.Identity, 0.0, 4096.0)
+    act(R("X2"), R("TRI"), AF.Identity, 0.0, -2.0)
+    act(R("X3"), R("TRI"), AF.Identity, 0.0, -32.0)
+    ts(cK1, cK, 1.0, add_)
+    ts(cRN, cR, 0.0, AL.is_gt, -1.0, mul)
+    tt(R("X2"), R("X2"), R("ID"), add_)
+    tt(R("M3"), R("X3"), R("BLK"), add_)
+    tt(R("K4"), R("ID"), S(0), sub)
+    act(R("M1"), R("X2"), AF.Identity, 0.0, 128.0)
+    ts(R("X4"), N128, cK1, AL.is_equal)
+    act(R("X5"), R("ID"), AF.Identity, 0.0, cRN)
+    tt(R("X4"), R("X4"), R("BLK"), mul)
+    ts(R("MB"), R("NM"), cR, AL.is_ge, 8192.0, mul)
+    tt(R("K5"), R("X4"), R("X5"), add_)
+    cp(R("LB"), R("NR", 0, 16))
+    iota(R("RS"), [[0, 8], [1, 48]], -32, 0)
+    iota(R("SC", 0, 24), [[1, 8], [0, 3]], 0, 0)
+    ts(R("MW"), R("RS"), cR, AL.is_ge, 8192.0, mul)
+    ms(R("MW", 0, 32), 8192.0)
+    ms(R("MW", 48, 64), 8192.0)
+    ts(R("FL"), R("RS"), -32.0, AL.not_equal)
+    ts(cD2, cR, 3080.0, add_)
+    ts(R("FL", 47, 384, 48), R("NR", 0, 128, 16), cD2, add_)
+    cp(R("L3"), R("SC", 0, 24))
+    ts(cD3, cR, 2048.0, add_)
+    ts(cD4, cR, 2064.0, add_)
+    ts(R("C128"), R("NR", 0, 16), 128.0, mul)
+    ts(cBE, cR, 2.0, AL.is_lt)
+    ts(cB0, cR, 4.0, AL.is_lt)
+    ts(cBO, cB0, cBE, sub)
+    ts(cR0, cR, 1.0, AL.is_lt)
+    act(R("BE"), R("BLK"), AF.Identity, 0.0, cBE)
+    act(R("BO"), R("BLK"), AF.Identity, 0.0, cBO)
+    act(R("HE"), R("ID"), AF.Identity, 0.0, cBE)
+    ts(cE, cK, -2.0, add_)
+    ts(R("HO"), N128, cE, AL.is_equal, cBO, mul)
+    ts(R("HX"), N128, cK1, AL.is_equal, cR0, mul)
+    ts(cE0, cR, 2.0, AL.is_equal)
+    ts(cBD, cE0, 4096.0, mul, cBE, add_)
+    act(R("BD"), R("BLK"), AF.Identity, 0.0, cBD)
+    act(R("NBD"), R("BD"), AF.Identity, 0.0, -1.0)
+    act(R("BP"), R("BLK"), AF.Identity, 0.0, cE0)
+    act(R("Z2"), R("Z"), AF.Identity, 0.0, cE0)
+    act(R("ZE"), R("Z"), AF.Identity, 0.0, cBE)
+    act(R("ZH"), R("Z"), AF.Identity, 0.0, -64.0)
+    ts(cB2, cR, 3.0, mn)
+    ts(kV, cG16, 0.25, mul, cB2, add_)
+    ms(R("XS", 0, 1), 0.0)
+    ms(R("BAD", 0, 1), 1.0)
+    ms(R("LE", 256, 264), -1.0)
+
+    def starts(t):
+        A, ND, NA, OW, BT, ZT, HL, AI, LO = [x + str(t) for x in ("A", "ND", "NA", "OW", "BT", "ZT", "HL", "AI", "LO")]
+        ts(R(BT, 0, 64), R("CD", 64 * t, 64 * t + 64), cM0, mul)
+        ts(R(BT, 64, 128), R("CD", 64 * t, 64 * t + 64), cM1, mul)
+        for q in range(4):
+            o, a = R(ZT, 32 * q, 32 * q + 32), R(BT, q, 128, 4)
+            add("v", lambda o=o, a=a: g.vector.transpose(val(o), val(a)), [a], [o])
+        for q in range(4):
+            tt(R(A, 16 * q, 16 * q + 16), R(ZT, 32 * q, 32 * q + 16), R(ZT, 32 * q + 16, 32 * q + 32), add_)
+        ms(R(ND, 63, 64), -200.0)
+        ms(R(NA, 64, 65), -4000.0)
+        tt(R(ND, 0, 63), R(A, 0, 63), R(A, 1, 64), sub)
+        if t == 0:
+            ts(R(OW), R(ND), -1.0, mul, 128.0, mn)
+            act(R(NA, 0, 64), R(A), AF.Identity, 0.0, -1.0)
+        else:
+            ts(R("DT"), R(ND), -1.0, mul, 128.0, mn)
+            ts(R(NA, 0, 64), R(A), -1.0, mul, c128, sub)
+            ts(R(OW), R("DT"), c128, add_)
+        cp(R(AI), R(A))
+        ts(R(LO), R(AI), 15, AL.bitwise_and)
+        for h in range(2):
+            tt(R(HL, 64 * h, 64 * h + 32), R(A, h, 64, 2), R(LO, h, 64, 2), sub)
+            cp(R(HL, 64 * h + 32, 64 * h + 64), R(LO, h, 64, 2))
+        AD = "AD%d" % t
+        for v in range(4):
+            dma("s", {"ap": T[AD][v:32:4, :], "reg": [(AD, v, v + 1)], "n": 1, "sz": 2}, R(HL, 32 * v, 32 * v + 32))
+        o, src = R("AR%d" % t), X(T[AD][:], AD)
+        add("g", lambda: g.indirect_dma_start(val(o), None, val(src), IndirectOffsetOnAxis(ap=val(kV), axis=0), bounds_check=31),
+            [src, kV], [o], "d", hold=1.7, lat=2.0)
+        act(R("V%d" % t), IND(R("AR%d" % t), R("LV")))
+
+    def wlook(t, off, k, base):
+        win = R("WP", 0, 136) if t == 0 else R("WR1", 0, 2056)
+        h = k // 2
+        act(R("GW", 0, 16 * h), IND(win, R(off, 0, h)))
+        cp(R("GW", 16 * h, 16 * k), IND(win, R(off, h, k)))
+        mm(R("B0", 0, k), R("ID32"), base, True, False)
+        for p in range(16):
+            mm(R("B0", 0, k), D(p) if t == 0 else S(p), R("GW", p, 16 * k, 16), False, p == 15)
+
+    def duel(t, k, base, nd, cj, midj):
+        P = "P%d" % t
+        w = R("B0", 0, k)
+        cp(R("OY", 0, k), w)
+        tt(R("TP", 0, k), w, nd, add_)
+        tt(R("TQ", 0, k), w, base, sub)
+        ts(R("OJ", 0, k), R("TP", 0, k), cj, add_)
+        ts(R("OP", 0, k), R("TQ", 0, k), c128, add_)
+        ts(R("C0", 0, k), R("TQ", 0, k), 0.0, AL.is_equal, 0.53125, add_)
+        cuts = [0, 10, 32, 64] if k == 64 else [0, 10, 32]
+        for a, b in zip(cuts, cuts[1:]):
+            act(R("Y", 16 * a, 16 * b), IND(R("TX", 0, 2048), R("OY", a, b)))
+        mm(R("B1", 0, k), R("IDB"), R("C0", 0, k), True, False)
+        mm(R("B2", 0, k), R("IDB"), R("C0", 0, k), True, False)
+        for a, b in zip(cuts, cuts[1:]):
+            tt(R("NJ", 16 * a, 16 * b), IND(R(P), R("OJ", a, b)), R("Y", 16 * a, 16 * b), AL.not_equal)
+            if b <= 32 and k == 64:
+                tt(R("NI", 16 * a, 16 * b), IND(R(P), R("OP", a, b)), R("Y", 16 * a, 16 * b), AL.not_equal)
+        for p in range(16):
+            mm(R("B1", 0, k), S(p, "ZQ"), R("NJ", p, 16 * k, 16), False, p == 15)
+        a = 32 if k == 64 else 0
+        tt(R("NI", 16 * a, 16 * k), IND(R(P), R("OP", a, k)), R("Y", 16 * a, 16 * k), AL.not_equal)
+        for p in range(16):
+            mm(R("B2", 0, k), S(p, "ZQ"), R("NI", p, 16 * k, 16), False, p == 15 and k == 32)
+        midj()
+
+    def apply(tab, msg):
+        cp(IND(R(tab), R(msg, 0, 8)), R(msg, 16, 144))
+
+    def round_(t):
+        A, O, MO, OB, PO, G2 = [x + str(t) for x in ("A", "O", "MO", "OB", "PO", "G")]
+        cp(R(O, 0, 16), R("OI") if t == 0 else R("MI0", 144, 160))
+        tt(R("TO"), R(O, 0, 16), R("C128"), add_)
+        act(R(OB), R(O, 0, 16))
+        cp(R("OPT"), R("TO"))
+        act(R(PO, 0, 256), IND(R("P%d" % t), R("OPT")))
+        mm(R("B5", 0, 16), R("K5"), R(OB), True, True)
+        act(R(G2), R("B5", 0, 16), AF.Identity, 0.0, 0.5)
+        iota(R("WN", 0, 528), [[0, 528]], 0, 0)
+        iota(R("WN", 4096, 4624), [[0, 528]], 0, 0)
+
+        wlook(t, "OW%d" % t, 64, R(A))
+
+        def j1():
+            act(R("KJ", 1, 64), R("B1", 0, 63), AF.Relu, 0.0, -64.0)
+            mm(R("B2", 0, 64), R("NID"), R("KJ", 0, 64), False, True)
+        duel(t, 64, R(A), R("NA%d" % t, 1, 65), c128 if t == 0 else c256, j1)
+        scan(R("LF", 1, 65), R("B2", 0, 64), R(A), -2048.0, mx, mn)
+        scan(R("NN", 0, 64, -1), R("B2", 0, 64, -1), R("NA%d" % t, 0, 64, -1), -8000.0, mx, mn)
+        ts(R("AL1"), R("B2", 0, 64), 0.0, AL.is_gt)
+        tt(R("ND2"), R("LF", 0, 64, 2), R("NN", 0, 64, 2), add_)
+        ts(R("OW2"), R("ND2"), -1.0, mul, 128.0 if t == 0 else c128b, mn)
+
+        ts(R("T1"), R("AL1"), -2 * BIG, mul, 2 * BIG, add_)
+        ts(R("T2"), R("AL1"), -BIG, mul)
+        tt(R("T1", 1, 64, 2), R("T1", 1, 64, 2), R("T2", 0, 64, 2), add_)
+        wlook(t, "OW2", 32, R("LF", 0, 64, 2))
+
+        def j2():
+            tt(R("KL", 0, 64, 2), R("B1", 0, 32), R("T1", 0, 64, 2), AL.is_le)
+            tt(R("KL", 1, 64, 2), R("B1", 0, 32), R("T1", 1, 64, 2), AL.is_le)
+            ts(R("TH"), R("KL"), 2 * BIG, mul)
+            ts(R("AL2", 62, 64), R("KL", 62, 64), 0.5, AL.is_lt)
+            tt(R("TH", 0, 64, 2), R("TH", 0, 64, 2), R("T2", 1, 64, 2), add_)
+            tt(R("ANY", 31, 32), R("AL2", 62, 63), R("AL2", 63, 64), mx)
+            tt(R("TM"), R("TH", 0, 64, 2), R("TH", 1, 64, 2), mn)
+        duel(t, 32, R("LF", 0, 64, 2), R("NN", 0, 64, 2), c128 if t == 0 else c256, j2)
+        mm(R("B0", 0, 32), R("ID32"), R("DUMP"), True, False)
+        tt(R("AL2", 0, 62, 2), R("B2", 1, 32), R("TH", 0, 62, 2), AL.is_gt)
+        tt(R("AL2", 1, 62, 2), R("B2", 1, 32), R("TH", 1, 62, 2), AL.is_gt)
+        tt(R("ANY", 0, 31), R("B2", 1, 32), R("TM", 0, 31), AL.is_gt)
+
+        scan(R("CUM"), R("AL2"), R("AL2"), 0.0, add_, mx)
+        tt(R("XD"), R("ANY"), R("NDU"), mul)
+        mm(R("B0", 0, 32), R("NID"), R("AL2", 0, 64, 2), False, False)
+        mm(R("B0", 0, 32), R("ID4"), R("AL2", 1, 64, 2), False, False)
+        mm(R("B3", 0, 1), R("TRI"), R("CUM", 63, 64), True, True)
+        mm(R("B3", 1, 2), R("TRI2"), R("CUM", 63, 64), True, True)
+        mm(R("B0", 0, 32), R("ID"), R("CUM", 1, 64, 2), False, False)
+        mm(R("B0", 0, 32), R("ID"), R("CUM", 1, 64, 2), False, False)
+        mm(R("B0", 0, 32), R("ID32"), R("XD"), False, True)
+        ts(R("SE", 0, 2), R("B3", 0, 2), -0.5, add_)
+        ts(R("OS"), R("B0", 0, 32), R("B3", 0, 1), add_, R("B3", 0, 1), add_)
+        act(R("SGE"), R("NR"), AF.Sign, R("SE", 1, 2), -1.0)
+        mm(R("B3", 0, 256), R("BLM8"), R("SGE"), True, True)
+        for r in range(16):
+            mm(R("B1", 0, 16), S(r), R("SGE", r, 256, 16), r == 0, r == 15)
+        h1 = cp(IND(R("WN"), R("OS", 0, 10)), R("V%d" % t, 0, 160))
+        h2 = ts(R("OPO"), R("B3", 0, 256), cMM, add_)
+        h3 = cp(IND(R("WN"), R("OS", 10, 16)), R("V%d" % t, 160, 256))
+        h4 = ts(R("PL"), R("B1", 0, 16), -0.5, mul, 8.0, add_)
+        h5 = cp(IND(R("WN"), R("OS", 16, 32)), R("V%d" % t, 256, 512))
+        hints.append([h1, h2, h3, h4, h5])
+        kog = act(R("OG"), IND(R(O, 0, 24), R("PL")))
+        for bk, a, b in (("B6", 0, 32), ("B7", 32, 256)):
+            o = R(bk, 0, b - a)
+            mm(o, R("ID"), R("OG", a, b), True, False)
+            mm(o, R("BE"), R("WN", 2 + 2 * a, 2 + 2 * b, 2), False, False)
+            mm(o, R("BO"), R("WN", 4098 + 2 * a, 4098 + 2 * b, 2), False, False)
+            mm(o, R("BO"), R("WN", 4099 + 2 * a, 4099 + 2 * b, 2), False, False)
+            mm(o, R("BE"), R("WN", 4100 + 2 * a, 4100 + 2 * b, 2), False, True)
+            hints.append([len(ops) - 1, len(ops) + 1 + (6 if a == 0 else 1)])
+            if a == 0:
+                hints.append([len(ops) - 1, len(ops) + 1])
+            cp(R("OTU", a, b), o)
+        o = R("B2", 0, 256)
+        mm(o, S(2, "ZH"), R("SGE"), True, False)
+        mm(o, R("HX"), R("OG"), False, False)
+        mm(o, R("HE"), R("WN", 2, 514, 2), False, False)
+        mm(o, R("HO"), R("WN", 4098, 4610, 2), False, False)
+        mm(o, R("HO"), R("WN", 4099, 4611, 2), False, False)
+        mm(o, R("HE"), R("WN", 4100, 4612, 2), False, True)
+        kxs = act(R("XS", 1, 257), o)
+        act(R("SGS"), R("NR"), AF.Sign, R("SE", 0, 1), -1.0)
+        mm(R("B0", 0, 256), R("ID"), R("SGE"), True, False)
+        mm(R("B0", 0, 256), R("NID"), R("SGS"), False, False)
+        mm(R("B0", 0, 256), R("ID"), R("IX"), False, True)
+        act(R("XX"), R("B0", 0, 256), AF.Relu, -1024.0, 512.0)
+        for r in range(16):
+            mm(R("B3", 0, 8), S(r, "Z2"), R("XS", 1 + 2 * r, 257, 32), r == 0, False)
+        for bk in ("B2", "B6", "B7"):
+            mm(R(bk, 0, 256), R("BD"), R("XS", 1, 257), True, False)
+            mm(R(bk, 0, 256), R("NBD"), R("XS", 0, 256), False, False)
+            if bk != "B7":
+                mm(R(bk, 0, 256), R("ID"), R("OG"), False, bk == "B2")
+            if bk == "B2":
+                kpen = act(R("PEN"), R("B2", 0, 256), AF.Relu, -127.5 * 1024, 1024.0)
+            else:
+                mm(R(bk, 0, 256), R("NID"), R("PEN"), False, False)
+        mm(R("B2", 0, 384), R("ID"), R("MW"), True, False)
+        for c in range(8):
+            u = max(c - 2, 0)
+            mm(R("B2", 48 * c + 16 * (u - c + 2), 48 * c + 48), R("BP"), R("XS", 1 + 32 * u, 33 + 32 * c, 2), False, False)
+        for r in range(16):
+            mm(R("B1", 0, 16), S(r, "ZE"), R("XS", 1 + r, 257, 16), r == 0, r == 15)
+        act(R("LX"), R("B1", 0, 16))
+        cp(R("OX", 0, 16, 2), R("LX", 0, 8))
+        cp(R("OX", 1, 16, 2), R("LX", 8, 16))
+        act(R("FV"), IND(R("TX", 0, 2048), R("OX")), AF.Identity, 255.0, -1.0)
+
+        cuts = [0, 32, 80, 136, 192, 256]
+        kp = []
+        for a, b in zip(cuts, cuts[1:]):
+            kp.append(act(R("PX", 16 * a, 16 * b), IND(R(PO), R("OPO", a, b))))
+            tt(R("NQ", 16 * a, 16 * b), IND(R("TX", 0, 2048), R("OTU", a, b)), R("PX", 16 * a, 16 * b), AL.not_equal)
+            if a in (0, 80):
+                continue
+            if b == 256:
+                hints.append([kp[0], kog, kp[1], kp[2], kxs, kp[3], kp[4], kpen])
+            a0 = {32: 0, 136: 80, 192: 192}[a]
+            o = R("B4", a0, b) if b < 256 else R("B5", 0, 64)
+            for m in range(16):
+                mm(o, S(m, "ZQ"), R("NQ", 16 * a0 + m, 16 * b, 16), m == 0, m == 15)
+        ts(R("BAD", 1, 193), R("B4", 0, 192), -16384.0 * 8.5, AL.is_lt)
+        ts(R("BAD", 193, 257), R("B5", 0, 64), -16384.0 * 8.5, AL.is_lt)
+
+        for bk in ("B7", "B6"):
+            mm(R(bk, 0, 192), R("M1"), R("BAD", 1, 193), False, False)
+            mm(R(bk, 0, 192), R("M2"), R("BAD", 0, 192), False, False)
+            mm(R(bk, 192, 256), R("M1"), R("BAD", 193, 257), False, False)
+            mm(R(bk, 192, 256), R("M2"), R("BAD", 192, 256), False, True)
+        mm(R("B0", 0, 256), R("BL4"), R("BAD", 1, 257), True, True)
+        mm(R("B1", 0, 256), R("M3"), R("BAD", 1, 257), True, True)
+        ts(R("UT"), R("B7", 1, 256, 2), 128.0, mx)
+        act(R("LE", 0, 256), R("B1", 0, 256), AF.Sign, -0.5)
+        act(R("UU"), R("B6", 0, 256), AF.Relu, -128.0)
+        tt(R("UD"), R("B7", 0, 256, 2), R("UT"), mx)
+        tt(R("YY"), R("B0", 0, 256), R("XX"), mn)
+        for c in range(8):
+            u = max(c - 2, 0)
+            mm(R("B2", 48 * c + 16 * (u - c + 2), 48 * c + 48), R("BLK"), R("UD", 16 * u, 16 * c + 16), False, c == 7)
+        hints.append([len(ops) - 1, len(ops)])
+        for r in range(16):
+            mm(R("B3", 0, 8), S(r), R("UD", r, 128, 16), False, r == 15)
+        mm(R("B4", 0, 128), S(0), R("UU", 0, 256, 2), True, False)
+        mm(R("B4", 0, 128), S(0), R("UU", 1, 256, 2), False, True)
+        mm(R("B1", 0, 16), R("ID"), R(OB), True, False)
+        mm(R("B1", 0, 16), R("K4"), R(G2), False, False)
+        o, a = R("RM", 0, 1), R("YY")
+        add("v", lambda: g.vector.tensor_reduce(val(o), val(a), AxisListType.X, mx), [a], [o], hold=256 * CY)
+        act(R("RS"), R("B2", 0, 384))
+        cp(R("LS"), R("B3", 0, 8))
+        ts(R("SX", 0, 1), R("RM", 0, 1), -1.0, mul, 256.0, add_)
+        tt(R("EQ"), IND(R("LS"), R("L3")), R("RS"), AL.is_equal)
+        tt(R("HH"), IND(R("LE"), R("SX", 0, 1)), R(G2), mul)
+        scan(R("SC"), R("FL"), R("EQ"), 0.0, mul, mx)
+        tt(R("LM"), R("SC", 47, 384, 48), R("LS"), mx)
+        mm(R("B1", 0, 16), R("K4"), R("HH"), False, True)
+        cp(R(MO, 16, 144), R("B4", 0, 128))
+        ts(R(MO, 0, 8), R("LM"), -1024.0, add_)
+        cp(R(MO, 144, 160), R("B1", 0, 16))
+        dst = prv if t == 0 else nxt
+        k = send("MI%d" % t, R(MO), relays(topo, core, dst)[0], "rm%d" % t)
+
+        mm(R("B6", 0, 128), R("BE"), R("XS", 1, 129), True, False)
+        mm(R("B6", 0, 128), R("BL4"), R("BAD", 1, 129), False, True)
+        mm(R("B7", 0, 256), R("BE"), R("XS", 1, 257), True, False)
+        mm(R("B7", 0, 128), R("ID"), R("MB"), False, False)
+        mm(R("B7", 128, 256), R("ID"), R("MB"), False, False)
+        mm(R("B7", 0, 256), R("BL4"), R("BAD", 1, 257), False, True)
+        mm(R("B0", 0, 16), R("ID32"), R("LX"), True, False)
+        for r in range(16):
+            mm(R("B0", 0, 16), S(r, "ZP"), R("BAD", 1 + r, 257, 16), False, r == 15)
+        act(R("RA"), R("B6", 0, 128))
+        act(R("RB"), R("B7", 0, 256))
+        cp(R("L2"), R("B0", 0, 16))
+        tt(R("E2"), IND(R("L2"), R("LB", 8, 16)), R("RA"), AL.is_equal)
+        tt(R("E1"), IND(R("L2"), R("LB")), R("RB"), AL.is_equal)
+        mm(R("B3", 0, 16), R("ID32"), R("L2"), True, False)
+        for r in range(16):
+            mm(R("B3", 8, 16), R("ID4"), R("E2", r, 128, 16), False, False)
+        for r in range(16):
+            mm(R("B3", 0, 16), R("ID4"), R("E1", r, 256, 16), False, r == 15)
+        ts(R("OA", 0, 16, 2), R("B3", 0, 8), cD3, mn)
+        ts(R("OA", 1, 16, 2), R("B3", 8, 16), cD4, mn)
+        for p in range(8):
+            cp(IND(R("TX"), R("OA", 2 * p, 2 * p + 2)), R("FV", 32 * p, 32 * p + 32))
+        return k
+
+    rl = relays(topo, core, prv)
+    wd = 2048 // len(rl)
+    trs = []
+    for k, c in enumerate(rl):
+        en = topo.engines(core, c)
+        h = len(en) // len(rl)
+        m = 0
+        for e in en[k * h:(k + 1) * h]:
+            m |= 1 << e
+        rid, pid = topo.addr(c, core)
+        trs.append(RemoteDMATransfer(dst_ids=[DstId(rid=rid, pnc=pid)], dma_engine_mask=m, remote_sem=T.sem.rp,
+                                     src=T.P0[:, k * wd:(k + 1) * wd], dst=T.P1[:, k * wd:(k + 1) * wd]))
+        sent[0] += h
+
+    def rows(name):
+        return {"ap": T[name][0:128:16, 0:2048], "reg": [(name, 0, 2048)], "n": 1, "sz": 4}
+
+    far = relays(topo, nxt, core)
+    cp(R("WP", 0, 128), R("WI"))
+    starts(0)
+    starts(1)
+    k1 = add("g", lambda: g.remote_dma_fused(trs, local_sem=T.sem.ls), [R("P0")], [], "r", hold=1.5)
+    k2 = send("WL", R("WP", 0, 128), rl[1], "rw")
+    for nm in ("WR1", "WR0"):
+        for a in range(0, 2080, 520):
+            iota(R(nm, a, a + 520), [[0, 520]], 0, 0)
+    dma("s", rows("WR0"), R("WP", 0, 128))
+    arrive([R("P1")], "ap", sum(len(topo.engines(c, core)) for c in far), k1, 20.0)
+    arrive([R("WL")], "aw", len(topo.engines(far[1], core)), k2, 14.0)
+    dma("s", rows("WR1"), R("WL"))
+    ms(R("WR1", 0, 2048, 128), 0.0, "v")
+    cp(R("W0"), R("WR0", 0, 2048, 128))
+    k = round_(0)
+    arrive([R("MI0")], "am0", len(topo.engines(far[0], core)), k, HOP)
+    apply("WR1", "MI0")
+    apply("WR0", "MO0")
+    k = round_(1)
+    for h, e in enumerate("sa"):
+        dma(e, X(T.yt[64 * h:64 * h + 64, :], "yt%d" % h), {"ap": T.TX[64 * h:64 * h + 64, 0:2048], "reg": [("TX", 0, 2048)], "n": 1, "sz": 2}, 4.0)
+    back = relays(topo, prv, core)[0]
+    arrive([R("MI1")], "am1", len(topo.engines(back, core)), k, HOP)
+    act_o = R("OO")
+    cp(act_o, R("MI1", 144, 160))
+    apply("WR0", "MI1")
+    cp(R("WR0", 0, 2048, 128), R("W0"))
+    dma("a", X(T.yo[:], "yo"), act_o)
+    dma("s", X(T.yw[:], "yw"), rows("WR0"))
+
+    def meet(a, b):
+        for x in a:
+            for y in b:
+                if x[0] == y[0] and x[1] < y[2] and y[1] < x[2]:
+                    if len(x) == 4 and len(y) == 4 and x[3] == y[3] and (x[1] - y[1]) % x[3]:
+                        continue
+                    return True
+        return False
+
+    last = {}
+    for i, o in enumerate(ops):
+        dep, soft = set(), set()
+        for nm in set(x[0] for x in o["r"] + o["w"]):
+            bank = nm[0] == "B"
+            prev = last.setdefault(nm, [])
+            for j in prev:
+                p = ops[j]
+                if p["e"] == o["e"] == "t":
+                    if bank:
+                        soft.add(j)
+                elif p["k"] == "r":
+                    continue
+                elif (bank and p["e"] != o["e"]) or meet(p["w"], o["r"]) or meet(p["w"], o["w"]) or meet(p["r"], o["w"]):
+                    dep.add(j)
+            prev.append(i)
+        if o["after"] is not None:
+            soft.add(o["after"])
+        o["dep"], o["soft"] = dep, soft
+    for h in hints:
+        for a, b in zip(h, h[1:]):
+            ops[b]["soft"].add(a)
+    topo_, mark = [], set()
+
+    def visit(i):
+        stack = [(i, False)]
+        while stack:
+            x, done = stack.pop()
+            if done:
+                topo_.append(x)
+            elif x not in mark:
+                mark.add(x)
+                stack.append((x, True))
+                stack.extend((j, False) for j in ops[x]["dep"] | ops[x]["soft"] if j not in mark)
+    for i in range(len(ops)):
+        visit(i)
+    level = [0.0] * len(ops)
+    for i in reversed(topo_):
+        o = ops[i]
+        level[i] += o["hold"]
+        for j in o["dep"]:
+            level[j] = max(level[j], level[i] + ops[j]["lat"] + WAKE)
+        for j in o["soft"]:
+            level[j] = max(level[j], level[i] + 1e-6)
+    busy = {}
+    for i in sorted(range(len(ops)), key=lambda x: (-level[x], x)):
+        o = ops[i]
+        t0 = 1.0
+        for j in o["dep"]:
+            t0 = max(t0, ops[j]["end"] + ops[j]["lat"] + WAKE)
+        for j in o["soft"]:
+            t0 = max(t0, ops[j]["end"])
+        line = busy.setdefault(o["e"], [])
+        pos = len(line)
+        for q, (a, b) in enumerate(line):
+            if t0 + o["hold"] <= a + 1e-9:
+                pos = q
+                break
+            t0 = max(t0, b)
+        line.insert(pos, (t0, t0 + o["hold"]))
+        o["t"], o["end"] = t0, t0 + o["hold"]
+    order = sorted(range(len(ops)), key=lambda x: (ops[x]["t"], ops[x]["end"], x))
+    place = {}
+    for q, i in enumerate(order):
+        place[i] = q
+    seen = {}
+    for i in order:
+        o = ops[i]
+        best = {}
+        for j in o["dep"]:
+            key = (o["e"], ops[j]["e"] if ops[j]["k"] == "c" else j)
+            if key not in best or place[best[key]] < place[j]:
+                best[key] = j
+        o["wait"] = []
+        for key, j in best.items():
+            if o["k"] != "x" and seen.get(key, -1) < place[j]:
+                seen[key] = place[j]
+                o["wait"].append(j)
+                ops[j]["sig"] = True
+    cnt = {"v": 0, "a": 0, "t": 0, "g": 0}
+    nd = 0
+    for i in order:
+        o = ops[i]
+        if o["k"] == "x":
+            o["tok"] = (T.sem[o["ext"][0]], o["ext"][1])
+            continue
+        for j in sorted(o["wait"], key=lambda x: place[x]):
+            Q[o["e"]].wait_ge(ops[j]["tok"][0], ops[j]["tok"][1])
+        ins = o["fn"]()
+        if o["k"] == "d":
+            o["tok"] = (T.sem["d%d" % nd], 16)
+            nd += 1
+            ins.then_inc(o["tok"][0], 16)
+        elif o["k"] == "c" and o.get("sig"):
+            cnt[o["e"]] += 1
+            o["tok"] = (T.sem["s" + o["e"]], cnt[o["e"]])
+            ins.then_inc(o["tok"][0], 1)
+    g.wait_ge(T.sem.ls, sent[0])
+    for o in ops:
+        if o["k"] == "d" and not o.get("sig"):
+            g.wait_ge(o["tok"][0], 16)

@@ -1,29 +1,34 @@
-from concourse.bass import DstId, RemoteDMATransfer, IndirectOffsetOnAxis
+from concourse.bass import DstId, RemoteDMATransfer
 from concourse.mybir import AluOpType as AL, AxisListType, ActivationFunctionType as AF
 
-F, B, U, I = "float32", "bfloat16", "uint16", "int32"
-SIZE = {F: 4, B: 2, U: 2, I: 4}
+F, B, U, I, H = "float32", "bfloat16", "uint16", "int32", "float16"
+SIZE = {F: 4, B: 2, U: 2, I: 4, H: 2}
 
-OWN = {"TX": (2080, B), "P0": (2048, B), "P1": (2048, B), "WP": (136, F), "WL": (128, F), "WR0": (2192, F), "WR1": (2192, F),
+OWN = {"TX0": (2112, B), "TX1": (2112, B), "P0": (2048, B), "WP": (136, F), "WR": (2192, F),
        "DG": (2048, B), "GW": (1024, B), "Y": (1024, B), "NJ": (1024, B), "NI": (1024, B), "WN": (8800, B), "PX": (4096, B),
-       "NQ": (4096, B), "MO0": (160, U), "MO1": (160, U), "MI0": (160, U), "MI1": (160, U), "CD": (128, I), "WI": (128, I),
-       "OI": (16, I), "AR0": (512, B), "AR1": (512, B), "HL0": (128, B), "HL1": (128, B), "OO": (16, F)}
+       "NQ": (4096, B), "CD": (128, I), "WI": (128, I), "OI": (16, I), "AR": (512, B),
+       "SO": (200, F), "SN": (200, F), "VO": (512, B), "V1": (512, B),
+       "HL0": (128, B), "HL1": (128, B), "O2": (16, F), "OA0": (24, U), "OA1": (24, U), "ON0": (24, U), "ON1": (24, U),
+       "FV0": (256, B), "FV1": (256, B), "FN0": (256, B), "FN1": (256, B)}
 SMALL = {
-    F: {"W0": 16, "O0": 32, "O1": 32, "KC": 32, "NR": 256, "N16": 128, "NM": 128, "ID32": 128,
-        "DUMP": 32, "NDU": 32, "RMK": 16, "C128": 16, "BT0": 128, "ZT0": 128, "BT1": 128, "ZT1": 128, "A0": 64, "A1": 64, "ND0": 64, "ND1": 64,
-        "NA0": 72, "NA1": 72, "DT": 64, "TP": 64, "LF": 72, "NN": 64, "ND2": 32, "AL1": 64, "T1": 64, "T2": 64, "KL": 64,
-        "TH": 64, "TM": 32, "ANY": 32, "XD": 32, "SE": 8, "TO": 16, "LS": 8, "RS": 384, "SC": 384, "FL": 384, "LM": 8, "TQ": 64, "RM": 8, "LX": 16, "L2": 16,
-        "RA": 128, "RB": 256},
-    B: {"OB0": 16, "OB1": 16, "ID": 128, "NID": 128, "IDB": 128, "ID4": 128, "NID4": 128, "BLK": 128, "BLM8": 128, "BL4": 128, "M2": 128, "TRI": 128,
-        "TRI2": 128, "M1": 128, "M3": 128, "K4": 128, "K5": 128, "HE": 128, "HO": 128, "HX": 128, "BD": 128, "NBD": 128, "BP": 128, "Z2": 144, "ZE": 144, "ZH": 144, "XS": 264, "BE": 128, "BO": 128, "X1": 128, "X2": 128, "X3": 128, "X4": 128, "X5": 128,
-        "Z": 144, "ZQ": 144, "ZP": 144, "MB": 128, "IX": 256, "C0": 64, "KJ": 72, "AL2": 64, "CUM": 64, "V0": 512, "V1": 512, "PO0": 272, "PO1": 272,
-        "SGE": 256, "SGS": 256, "OG": 256, "PR": 264, "DB": 256, "PEN": 256, "XX": 256, "BAD": 264, "UU": 256, "UT": 128,
-        "UD": 128, "EQ": 384, "MW": 384, "YY": 256, "LE": 264, "G0": 16, "G1": 16, "HH": 16, "E1": 256, "E2": 128, "FV": 256},
-    U: {"LB": 16, "L3": 24, "LV": 32, "OW0": 64, "OW1": 64, "OY": 64, "OJ": 64, "OP": 64, "OW2": 32, "OS": 32, "OTU": 256, "OPO": 256, "OPT": 16,
-        "PL": 16, "SX": 2, "OX": 16, "OA": 16},
-    I: {"KI": 8, "AI0": 64, "AI1": 64, "LO0": 64, "LO1": 64},
+    F: {"W0": 16, "O0": 32, "O1": 32, "KC": 16, "NR": 264, "ID32": 128, "R16": 16, "R32": 16, "RLT": 8,
+        "DUMP": 32, "NDU": 32, "RMK": 16, "C128": 16, "BT0": 128, "ZT0": 128, "BT1": 128, "ZT1": 128, "A0": 64,
+        "ND0": 64, "ND1": 64, "NA0": 72, "DT": 64, "TP": 64, "LF": 72, "NN": 64, "ND2": 32, "AL1": 64, "T1": 64,
+        "T2": 64, "KL": 64, "TH": 64, "TM": 32, "ANY": 32, "XD": 32, "SE": 8, "TO": 16, "SC": 392, "FL": 392,
+        "EQ": 392, "TQ": 64, "RM": 8, "SF": 408, "RX": 408},
+    B: {"OB0": 16, "OB1": 16, "ID": 128, "NID": 128, "IDB": 128, "ID4": 128, "IDN4": 128, "BLK": 128, "BLM8": 128, "BL8": 128,
+        "M2": 128, "TRI": 128, "TRI2": 128, "M1": 128, "HE": 128, "HO": 128, "HX": 128,
+        "BD": 128, "NBD": 128, "BP": 128, "Z2": 144, "ZE": 144, "ZN": 144, "ZH": 144, "XS": 264, "BE": 128, "BO": 128,
+        "X3": 128, "X4": 128, "NX4": 128, "Z": 144, "ZQ": 144, "SG": 408, "RS": 392, "ALT": 256,
+        "PAD": 32, "IX": 256, "C0": 64, "KJ": 72, "AL2": 64, "CUM": 64, "V0": 512, "PO0": 272, "PO1": 272,
+        "SGE": 256, "OG": 256, "PEN": 256, "XX": 256, "BAD": 264, "UU": 256, "UD": 256, "YY": 256, "LE": 264, "G0": 16,
+        "G1": 16, "HH": 16, "MP": 408, "MV": 128},
+    U: {"LV": 32, "OW0": 64, "OW1": 64, "OY": 64, "OJ": 64, "OP": 64, "OW2": 32, "OS": 32, "OTU": 256, "OPO": 256,
+        "OPT": 16, "PL": 16, "SX": 2, "OX": 16, "OF": 8},
+    I: {"KI": 8},
+    H: {"NIH": 128, "LH": 16},
 }
-SCRATCH = {"AD0": ("dram", [32, 512], B), "AD1": ("dram", [32, 512], B)}
+SCRATCH = {}
 PLACE = {}
 for _k, (_n, _d) in OWN.items():
     SCRATCH[_k] = ("sbuf", [128, _n], _d)
@@ -38,10 +43,19 @@ for _k in range(8):
     SCRATCH["B%d" % _k] = ("psum", [128, 512], F)
     PLACE["B%d" % _k] = ("B%d" % _k, 0, 512, 4)
 
+for _k, _b, _o, _n in (("AO", "SO", 0, 64), ("NAO", "SO", 64, 72), ("OWO", "SO", 136, 64),
+                       ("A1", "SN", 0, 64), ("NA1", "SN", 64, 72), ("OWN", "SN", 136, 64)):
+    PLACE[_k] = (_b, _o, _n, 4)
+
 NDMA = 24
-SEMAPHORES = ["sv", "sa", "st", "sg", "ls", "rp", "rw", "rm0", "rm1", "ap", "aw", "am0", "am1"] + ["d%d" % k for k in range(NDMA)]
+MSG = ["p", "s", "v", "f0", "a0", "b0", "f1", "a1", "b1"]
+SEMAPHORES = (["sv", "sa", "st", "sg", "ls", "lt"] + ["r" + m for m in MSG] + ["a" + m for m in MSG]
+              + ["d%d" % k for k in range(NDMA)])
 BIG = 1.0e6
-CY, PE, WAKE, HOP = 1.04e-3, 0.55e-3, 0.1, 5.5
+SA = 192
+TL, TH = 32, 2080
+CY, PE, WAKE, HOP = 1.04e-3, 0.52e-3, 0.1, 4.0
+WSPLIT = 40
 
 
 def relays(topo, src, dst):
@@ -49,36 +63,38 @@ def relays(topo, src, dst):
     return [x for x in c if topo.die(x) == topo.die(src)] + [x for x in c if topo.die(x) != topo.die(src)]
 
 
-def relay_program(g, core, T, topo):
+def messages(T, topo, src):
     n = len(T.cores)
+    r = T.rank_of(src)
+    prv, nxt = T.cores[(r - 1) % n], T.cores[(r + 1) % n]
+    rl = relays(topo, src, nxt)
+    wd = (TH - TL) // len(rl)
+    out = [("p", c, nxt, ("TX0", TL + k * wd, TL + (k + 1) * wd), ("TX1", TL + k * wd, TL + (k + 1) * wd)) for k, c in enumerate(rl)]
+    out += [("s", rl[1], nxt, ("SO", 0, 200), ("SN", 0, 200)), ("v", rl[3], nxt, ("VO", 0, 512), ("V1", 0, 512))]
+    for t, dst in enumerate((nxt, prv)):
+        rl = relays(topo, src, dst)
+        out += [("f%d" % t, rl[2], dst, ("FV%d" % t, 0, 256), ("FN%d" % t, 0, 256)),
+                ("a%d" % t, rl[1], dst, ("OA%d" % t, 0, SA // 16), ("ON%d" % t, 0, SA // 16)),
+                ("b%d" % t, rl[0], dst, ("OA%d" % t, 16, 32 - SA // 16), ("ON%d" % t, 16, 32 - SA // 16))]
+    return out
+
+
+def relay_program(g, core, T, topo):
     own = [c for c in topo.cores_of(core) if T.rank_of(c) is not None]
     if not own:
         return
-    src = own[0]
-    r = T.rank_of(src)
-    prv, nxt = T.cores[(r - 1) % n], T.cores[(r + 1) % n]
-    rl = relays(topo, src, prv)
-    if core not in rl:
-        return
-    k = rl.index(core)
-    wd = 2048 // len(rl)
-    ne = len(topo.engines(src, core))
-    tot = [0]
-
-    def hand(buf, sem, cnt, dst, rsem):
-        g.wait_ge(T.sem[sem], cnt)
+    msgs = messages(T, topo, own[0])
+    tot = 0
+    for name, via, dst, _, (buf, a, b) in msgs:
+        if via != core:
+            continue
+        share = sum(1 for m in msgs if m[0] == name)
+        g.wait_ge(T.sem["r" + name], len(topo.engines(own[0], core)) // share)
         rid, pid = topo.addr(dst, core)
-        g.remote_dma(buf, buf, T.sem[rsem], T.sem.ls, pid, rid, topo.mask(core, dst))
-        tot[0] += len(topo.engines(core, dst))
-
-    hand(T.P1[:, k * wd:(k + 1) * wd], "rp", ne // len(rl), prv, "ap")
-    if k == 1:
-        hand(T.WL[:], "rw", ne, prv, "aw")
-    if k == 0:
-        hand(T.MI0[:], "rm0", ne, prv, "am0")
-    if core == relays(topo, src, nxt)[0]:
-        hand(T.MI1[:], "rm1", ne, nxt, "am1")
-    g.wait_ge(T.sem.ls, tot[0])
+        g.remote_dma(T[buf][:, a:b], T[buf][:, a:b], T.sem["a" + name], T.sem.ls, pid, rid, topo.mask(core, dst))
+        tot += len(topo.engines(core, dst))
+    if tot:
+        g.wait_ge(T.sem.ls, tot)
 
 
 def rank_program(g, core, T, topo):
@@ -86,8 +102,6 @@ def rank_program(g, core, T, topo):
     if rank is None:
         relay_program(g, core, T, topo)
         return
-    n = len(T.cores)
-    prv, nxt = T.cores[(rank - 1) % n], T.cores[(rank + 1) % n]
     ops = []
     Q = {"v": g.vector, "a": g.scalar, "t": g.tensor, "g": g, "s": g.sync}
 
@@ -140,6 +154,7 @@ def rank_program(g, core, T, topo):
         if op == AL.not_equal:
             ops[k]["after"] = chain[0]
             chain[0] = k
+        return k
 
     def ts(o, a, s1, op0, s2=None, op1=None):
         if op1 is None:
@@ -158,14 +173,15 @@ def rank_program(g, core, T, topo):
             add("v", lambda: g.vector.memset(val(o), c), [], [o])
 
     def scan(o, d0, d1, init, op0, op1):
-        add("v", lambda: g.vector.tensor_tensor_scan(val(o), val(d0), val(d1), init, op0, op1), [d0, d1], [o])
+        return add("v", lambda: g.vector.tensor_tensor_scan(val(o), val(d0), val(d1), init, op0, op1), [d0, d1], [o],
+                   hold=max(64, o["n"]) * CY)
 
     def act(o, a, f=AF.Identity, bias=0.0, scale=1.0):
         return add("a", lambda: g.scalar.activation(val(o), val(a), f, bias=val(bias), scale=val(scale)), [a, bias, scale], [o])
 
     def mm(o, l, r_, st, sp):
-        add("t", lambda: g.tensor.matmul(val(o), val(l), val(r_), st, sp), [l, r_], [o],
-            hold=max(64, r_["n"]) * PE * (4 if r_["sz"] == 4 else 1), lat=0.1)
+        return add("t", lambda: g.tensor.matmul(val(o), val(l), val(r_), st, sp), [l, r_], [o],
+                   hold=max(64, r_["n"]) * PE * (4 if r_["sz"] == 4 else 1), lat=0.1)
 
     def iota(o, pat, base, cm, fl=True):
         if fl:
@@ -173,21 +189,41 @@ def rank_program(g, core, T, topo):
         else:
             add("g", lambda: g.iota(val(o), pat, base, cm), [], [o], hold=0.13 + 2 * o["n"] * CY)
 
-    def dma(e, o, a, lat=2.2):
+    def pick(o, a, pat, op, fill, base, cm):
+        add("g", lambda: g.affine_select(val(o), val(a), pat, op, fill, base, cm), [a], [o], hold=0.17 + 2 * o["n"] * CY)
+
+    def dma(e, o, a, lat=2.4):
         add(e, lambda: Q[e].dma_start(val(o), val(a)), [a], [o], "d", hold=0.1, lat=lat)
 
     def X(ap, name):
         return {"ap": ap, "reg": [(name, 0, 1 << 20)], "n": 1, "sz": 4}
 
-    def arrive(bufs, sem, cnt, after, lat):
-        add("x", None, [], bufs, "x", (sem, cnt), hold=0.0, lat=lat, after=after)
+    mine = messages(T, topo, core)
+    coming = [m for c in T.cores if c != core for m in messages(T, topo, c) if m[2] == core]
+    sent = {"ls": 0, "lt": 0}
 
-    sent = [0]
+    def send(name, sem="ls", hold=0.5):
+        parts = [m for m in mine if m[0] == name]
+        trs = []
+        for k, (_, via, _, s_, d_) in enumerate(parts):
+            en = topo.engines(core, via)
+            h = len(en) // len(parts)
+            rid, pid = topo.addr(via, core)
+            trs.append((R(*d_)["ap"], R(*s_)["ap"], pid, rid, sum(1 << e for e in en[k * h:(k + 1) * h])))
+            sent[sem] += h
+        if len(trs) == 1:
+            o, a, pid, rid, m = trs[0]
+            fn = lambda: g.remote_dma(o, a, T.sem["r" + name], T.sem[sem], pid, rid, m)
+        else:
+            tl = [RemoteDMATransfer(dst_ids=[DstId(rid=rid, pnc=pid)], dma_engine_mask=m, remote_sem=T.sem["r" + name], src=a, dst=o)
+                  for o, a, pid, rid, m in trs]
+            fn = lambda: g.remote_dma_fused(tl, local_sem=T.sem[sem])
+        return add("g", fn, [R(*m[3]) for m in parts], [], "r", hold=hold)
 
-    def send(o_name, a, dst, sem):
-        rid, pid = topo.addr(dst, core)
-        sent[0] += len(topo.engines(core, dst))
-        return add("g", lambda: g.remote_dma(T[o_name][:], val(a), T.sem[sem], T.sem.ls, pid, rid, topo.mask(core, dst)), [a], [], "r", hold=0.5)
+    def arrive(name, after, lat):
+        parts = [m for m in coming if m[0] == name]
+        cnt = sum(len(topo.engines(m[1], core)) for m in parts)
+        add("x", None, [], [R(*m[4]) for m in parts], "x", ("a" + name, cnt), hold=0.0, lat=lat, after=after)
 
     def S(p, z="Z"):
         return R(z, 15 - p, 143 - p)
@@ -195,22 +231,26 @@ def rank_program(g, core, T, topo):
     def D(p):
         return R("DG", 128 * p, 128 * p + 128)
 
-    (cK, cR, cG16, cM0, cM1, c128, c128b, c256, cZ, cE, cE0, cK1, cRN, cMM, cDU, cD2, cD3, cD4, cBE, cBO, cB0, cB2, cR0, c32, cBD) = [R("KC", k, k + 1) for k in range(25)]
-    kK, kR, kG, kH, kV, kW = [R("KI", k, k + 1) for k in range(6)]
+    cK, cR, cG16, cM0, cM1, c128b, cN128, cBO, cBD, cBN, cBM, cXB, cGS = [R("KC", k, k + 1) for k in range(13)]
+    kK, kR, kG, kH = [R("KI", k, k + 1) for k in range(4)]
+    c32, c128, c256 = [R("R32", k, k + 1) for k in (1, 4, 8)]
+    cLD, cMM = [cR, R("R16", 1, 2)], R("R16", 8, 9)
+    cHD = [R("FL", 97, 98), R("FL", 146, 147)]
+    cR0, cE2, cE3, cBE, cB4 = R("RMK", 0, 1), R("RMK", 2, 3), R("RMK", 3, 4), R("RLT", 2, 3), R("RLT", 4, 5)
     add_, sub, mul, mx, mn = AL.add, AL.subtract, AL.mult, AL.max, AL.min
+    ne, gt, ge, eq = AL.not_equal, AL.is_gt, AL.is_ge, AL.is_equal
     N128 = R("NR", 0, 128)
 
     dma("s", R("CD"), X(T.cd[:], "cd"))
     dma("a", R("WI"), X(T.wit[:], "wit"))
-    dma("s", R("TX", 0, 2048), X(T.txt[:], "txt"), 5.0)
-    dma("a", R("P0"), X(T.pat[:], "pat"), 5.0)
+    dma("s", R("TX0", TL, TH), X(T.txt[:], "txt"), 4.0)
+    dma("a", R("P0"), X(T.pat[:], "pat"), 4.0)
     dma("s", R("OI"), X(T.prb[:], "prb"))
     hints.extend([[0, 2, 4], [1, 3]])
 
+    diag = [[1, 128]]
     iota(kK, [[0, 1]], 0, 1, False)
-    iota(R("NR"), [[1, 256]], 0, 0)
-    iota(R("N16"), [[16, 8], [0, 16]], 0, 0)
-    iota(R("NM"), [[0, 8], [1, 16]], 0, 0)
+    iota(R("NR"), [[1, 264]], 0, 0)
     ms(R("WP", 128, 136), 0.0)
     ts(kR, kK, 15, AL.bitwise_and)
     ts(kG, kK, 4, AL.arith_shift_right)
@@ -220,95 +260,63 @@ def rank_program(g, core, T, topo):
     ts(cG16, kG, 16.0, mul)
     cp(cM1, kH)
     ts(cM0, kH, -1.0, mul, 1.0, add_)
-    ts(c128, kR, 128.0, mul)
-    ts(R("ID"), N128, cK, AL.is_equal)
-    ts(R("RMK"), R("NR", 0, 16), cR, AL.is_equal)
+    ts(R("ID"), N128, cK, eq)
+    ts(R("RMK"), R("NR", 0, 16), cR, eq)
     for p in range(7):
         act(D(p), R("ID"), AF.Identity, 0.0, R("RMK", p, p + 1))
     for p in range(7, 16):
         ts(D(p), R("ID"), R("RMK", p, p + 1), mul)
-    ts(c128b, kR, 128.0, mul, 128.0, add_)
-    ts(c256, kR, 256.0, mul)
-    ts(cZ, cG16, 15.0, add_)
-    act(R("IDB"), R("ID"), AF.Identity, 0.0, 262144.0)
-    act(R("NID"), R("ID"), AF.Identity, 0.0, -1.0)
-    ts(R("Z"), R("NR", 0, 144), cZ, AL.is_equal)
-    act(R("ZQ"), R("Z"), AF.Identity, 0.0, -16384.0)
-    act(R("ZP"), R("Z"), AF.Identity, 0.0, 4096.0)
+    ts(R("R16", 0, 9), R("NR", 0, 144, 16), cR, add_)
+    ts(R("R32", 0, 9), R("NR", 0, 264, 32), cR, mul)
+    ts(R("RLT"), R("NR", 0, 8), cR, gt)
+    ts(R("Z"), R("NR", 0, 144), cG16, sub, 15.0, eq)
+    ts(R("DUMP"), R("NR", 0, 32), c32, add_, 6201.0, add_)
+    ts(R("LV"), R("NR", 0, 32), c32, add_)
     ms(R("KJ", 0, 1), 0.0)
     ms(R("LF", 0, 1), -2048.0)
-    ts(R("BLK"), R("N16"), cG16, AL.is_equal)
-    ts(R("X1"), N128, cK, AL.is_gt)
-    ts(cDU, kR, 32.0, mul, 6201.0, add_)
-    ts(cMM, kR, 128.0, add_)
-    ts(c32, kR, 32.0, mul)
-    tt(R("TRI"), R("X1"), R("BLK"), mul)
-    ts(R("DUMP"), R("NR", 0, 32), cDU, add_)
-    ts(R("NDU"), R("DUMP"), -1.0, mul, 1.0, add_)
-    ts(R("LV"), R("NR", 0, 32), c32, add_)
-    act(R("IX"), R("NR"), AF.Identity, 0.5, -1.0 / 512)
-    tt(R("TRI2"), R("TRI"), R("ID"), add_)
+    ms(R("BLK"), 1.0)
+    pick(R("BLK"), R("BLK"), [[-16, 8], [0, 16]], ge, 0.0, 0, 1)
+    pick(R("BLK"), R("BLK"), [[16, 8], [0, 16]], ge, 0.0, 15, -1)
+    pick(R("TRI"), R("BLK"), diag, gt, 0.0, 0, -1)
+    pick(R("TRI2"), R("BLK"), diag, ge, 0.0, 0, -1)
+    pick(R("X4"), R("BLK"), diag, eq, 0.0, -1, -1)
+    for nm, of, sc in (("ID32", "ID", 1.0), ("IDB", "ID", 262144.0), ("NID", "ID", -1.0), ("ID4", "ID", 4096.0), ("HE", "ID", cBE),
+                       ("IDN4", "ID", -4096.0), ("ZQ", "Z", -16384.0), ("ZH", "Z", -64.0), ("ZN", "Z", -1.0), ("Z2", "Z", cE2),
+                       ("ZE", "Z", cBE), ("BLM8", "BLK", -8.0), ("BL8", "BLK", 8192.0), ("M2", "BLK", -256.0), ("BE", "BLK", cBE),
+                       ("BP", "BLK", cE2), ("X3", "TRI", -32.0), ("NX4", "X4", -1.0), ("HX", "X4", cR0)):
+        act(R(nm), R(of), AF.Identity, 0.0, sc)
+    for o, a, bias, sc in ((c128b, c128, 128.0, 1.0), (cN128, c128, 0.0, -1.0), (cBO, cBE, cB4, -1.0), (cBD, cE2, cBE, 4096.0),
+                           (cBN, cBD, 0.0, -1.0), (cBM, cE3, cBD, -128.0), (cXB, cR0, -1024.0, 512.0), (cGS, cR0, 0.5, -0.5),
+                           (R("NDU"), R("DUMP"), 1.0, -1.0), (R("C128"), R("NR", 0, 16), 0.0, 128.0),
+                           (R("IX"), R("NR", 0, 256), 0.5, -1.0 / 512),
+                           (R("BO"), R("BLK"), 0.0, cBO), (R("BD"), R("BLK"), 0.0, cBM), (R("NBD"), R("BLK"), 0.0, cBN)):
+        act(o, a, AF.Identity, bias, sc)
+    pick(R("HO"), R("BO"), diag, eq, 0.0, 2, -1)
+    pick(R("M1"), R("M2"), diag, gt, 0.0, 0, -1)
+    pick(R("M1"), R("M1"), diag, ne, 128.0, 0, -1)
+    cp(R("NIH"), R("NID"))
     for t in range(2):
         ms(R("O%d" % t, 16, 32), 200.0)
         ms(R("PO%d" % t, 256, 272), 999.0)
-        ms(R("MO%d" % t, 8, 16), 0, "v")
-    act(R("BLM8"), R("BLK"), AF.Identity, 0.0, -8.0)
-    act(R("BL4"), R("BLK"), AF.Identity, 0.0, 4096.0)
-    act(R("M2"), R("BLK"), AF.Identity, 0.0, -256.0)
-    act(R("ID32"), R("ID"))
-    act(R("ID4"), R("ID"), AF.Identity, 0.0, 4096.0)
-    act(R("X2"), R("TRI"), AF.Identity, 0.0, -2.0)
-    act(R("X3"), R("TRI"), AF.Identity, 0.0, -32.0)
-    ts(cK1, cK, 1.0, add_)
-    ts(cRN, cR, 0.0, AL.is_gt, -1.0, mul)
-    tt(R("X2"), R("X2"), R("ID"), add_)
-    tt(R("M3"), R("X3"), R("BLK"), add_)
-    tt(R("K4"), R("ID"), S(0), sub)
-    act(R("M1"), R("X2"), AF.Identity, 0.0, 128.0)
-    ts(R("X4"), N128, cK1, AL.is_equal)
-    act(R("X5"), R("ID"), AF.Identity, 0.0, cRN)
-    tt(R("X4"), R("X4"), R("BLK"), mul)
-    ts(R("MB"), R("NM"), cR, AL.is_ge, 8192.0, mul)
-    tt(R("K5"), R("X4"), R("X5"), add_)
-    cp(R("LB"), R("NR", 0, 16))
-    iota(R("RS"), [[0, 8], [1, 48]], -32, 0)
-    iota(R("SC", 0, 24), [[1, 8], [0, 3]], 0, 0)
-    ts(R("MW"), R("RS"), cR, AL.is_ge, 8192.0, mul)
-    ms(R("MW", 0, 32), 8192.0)
-    ms(R("MW", 48, 64), 8192.0)
-    ts(R("FL"), R("RS"), -32.0, AL.not_equal)
-    ts(cD2, cR, 3080.0, add_)
-    ts(R("FL", 47, 384, 48), R("NR", 0, 128, 16), cD2, add_)
-    cp(R("L3"), R("SC", 0, 24))
-    ts(cD3, cR, 2048.0, add_)
-    ts(cD4, cR, 2064.0, add_)
-    ts(R("C128"), R("NR", 0, 16), 128.0, mul)
-    ts(cBE, cR, 2.0, AL.is_lt)
-    ts(cB0, cR, 4.0, AL.is_lt)
-    ts(cBO, cB0, cBE, sub)
-    ts(cR0, cR, 1.0, AL.is_lt)
-    act(R("BE"), R("BLK"), AF.Identity, 0.0, cBE)
-    act(R("BO"), R("BLK"), AF.Identity, 0.0, cBO)
-    act(R("HE"), R("ID"), AF.Identity, 0.0, cBE)
-    ts(cE, cK, -2.0, add_)
-    ts(R("HO"), N128, cE, AL.is_equal, cBO, mul)
-    ts(R("HX"), N128, cK1, AL.is_equal, cR0, mul)
-    ts(cE0, cR, 2.0, AL.is_equal)
-    ts(cBD, cE0, 4096.0, mul, cBE, add_)
-    act(R("BD"), R("BLK"), AF.Identity, 0.0, cBD)
-    act(R("NBD"), R("BD"), AF.Identity, 0.0, -1.0)
-    act(R("BP"), R("BLK"), AF.Identity, 0.0, cE0)
-    act(R("Z2"), R("Z"), AF.Identity, 0.0, cE0)
-    act(R("ZE"), R("Z"), AF.Identity, 0.0, cBE)
-    act(R("ZH"), R("Z"), AF.Identity, 0.0, -64.0)
-    ts(cB2, cR, 3.0, mn)
-    ts(kV, cG16, 0.25, mul, cB2, add_)
-    ms(R("XS", 0, 1), 0.0)
+    ms(R("PAD"), 8192.0)
+    iota(R("ALT"), [[0, 128], [1, 2]], 0, 0)
+    iota(R("RS"), [[0, 8], [1, 49]], -16, 0)
+    act(R("RS"), R("RS"), AF.Sign, cR)
+    act(R("FL"), R("RS"), AF.Abs)
+    ts(R("FL", 48, 392, 49), R("NR", 0, 128, 16), cR, add_, TH - 16.0, add_)
+    iota(R("MP"), [[0, 24], [1, 17]], 0, 0)
+    pick(R("MP"), R("MP"), [[0, 8], [1, 3], [0, 17]], gt, -100.0, 0, 0)
+    act(R("SG"), R("MP"), AF.Sign, cR, -1.0)
+    ms(R("RX"), 0.0)
+    ms(R("RX", 0, 408, 51), BIG)
+    ms(R("RX", 34, 408, 51), BIG)
+    ms(R("XS", 0, 264, 257), 0.0)
     ms(R("BAD", 0, 1), 1.0)
     ms(R("LE", 256, 264), -1.0)
 
     def starts(t):
-        A, ND, NA, OW, BT, ZT, HL, AI, LO = [x + str(t) for x in ("A", "ND", "NA", "OW", "BT", "ZT", "HL", "AI", "LO")]
+        ND, BT, ZT, HL = [x + str(t) for x in ("ND", "BT", "ZT", "HL")]
+        A, NA, OW, V = [x + "0O"[t] for x in ("A", "NA", "OW", "V")]
         ts(R(BT, 0, 64), R("CD", 64 * t, 64 * t + 64), cM0, mul)
         ts(R(BT, 64, 128), R("CD", 64 * t, 64 * t + 64), cM1, mul)
         for q in range(4):
@@ -317,31 +325,24 @@ def rank_program(g, core, T, topo):
         for q in range(4):
             tt(R(A, 16 * q, 16 * q + 16), R(ZT, 32 * q, 32 * q + 16), R(ZT, 32 * q + 16, 32 * q + 32), add_)
         ms(R(ND, 63, 64), -200.0)
-        ms(R(NA, 64, 65), -4000.0)
+        ms(R(NA, 64, 72), -4000.0)
         tt(R(ND, 0, 63), R(A, 0, 63), R(A, 1, 64), sub)
         if t == 0:
             ts(R(OW), R(ND), -1.0, mul, 128.0, mn)
             act(R(NA, 0, 64), R(A), AF.Identity, 0.0, -1.0)
         else:
             ts(R("DT"), R(ND), -1.0, mul, 128.0, mn)
-            ts(R(NA, 0, 64), R(A), -1.0, mul, c128, sub)
-            ts(R(OW), R("DT"), c128, add_)
-        cp(R(AI), R(A))
-        ts(R(LO), R(AI), 15, AL.bitwise_and)
+            act(R(NA, 0, 64), R(A), AF.Identity, cN128, -1.0)
+            act(R(OW), R("DT"), AF.Identity, c128)
         for h in range(2):
-            tt(R(HL, 64 * h, 64 * h + 32), R(A, h, 64, 2), R(LO, h, 64, 2), sub)
-            cp(R(HL, 64 * h + 32, 64 * h + 64), R(LO, h, 64, 2))
-        AD = "AD%d" % t
+            act(R(HL, 64 * h, 64 * h + 32), R(A, h, 64, 2))
+            tt(R(HL, 64 * h + 32, 64 * h + 64), R(A, h, 64, 2), R(HL, 64 * h, 64 * h + 32), sub)
         for v in range(4):
-            dma("s", {"ap": T[AD][v:32:4, :], "reg": [(AD, v, v + 1)], "n": 1, "sz": 2}, R(HL, 32 * v, 32 * v + 32))
-        o, src = R("AR%d" % t), X(T[AD][:], AD)
-        add("g", lambda: g.indirect_dma_start(val(o), None, val(src), IndirectOffsetOnAxis(ap=val(kV), axis=0), bounds_check=31),
-            [src, kV], [o], "d", hold=1.7, lat=2.0)
-        act(R("V%d" % t), IND(R("AR%d" % t), R("LV")))
+            dma("s", {"ap": T.AR[v:128:16, :], "reg": [("AR", v, 512, 4)], "n": 1, "sz": 2}, R(HL, 32 * v, 32 * v + 32))
+        return act(R(V), IND(R("AR"), R("LV")))
 
-    def wlook(t, off, k, base):
-        win = R("WP", 0, 136) if t == 0 else R("WR1", 0, 2056)
-        h = k // 2
+    def wlook(t, off, k, base, h):
+        win = R("WP", 0, 136) if t == 0 else R("WR", 0, 2056)
         act(R("GW", 0, 16 * h), IND(win, R(off, 0, h)))
         cp(R("GW", 16 * h, 16 * k), IND(win, R(off, h, k)))
         mm(R("B0", 0, k), R("ID32"), base, True, False)
@@ -349,47 +350,50 @@ def rank_program(g, core, T, topo):
             mm(R("B0", 0, k), D(p) if t == 0 else S(p), R("GW", p, 16 * k, 16), False, p == 15)
 
     def duel(t, k, base, nd, cj, midj):
-        P = "P%d" % t
         w = R("B0", 0, k)
         cp(R("OY", 0, k), w)
         tt(R("TP", 0, k), w, nd, add_)
         tt(R("TQ", 0, k), w, base, sub)
         ts(R("OJ", 0, k), R("TP", 0, k), cj, add_)
         ts(R("OP", 0, k), R("TQ", 0, k), c128, add_)
-        ts(R("C0", 0, k), R("TQ", 0, k), 0.0, AL.is_equal, 0.53125, add_)
+        ts(R("C0", 0, k), R("TQ", 0, k), 0.0, eq, 0.53125, add_)
         cuts = [0, 10, 32, 64] if k == 64 else [0, 10, 32]
         for a, b in zip(cuts, cuts[1:]):
-            act(R("Y", 16 * a, 16 * b), IND(R("TX", 0, 2048), R("OY", a, b)))
+            act(R("Y", 16 * a, 16 * b), IND(R("TX%d" % t, TL, TH), R("OY", a, b)))
         mm(R("B1", 0, k), R("IDB"), R("C0", 0, k), True, False)
         mm(R("B2", 0, k), R("IDB"), R("C0", 0, k), True, False)
         for a, b in zip(cuts, cuts[1:]):
-            tt(R("NJ", 16 * a, 16 * b), IND(R(P), R("OJ", a, b)), R("Y", 16 * a, 16 * b), AL.not_equal)
+            tt(R("NJ", 16 * a, 16 * b), IND(R("P0"), R("OJ", a, b)), R("Y", 16 * a, 16 * b), ne)
             if b <= 32 and k == 64:
-                tt(R("NI", 16 * a, 16 * b), IND(R(P), R("OP", a, b)), R("Y", 16 * a, 16 * b), AL.not_equal)
+                tt(R("NI", 16 * a, 16 * b), IND(R("P0"), R("OP", a, b)), R("Y", 16 * a, 16 * b), ne)
         for p in range(16):
             mm(R("B1", 0, k), S(p, "ZQ"), R("NJ", p, 16 * k, 16), False, p == 15)
         a = 32 if k == 64 else 0
-        tt(R("NI", 16 * a, 16 * k), IND(R(P), R("OP", a, k)), R("Y", 16 * a, 16 * k), AL.not_equal)
+        tt(R("NI", 16 * a, 16 * k), IND(R("P0"), R("OP", a, k)), R("Y", 16 * a, 16 * k), ne)
         for p in range(16):
             mm(R("B2", 0, k), S(p, "ZQ"), R("NI", p, 16 * k, 16), False, p == 15 and k == 32)
         midj()
 
-    def apply(tab, msg):
-        cp(IND(R(tab), R(msg, 0, 8)), R(msg, 16, 144))
+    def flip(tx, off, new):
+        for q in range(8):
+            c = 2 * q if 32 * q < SA else 16 + 2 * q - SA // 16
+            cp(IND(R(tx), R(off, c, c + 2)), R(new, 32 * q, 32 * q + 32))
 
     def round_(t):
-        A, O, MO, OB, PO, G2 = [x + str(t) for x in ("A", "O", "MO", "OB", "PO", "G")]
-        cp(R(O, 0, 16), R("OI") if t == 0 else R("MI0", 144, 160))
+        A, O, OB, PO, G2, TX, OA, FV = [x + str(t) for x in ("A", "O", "OB", "PO", "G", "TX", "OA", "FV")]
+        text = R(TX, TL, TH)
         tt(R("TO"), R(O, 0, 16), R("C128"), add_)
         act(R(OB), R(O, 0, 16))
         cp(R("OPT"), R("TO"))
-        act(R(PO, 0, 256), IND(R("P%d" % t), R("OPT")))
-        mm(R("B5", 0, 16), R("K5"), R(OB), True, True)
-        act(R(G2), R("B5", 0, 16), AF.Identity, 0.0, 0.5)
+        kpo = act(R(PO, 0, 256), IND(R("P0"), R("OPT")))
+        ops[kpo]["lat"] = 4.0
+        mm(R("B5", 0, 16), R("X4"), R(OB), True, False)
+        mm(R("B5", 0, 16), R("NID"), R(OB), False, True)
+        act(R(G2), R("B5", 0, 16), AF.Identity, 0.0, cGS)
         iota(R("WN", 0, 528), [[0, 528]], 0, 0)
         iota(R("WN", 4096, 4624), [[0, 528]], 0, 0)
 
-        wlook(t, "OW%d" % t, 64, R(A))
+        wlook(t, "OW%d" % t, 64, R(A), 32 if t == 0 else WSPLIT)
 
         def j1():
             act(R("KJ", 1, 64), R("B1", 0, 63), AF.Relu, 0.0, -64.0)
@@ -397,14 +401,14 @@ def rank_program(g, core, T, topo):
         duel(t, 64, R(A), R("NA%d" % t, 1, 65), c128 if t == 0 else c256, j1)
         scan(R("LF", 1, 65), R("B2", 0, 64), R(A), -2048.0, mx, mn)
         scan(R("NN", 0, 64, -1), R("B2", 0, 64, -1), R("NA%d" % t, 0, 64, -1), -8000.0, mx, mn)
-        ts(R("AL1"), R("B2", 0, 64), 0.0, AL.is_gt)
+        ts(R("AL1"), R("B2", 0, 64), 0.0, gt)
         tt(R("ND2"), R("LF", 0, 64, 2), R("NN", 0, 64, 2), add_)
         ts(R("OW2"), R("ND2"), -1.0, mul, 128.0 if t == 0 else c128b, mn)
 
         ts(R("T1"), R("AL1"), -2 * BIG, mul, 2 * BIG, add_)
         ts(R("T2"), R("AL1"), -BIG, mul)
         tt(R("T1", 1, 64, 2), R("T1", 1, 64, 2), R("T2", 0, 64, 2), add_)
-        wlook(t, "OW2", 32, R("LF", 0, 64, 2))
+        wlook(t, "OW2", 32, R("LF", 0, 64, 2), 16)
 
         def j2():
             tt(R("KL", 0, 64, 2), R("B1", 0, 32), R("T1", 0, 64, 2), AL.is_le)
@@ -416,9 +420,9 @@ def rank_program(g, core, T, topo):
             tt(R("TM"), R("TH", 0, 64, 2), R("TH", 1, 64, 2), mn)
         duel(t, 32, R("LF", 0, 64, 2), R("NN", 0, 64, 2), c128 if t == 0 else c256, j2)
         mm(R("B0", 0, 32), R("ID32"), R("DUMP"), True, False)
-        tt(R("AL2", 0, 62, 2), R("B2", 1, 32), R("TH", 0, 62, 2), AL.is_gt)
-        tt(R("AL2", 1, 62, 2), R("B2", 1, 32), R("TH", 1, 62, 2), AL.is_gt)
-        tt(R("ANY", 0, 31), R("B2", 1, 32), R("TM", 0, 31), AL.is_gt)
+        tt(R("AL2", 0, 62, 2), R("B2", 1, 32), R("TH", 0, 62, 2), gt)
+        tt(R("AL2", 1, 62, 2), R("B2", 1, 32), R("TH", 1, 62, 2), gt)
+        tt(R("ANY", 0, 31), R("B2", 1, 32), R("TM", 0, 31), gt)
 
         scan(R("CUM"), R("AL2"), R("AL2"), 0.0, add_, mx)
         tt(R("XD"), R("ANY"), R("NDU"), mul)
@@ -429,9 +433,9 @@ def rank_program(g, core, T, topo):
         mm(R("B0", 0, 32), R("ID"), R("CUM", 1, 64, 2), False, False)
         mm(R("B0", 0, 32), R("ID"), R("CUM", 1, 64, 2), False, False)
         mm(R("B0", 0, 32), R("ID32"), R("XD"), False, True)
-        ts(R("SE", 0, 2), R("B3", 0, 2), -0.5, add_)
+        ts(R("SE", 1, 2), R("B3", 1, 2), -0.5, add_)
         ts(R("OS"), R("B0", 0, 32), R("B3", 0, 1), add_, R("B3", 0, 1), add_)
-        act(R("SGE"), R("NR"), AF.Sign, R("SE", 1, 2), -1.0)
+        act(R("SGE"), R("NR", 0, 256), AF.Sign, R("SE", 1, 2), -1.0)
         mm(R("B3", 0, 256), R("BLM8"), R("SGE"), True, True)
         for r in range(16):
             mm(R("B1", 0, 16), S(r), R("SGE", r, 256, 16), r == 0, r == 15)
@@ -460,160 +464,138 @@ def rank_program(g, core, T, topo):
         mm(o, R("HO"), R("WN", 4098, 4610, 2), False, False)
         mm(o, R("HO"), R("WN", 4099, 4611, 2), False, False)
         mm(o, R("HE"), R("WN", 4100, 4612, 2), False, True)
-        kxs = act(R("XS", 1, 257), o)
-        act(R("SGS"), R("NR"), AF.Sign, R("SE", 0, 1), -1.0)
-        mm(R("B0", 0, 256), R("ID"), R("SGE"), True, False)
-        mm(R("B0", 0, 256), R("NID"), R("SGS"), False, False)
-        mm(R("B0", 0, 256), R("ID"), R("IX"), False, True)
-        act(R("XX"), R("B0", 0, 256), AF.Relu, -1024.0, 512.0)
+        kxs = act(R("XS", 1, 257), o, AF.Identity, cE3)
+
         for r in range(16):
-            mm(R("B3", 0, 8), S(r, "Z2"), R("XS", 1 + 2 * r, 257, 32), r == 0, False)
-        for bk in ("B2", "B6", "B7"):
+            mm(R("B0", 0, 16), S(r, "ZE"), R("XS", 1 + r, 257, 16), r == 0, r == 15)
+        kx = [cp(R("LH"), R("B0", 0, 16)), cp(R("OX"), R("B0", 0, 16))]
+        krx = [act(R("RX", 50 - 17 * e, 408, 51), R("B0", e, 16, 2), AF.Identity, float(TL)) for e in range(2)]
+        kfv = act(R(FV), IND(text, R("OX")), AF.Identity, 255.0, -1.0)
+        kf = send("f%d" % t)
+        for q in range(8):
+            mm(R("B1", 51 * q, 51 * q + 34), R("BE"), R("XS", 32 * q, 32 * q + 34), q == 0, False)
+            mm(R("B1", 51 * q + 34, 51 * q + 51), R("BE"), R("XS", 32 * q + 1, 32 * q + 18), False, False)
+        for i in list(range(33)) + list(range(34, 50)):
+            mm(R("B1", i, 408, 51), R("NIH"), R("LH", 1 if i < 34 else 0, 16, 2), False, i == 49)
+        kmp = act(R("MP"), R("B1", 0, 408), AF.Abs, 0.0, 8192.0)
+        for bk, a, b in (("B3", 0, 51 * SA // 32), ("B7", 51 * SA // 32, 408)):
+            mm(R(bk, a, b), R("IDN4"), R("SG", a, b), True, False)
+            mm(R(bk, a, b), R("ID"), R("MP", a, b), False, False)
+        for bk in ("B2", "B6", "B0"):
             mm(R(bk, 0, 256), R("BD"), R("XS", 1, 257), True, False)
             mm(R(bk, 0, 256), R("NBD"), R("XS", 0, 256), False, False)
-            if bk != "B7":
+            if bk != "B0":
                 mm(R(bk, 0, 256), R("ID"), R("OG"), False, bk == "B2")
             if bk == "B2":
-                kpen = act(R("PEN"), R("B2", 0, 256), AF.Relu, -127.5 * 1024, 1024.0)
+                kpen = act(R("PEN"), R("B2", 0, 256), AF.Relu, 512.0, 1024.0)
             else:
                 mm(R(bk, 0, 256), R("NID"), R("PEN"), False, False)
-        mm(R("B2", 0, 384), R("ID"), R("MW"), True, False)
-        for c in range(8):
-            u = max(c - 2, 0)
-            mm(R("B2", 48 * c + 16 * (u - c + 2), 48 * c + 48), R("BP"), R("XS", 1 + 32 * u, 33 + 32 * c, 2), False, False)
+        mm(R("B2", 0, 32), R("ID"), R("PAD"), True, False)
+        mm(R("B2", 32, 160), R("BP"), R("XS", 1, 257, 2), False, False)
         for r in range(16):
-            mm(R("B1", 0, 16), S(r, "ZE"), R("XS", 1 + r, 257, 16), r == 0, r == 15)
-        act(R("LX"), R("B1", 0, 16))
-        cp(R("OX", 0, 16, 2), R("LX", 0, 8))
-        cp(R("OX", 1, 16, 2), R("LX", 8, 16))
-        act(R("FV"), IND(R("TX", 0, 2048), R("OX")), AF.Identity, 255.0, -1.0)
+            mm(R("B2", 192, 200), S(r, "Z2"), R("XS", 1 + 2 * r, 257, 32), False, False)
 
-        cuts = [0, 32, 80, 136, 192, 256]
-        kp = []
+        cuts = [0, 32, 96, 144, SA, SA + 28, 244, 256]
+        kp, kq, ks = {}, {}, [kf]
         for a, b in zip(cuts, cuts[1:]):
-            kp.append(act(R("PX", 16 * a, 16 * b), IND(R(PO), R("OPO", a, b))))
-            tt(R("NQ", 16 * a, 16 * b), IND(R("TX", 0, 2048), R("OTU", a, b)), R("PX", 16 * a, 16 * b), AL.not_equal)
-            if a in (0, 80):
-                continue
-            if b == 256:
-                hints.append([kp[0], kog, kp[1], kp[2], kxs, kp[3], kp[4], kpen])
-            a0 = {32: 0, 136: 80, 192: 192}[a]
-            o = R("B4", a0, b) if b < 256 else R("B5", 0, 64)
-            for m in range(16):
-                mm(o, S(m, "ZQ"), R("NQ", 16 * a0 + m, 16 * b, 16), m == 0, m == 15)
-        ts(R("BAD", 1, 193), R("B4", 0, 192), -16384.0 * 8.5, AL.is_lt)
-        ts(R("BAD", 193, 257), R("B5", 0, 64), -16384.0 * 8.5, AL.is_lt)
+            if a < 244:
+                e = b if a <= SA else 256
+                kp[a] = act(R("PX", 16 * a, 16 * e), IND(R(PO), R("OPO", a, e)))
+            kq[a] = tt(R("NQ", 16 * a, 16 * b), IND(text, R("OTU", a, b)), R("PX", 16 * a, 16 * b), ne)
+        kv = []
+        for a, b, bk, nm, parts in ((0, SA, "B4", "a", [0, 96, 144, SA]), (SA, 256, "B5", "b", [SA, 256])):
+            for u, w in zip(parts, parts[1:]):
+                for m in range(16):
+                    mm(R(bk, u - a, w - a), S(m, "ZQ"), R("NQ", 16 * u + m, 16 * w, 16), m == 0, m == 15)
+            kv.append(ts(R("BAD", 1 + a, 1 + b), R(bk, 0, b - a), -16384.0 * 8.5, AL.is_lt))
+            qa, qb = a // 32, b // 32
+            fb = "B3" if a == 0 else "B7"
+            for q in range(qa, qb):
+                mm(R(fb, 51 * q, 51 * q + 33), R("BL8"), R("BAD", 32 * q, 32 * q + 33), False, False)
+                mm(R(fb, 51 * q + 34, 51 * q + 50), R("BL8"), R("BAD", 32 * q + 1, 32 * q + 17), False, q == qb - 1)
+            kv.append(scan(R("SF", 51 * qa, 51 * qb), R("RX", 51 * qa, 51 * qb), R(fb, 51 * qa, 51 * qb), 0.0, add_, mn))
+            c = 0 if a == 0 else 16
+            for e in range(2):
+                kv.append(ts(R(OA, c + e, c + 2 * (qb - qa), 2), R("SF", 51 * qa + 50 - 17 * e, 51 * qb, 51), cHD[e], mn, cLD[e], mx))
+            ks.append(send("%s%d" % (nm, t)))
+            for bk in ("B0", "B6"):
+                mm(R(bk, a, b), R("M1"), R("BAD", 1 + a, 1 + b), False, False)
+                mm(R(bk, a, b), R("M2"), R("BAD", a, b), False, b == 256)
+        hints.append([kp[0], kog, kp[32], kxs, kp[96], kp[144], kp[SA], kfv, kp[SA + 28], kmp] + krx + [kpen])
+        hints.append([kq[32]] + kx + [kq[96], kq[144], kq[SA], kv[0], kq[SA + 28]] + kv[1:4] + [kq[244]] + late[t])
 
-        for bk in ("B7", "B6"):
-            mm(R(bk, 0, 192), R("M1"), R("BAD", 1, 193), False, False)
-            mm(R(bk, 0, 192), R("M2"), R("BAD", 0, 192), False, False)
-            mm(R(bk, 192, 256), R("M1"), R("BAD", 193, 257), False, False)
-            mm(R(bk, 192, 256), R("M2"), R("BAD", 192, 256), False, True)
-        mm(R("B0", 0, 256), R("BL4"), R("BAD", 1, 257), True, True)
-        mm(R("B1", 0, 256), R("M3"), R("BAD", 1, 257), True, True)
-        ts(R("UT"), R("B7", 1, 256, 2), 128.0, mx)
-        act(R("LE", 0, 256), R("B1", 0, 256), AF.Sign, -0.5)
-        act(R("UU"), R("B6", 0, 256), AF.Relu, -128.0)
-        tt(R("UD"), R("B7", 0, 256, 2), R("UT"), mx)
-        tt(R("YY"), R("B0", 0, 256), R("XX"), mn)
-        for c in range(8):
-            u = max(c - 2, 0)
-            mm(R("B2", 48 * c + 16 * (u - c + 2), 48 * c + 48), R("BLK"), R("UD", 16 * u, 16 * c + 16), False, c == 7)
-        hints.append([len(ops) - 1, len(ops)])
+        scan(R("UD"), R("ALT"), R("B0", 0, 256), 0.0, mul, mx)
+        act(R("UU"), R("B6", 0, 256), AF.Relu)
+        mm(R("B2", 32, 160), R("BLK"), R("UD", 1, 256, 2), False, False)
         for r in range(16):
-            mm(R("B3", 0, 8), S(r), R("UD", r, 128, 16), False, r == 15)
+            mm(R("B2", 192, 200), S(r), R("UD", 1 + 2 * r, 256, 32), False, r == 15)
         mm(R("B4", 0, 128), S(0), R("UU", 0, 256, 2), True, False)
         mm(R("B4", 0, 128), S(0), R("UU", 1, 256, 2), False, True)
-        mm(R("B1", 0, 16), R("ID"), R(OB), True, False)
-        mm(R("B1", 0, 16), R("K4"), R(G2), False, False)
+        act(R("MV"), R("B4", 0, 128))
+        for c in range(8):
+            ts(R("EQ", 49 * c, 49 * c + 48), R("B2", 16 * c, 16 * c + 48, -1), R("B2", 192 + c, 193 + c), eq)
+        ts(R("EQ", 48, 392, 49), R("B2", 192, 200), 1024.0, add_)
+        scan(R("SC"), R("FL"), R("EQ"), 0.0, mul, mx)
+        cp(R("OF"), R("SC", 48, 392, 49))
+        cp(IND(R("WR"), R("OF")), R("MV"))
+
+        mm(R("B7", 0, 256), R("ID"), R("SGE"), True, False)
+        mm(R("B7", 0, 256), R("NX4"), R("SGE"), False, False)
+        mm(R("B7", 0, 256), R("ID"), R("IX"), False, True)
+        act(R("XX"), R("B7", 0, 256), AF.Relu, cXB, 512.0)
+        mm(R("B7", 0, 256), R("BL8"), R("BAD", 1, 257), True, True)
+        mm(R("B5", 0, 256), R("BLK"), R("BAD", 1, 257), True, False)
+        mm(R("B5", 0, 256), R("X3"), R("BAD", 1, 257), False, True)
+        act(R("LE", 0, 256), R("B5", 0, 256), AF.Sign, -0.5)
+        tt(R("YY"), R("B7", 0, 256), R("XX"), mn)
+        mm(R("B6", 0, 16), R("ID"), R(OB), True, False)
+        mm(R("B6", 0, 16), R("ID"), R(G2), False, False)
+        mm(R("B6", 0, 16), S(0, "ZN"), R(G2), False, False)
         o, a = R("RM", 0, 1), R("YY")
         add("v", lambda: g.vector.tensor_reduce(val(o), val(a), AxisListType.X, mx), [a], [o], hold=256 * CY)
-        act(R("RS"), R("B2", 0, 384))
-        cp(R("LS"), R("B3", 0, 8))
         ts(R("SX", 0, 1), R("RM", 0, 1), -1.0, mul, 256.0, add_)
-        tt(R("EQ"), IND(R("LS"), R("L3")), R("RS"), AL.is_equal)
         tt(R("HH"), IND(R("LE"), R("SX", 0, 1)), R(G2), mul)
-        scan(R("SC"), R("FL"), R("EQ"), 0.0, mul, mx)
-        tt(R("LM"), R("SC", 47, 384, 48), R("LS"), mx)
-        mm(R("B1", 0, 16), R("K4"), R("HH"), False, True)
-        cp(R(MO, 16, 144), R("B4", 0, 128))
-        ts(R(MO, 0, 8), R("LM"), -1024.0, add_)
-        cp(R(MO, 144, 160), R("B1", 0, 16))
-        dst = prv if t == 0 else nxt
-        k = send("MI%d" % t, R(MO), relays(topo, core, dst)[0], "rm%d" % t)
-
-        mm(R("B6", 0, 128), R("BE"), R("XS", 1, 129), True, False)
-        mm(R("B6", 0, 128), R("BL4"), R("BAD", 1, 129), False, True)
-        mm(R("B7", 0, 256), R("BE"), R("XS", 1, 257), True, False)
-        mm(R("B7", 0, 128), R("ID"), R("MB"), False, False)
-        mm(R("B7", 128, 256), R("ID"), R("MB"), False, False)
-        mm(R("B7", 0, 256), R("BL4"), R("BAD", 1, 257), False, True)
-        mm(R("B0", 0, 16), R("ID32"), R("LX"), True, False)
-        for r in range(16):
-            mm(R("B0", 0, 16), S(r, "ZP"), R("BAD", 1 + r, 257, 16), False, r == 15)
-        act(R("RA"), R("B6", 0, 128))
-        act(R("RB"), R("B7", 0, 256))
-        cp(R("L2"), R("B0", 0, 16))
-        tt(R("E2"), IND(R("L2"), R("LB", 8, 16)), R("RA"), AL.is_equal)
-        tt(R("E1"), IND(R("L2"), R("LB")), R("RB"), AL.is_equal)
-        mm(R("B3", 0, 16), R("ID32"), R("L2"), True, False)
-        for r in range(16):
-            mm(R("B3", 8, 16), R("ID4"), R("E2", r, 128, 16), False, False)
-        for r in range(16):
-            mm(R("B3", 0, 16), R("ID4"), R("E1", r, 256, 16), False, r == 15)
-        ts(R("OA", 0, 16, 2), R("B3", 0, 8), cD3, mn)
-        ts(R("OA", 1, 16, 2), R("B3", 8, 16), cD4, mn)
-        for p in range(8):
-            cp(IND(R("TX"), R("OA", 2 * p, 2 * p + 2)), R("FV", 32 * p, 32 * p + 32))
-        return k
-
-    rl = relays(topo, core, prv)
-    wd = 2048 // len(rl)
-    trs = []
-    for k, c in enumerate(rl):
-        en = topo.engines(core, c)
-        h = len(en) // len(rl)
-        m = 0
-        for e in en[k * h:(k + 1) * h]:
-            m |= 1 << e
-        rid, pid = topo.addr(c, core)
-        trs.append(RemoteDMATransfer(dst_ids=[DstId(rid=rid, pnc=pid)], dma_engine_mask=m, remote_sem=T.sem.rp,
-                                     src=T.P0[:, k * wd:(k + 1) * wd], dst=T.P1[:, k * wd:(k + 1) * wd]))
-        sent[0] += h
+        mm(R("B6", 0, 16), R("ID"), R("HH"), False, False)
+        mm(R("B6", 0, 16), S(0, "ZN"), R("HH"), False, True)
+        act(R("O%d" % (t + 1), 0, 16), R("B6", 0, 16))
+        return ks
 
     def rows(name):
         return {"ap": T[name][0:128:16, 0:2048], "reg": [(name, 0, 2048)], "n": 1, "sz": 4}
 
-    far = relays(topo, nxt, core)
+    def take(t, ks):
+        for nm, k in zip("fab", ks):
+            arrive("%s%d" % (nm, t), k, HOP)
+        flip("TX%d" % (1 - t), "ON%d" % t, "FN%d" % t)
+
     cp(R("WP", 0, 128), R("WI"))
+    cp(R("O0", 0, 16), R("OI"))
+    ms(R("AR"), 0.0)
     starts(0)
+    kp_ = send("p", "lt", 1.5)
     starts(1)
-    k1 = add("g", lambda: g.remote_dma_fused(trs, local_sem=T.sem.ls), [R("P0")], [], "r", hold=1.5)
-    k2 = send("WL", R("WP", 0, 128), rl[1], "rw")
-    for nm in ("WR1", "WR0"):
-        for a in range(0, 2080, 520):
-            iota(R(nm, a, a + 520), [[0, 520]], 0, 0)
-    dma("s", rows("WR0"), R("WP", 0, 128))
-    arrive([R("P1")], "ap", sum(len(topo.engines(c, core)) for c in far), k1, 20.0)
-    arrive([R("WL")], "aw", len(topo.engines(far[1], core)), k2, 14.0)
-    dma("s", rows("WR1"), R("WL"))
-    ms(R("WR1", 0, 2048, 128), 0.0, "v")
-    cp(R("W0"), R("WR0", 0, 2048, 128))
-    k = round_(0)
-    arrive([R("MI0")], "am0", len(topo.engines(far[0], core)), k, HOP)
-    apply("WR1", "MI0")
-    apply("WR0", "MO0")
-    k = round_(1)
+    arrive("s", send("s"), 15.0)
+    arrive("v", send("v"), 30.0)
+    late = [[cp(R("OW1"), R("OWN"))], []]
+    ms(R("WR", 0, 548), 0.0)
+    for a in range(548, 2192, 548):
+        dma("s", R("WR", a, a + 548), R("WR", 0, 548), 4.0)
+    dma("s", rows("WR"), R("WP", 0, 128), 8.0)
+    cp(R("W0"), R("WR", 0, 2048, 128))
+    ms(R("WR", 0, 2048, 128), 0.0, "v")
+    arrive("p", kp_, 20.0)
+    ks = round_(0)
+    take(0, ks)
+    add("x", None, [], [R("TX0")], "x", ("lt", sent["lt"]), hold=0.0, lat=10.0, after=kp_)
+    flip("TX0", "OA0", "FV0")
+    ks = round_(1)
+    take(1, ks)
     for h, e in enumerate("sa"):
-        dma(e, X(T.yt[64 * h:64 * h + 64, :], "yt%d" % h), {"ap": T.TX[64 * h:64 * h + 64, 0:2048], "reg": [("TX", 0, 2048)], "n": 1, "sz": 2}, 4.0)
-    back = relays(topo, prv, core)[0]
-    arrive([R("MI1")], "am1", len(topo.engines(back, core)), k, HOP)
-    act_o = R("OO")
-    cp(act_o, R("MI1", 144, 160))
-    apply("WR0", "MI1")
-    cp(R("WR0", 0, 2048, 128), R("W0"))
-    dma("a", X(T.yo[:], "yo"), act_o)
-    dma("s", X(T.yw[:], "yw"), rows("WR0"))
+        dma(e, X(T.yt[64 * h:64 * h + 64, :], "yt%d" % h), {"ap": T.TX0[64 * h:64 * h + 64, TL:TH], "reg": [("TX0", TL, TH)], "n": 1, "sz": 2}, 3.2)
+        ops[-1]["tail"] = 3.2
+    cp(R("WR", 0, 2048, 128), R("W0"))
+    dma("a", X(T.yo[:], "yo"), R("O2"))
+    dma("s", X(T.yw[:], "yw"), rows("WR"))
 
     def meet(a, b):
         for x in a:
@@ -660,7 +642,7 @@ def rank_program(g, core, T, topo):
                 stack.extend((j, False) for j in ops[x]["dep"] | ops[x]["soft"] if j not in mark)
     for i in range(len(ops)):
         visit(i)
-    level = [0.0] * len(ops)
+    level = [o.get("tail", 0.0) for o in ops]
     for i in reversed(topo_):
         o = ops[i]
         level[i] += o["hold"]
@@ -671,7 +653,7 @@ def rank_program(g, core, T, topo):
     busy = {}
     for i in sorted(range(len(ops)), key=lambda x: (-level[x], x)):
         o = ops[i]
-        t0 = 1.0
+        t0 = 0.5
         for j in o["dep"]:
             t0 = max(t0, ops[j]["end"] + ops[j]["lat"] + WAKE)
         for j in o["soft"]:
@@ -721,7 +703,7 @@ def rank_program(g, core, T, topo):
             cnt[o["e"]] += 1
             o["tok"] = (T.sem["s" + o["e"]], cnt[o["e"]])
             ins.then_inc(o["tok"][0], 1)
-    g.wait_ge(T.sem.ls, sent[0])
+    g.wait_ge(T.sem.ls, sent["ls"])
     for o in ops:
         if o["k"] == "d" and not o.get("sig"):
             g.wait_ge(o["tok"][0], 16)

@@ -5,26 +5,26 @@ F, B, U, I, H = "float32", "bfloat16", "uint16", "int32", "float16"
 SIZE = {F: 4, B: 2, U: 2, I: 4, H: 2}
 
 OWN = {"TX0": (2112, B), "TX1": (2112, B), "P0": (2048, B), "WP": (136, F), "WR": (2192, F),
-       "DG": (2048, B), "GW": (1024, B), "Y": (1024, B), "NJ": (1024, B), "NI": (1024, B), "WN": (8800, B), "PX": (4096, B),
-       "NQ": (4096, B), "CD": (128, I), "WI": (128, I), "OI": (16, I), "AR": (512, B),
-       "SO": (200, F), "SN": (200, F), "VO": (512, B), "V1": (512, B),
+       "DG": (2048, B), "GW": (1024, B), "Y": (1024, B), "NJ": (1024, B), "NI": (1024, B), "QI": (1024, B), "WN": (8800, B),
+       "PX": (4096, B), "NQ": (4096, B), "CD": (128, I), "WI": (128, I), "OI": (16, I), "AR": (512, B), "ZB": (528, B),
+       "SO": (136, F), "SN": (136, F), "VO": (512, B), "V1": (512, B), "OWO": (64, U), "OW1": (64, U),
        "HL0": (128, B), "HL1": (128, B), "O2": (16, F), "OA0": (24, U), "OA1": (24, U), "ON0": (24, U), "ON1": (24, U),
-       "FV0": (256, B), "FV1": (256, B), "FN0": (256, B), "FN1": (256, B)}
+       "OX0": (16, U), "OX1": (16, U), "XN0": (16, U), "XN1": (16, U)}
 SMALL = {
-    F: {"W0": 16, "O0": 32, "O1": 32, "KC": 16, "NR": 264, "ID32": 128, "R16": 16, "R32": 16, "RLT": 8,
-        "DUMP": 32, "NDU": 32, "RMK": 16, "C128": 16, "BT0": 128, "ZT0": 128, "BT1": 128, "ZT1": 128, "A0": 64,
-        "ND0": 64, "ND1": 64, "NA0": 72, "DT": 64, "TP": 64, "LF": 72, "NN": 64, "ND2": 32, "AL1": 64, "T1": 64,
-        "T2": 64, "KL": 64, "TH": 64, "TM": 32, "ANY": 32, "XD": 32, "SE": 8, "TO": 16, "SC": 392, "FL": 392,
-        "EQ": 392, "TQ": 64, "RM": 8, "SF": 408, "RX": 408},
-    B: {"OB0": 16, "OB1": 16, "ID": 128, "NID": 128, "IDB": 128, "ID4": 128, "IDN4": 128, "BLK": 128, "BLM8": 128, "BL8": 128,
-        "M2": 128, "TRI": 128, "TRI2": 128, "M1": 128, "HE": 128, "HO": 128, "HX": 128,
-        "BD": 128, "NBD": 128, "BP": 128, "Z2": 144, "ZE": 144, "ZN": 144, "ZH": 144, "XS": 264, "BE": 128, "BO": 128,
-        "X3": 128, "X4": 128, "NX4": 128, "Z": 144, "ZQ": 144, "SG": 408, "RS": 392, "ALT": 256,
-        "PAD": 32, "IX": 256, "C0": 64, "KJ": 72, "AL2": 64, "CUM": 64, "V0": 512, "PO0": 272, "PO1": 272,
-        "SGE": 256, "OG": 256, "PEN": 256, "XX": 256, "BAD": 264, "UU": 256, "UD": 256, "YY": 256, "LE": 264, "G0": 16,
-        "G1": 16, "HH": 16, "MP": 408, "MV": 128},
-    U: {"LV": 32, "OW0": 64, "OW1": 64, "OY": 64, "OJ": 64, "OP": 64, "OW2": 32, "OS": 32, "OTU": 256, "OPO": 256,
-        "OPT": 16, "PL": 16, "SX": 2, "OX": 16, "OF": 8},
+    F: {"W0": 16, "KC": 24, "NR": 264, "ID32": 128, "R16": 16, "R32": 16, "RH": 2, "TP": 64,
+        "DUMP": 32, "NDU": 32, "RMK": 16, "BT0": 128, "ZT0": 128, "BT1": 128, "ZT1": 128, "A0": 64,
+        "ND0": 64, "ND1": 64, "NA0": 72, "LF": 72, "NN": 64, "ND2": 32, "AL1": 64, "T1": 64,
+        "T2": 64, "T3": 32, "KL": 64, "TH": 64, "TM": 32, "ANY": 32, "XD": 32, "SE": 8, "SC": 392, "FL": 392,
+        "EQ": 392, "NL": 8, "RM": 8, "SF": 408, "RX": 408, "CO0": 1, "CO1": 1},
+    B: {"OB0": 32, "OB1": 32, "ID": 128, "NID": 128, "IDB": 128, "ID4": 128, "C256": 128, "ID5": 128, "BLK": 128,
+        "BL8": 128, "M2": 128, "TRI": 128, "TRI2": 128, "M1": 128, "HE": 128, "HO": 128, "BX": 128, "BR0": 128, "PW": 8,
+        "FV": 256, "FN": 256, "BD": 128, "NBD": 128, "BP": 128, "Z0": 144, "ZE": 144, "ZH": 144, "XS": 264,
+        "BE": 128, "BO": 128, "IDB2": 128, "ZQ2": 144, "X3": 128, "X4": 128, "NX5": 128, "Z": 144, "ZQ": 144, "SG": 408,
+        "RS": 392, "ALT": 256, "PAD": 32, "IX": 256, "C0": 64, "HALF": 72, "C128": 16, "KJ": 72, "AL2": 64, "CUM": 64,
+        "V0": 512, "PO0": 272, "PO1": 272, "BDO": 256, "LT0": 128, "LT1": 128, "SGE": 256, "OG": 256, "PEN": 256,
+        "BAD": 264, "UU": 256, "UD": 256, "LE": 264, "G0": 16, "G1": 16, "HH": 16, "MP": 408, "MV": 128},
+    U: {"LV": 32, "LBD": 16, "OW0": 64, "OY": 64, "OJ": 64, "OP": 64, "OW2": 32, "OS": 32, "OTU": 256, "OPO": 256,
+        "OPT": 16, "SX": 2, "OF": 8},
     I: {"KI": 8},
     H: {"NIH": 128, "LH": 16},
 }
@@ -43,19 +43,23 @@ for _k in range(8):
     SCRATCH["B%d" % _k] = ("psum", [128, 512], F)
     PLACE["B%d" % _k] = ("B%d" % _k, 0, 512, 4)
 
-for _k, _b, _o, _n in (("AO", "SO", 0, 64), ("NAO", "SO", 64, 72), ("OWO", "SO", 136, 64),
-                       ("A1", "SN", 0, 64), ("NA1", "SN", 64, 72), ("OWN", "SN", 136, 64)):
+for _k, _b, _o, _n in (("AO", "SO", 0, 64), ("NAO", "SO", 64, 72), ("A1", "SN", 0, 64), ("NA1", "SN", 64, 72)):
     PLACE[_k] = (_b, _o, _n, 4)
 
-NDMA = 24
-MSG = ["p", "s", "v", "f0", "a0", "b0", "f1", "a1", "b1"]
+NDMA = 28
+MSG = ["p", "v", "s", "w", "x0", "a0", "b0", "x1", "a1", "b1"]
 SEMAPHORES = (["sv", "sa", "st", "sg", "ls", "lt"] + ["r" + m for m in MSG] + ["a" + m for m in MSG]
               + ["d%d" % k for k in range(NDMA)])
-BIG = 1.0e6
+BIG, HUGE = 1.0e6, 1.0e9
 SA = 192
+SF = 96
 TL, TH = 32, 2080
-CY, PE, WAKE, HOP = 1.04e-3, 0.52e-3, 0.1, 4.0
-WSPLIT = 40
+WL = 128
+WSPLIT = 48
+ZI = {64: 32, 32: 8}
+EA = 5
+PASSES = 4
+CY, PE, FIX, WAKE, HOP = 1.0e-3, 0.5e-3, 0.07, 0.11, 3.6
 
 
 def relays(topo, src, dst):
@@ -70,10 +74,11 @@ def messages(T, topo, src):
     rl = relays(topo, src, nxt)
     wd = (TH - TL) // len(rl)
     out = [("p", c, nxt, ("TX0", TL + k * wd, TL + (k + 1) * wd), ("TX1", TL + k * wd, TL + (k + 1) * wd)) for k, c in enumerate(rl)]
-    out += [("s", rl[1], nxt, ("SO", 0, 200), ("SN", 0, 200)), ("v", rl[3], nxt, ("VO", 0, 512), ("V1", 0, 512))]
+    out += [("v", rl[3], nxt, ("VO", 0, 512), ("V1", 0, 512)), ("s", rl[1], nxt, ("SO", 0, 136), ("SN", 0, 136)),
+            ("w", rl[0], nxt, ("OWO", 0, 64), ("OW1", 0, 64))]
     for t, dst in enumerate((nxt, prv)):
         rl = relays(topo, src, dst)
-        out += [("f%d" % t, rl[2], dst, ("FV%d" % t, 0, 256), ("FN%d" % t, 0, 256)),
+        out += [("x%d" % t, rl[2], dst, ("OX%d" % t, 0, 16), ("XN%d" % t, 0, 16)),
                 ("a%d" % t, rl[1], dst, ("OA%d" % t, 0, SA // 16), ("ON%d" % t, 0, SA // 16)),
                 ("b%d" % t, rl[0], dst, ("OA%d" % t, 16, 32 - SA // 16), ("ON%d" % t, 16, 32 - SA // 16))]
     return out
@@ -138,19 +143,19 @@ def rank_program(g, core, T, topo):
             elif any("off" in x for x in rd):
                 hold = 0.06 + 1.56 * m * CY
             elif e == "a":
-                hold = 0.05 + max(64, m) * CY
+                hold = FIX + max(64, m) * CY
             else:
-                hold = max(64, m * (0.5 if all(x["sz"] == 2 for x in rd + wr if x["n"] > 1) else 1)) * CY
+                hold = FIX + max(64, m * (0.5 if all(x["sz"] == 2 for x in rd + wr if x["n"] > 1) else 1)) * CY
         ops.append({"e": e, "fn": fn, "r": r_, "w": w_, "k": kind, "ext": ext, "hold": hold, "lat": lat, "after": after})
         return len(ops) - 1
 
-    chain = [None]
+    chain, lasta = [None], [None]
 
     def tt(o, a, b, op):
         two = "off" not in a and a["reg"][0][0][0] != "B" and b["reg"][0][0][0] != "B"
         k = add("v", lambda: g.vector.tensor_tensor(val(o), val(a), val(b), op), [a, b], [o])
-        if two and o["n"] > 32:
-            ops[k]["hold"] *= 2
+        if two:
+            ops[k]["hold"] = FIX + max(64, o["n"] * (1 if o["sz"] == a["sz"] == b["sz"] == 2 else 2)) * CY
         if op == AL.not_equal:
             ops[k]["after"] = chain[0]
             chain[0] = k
@@ -166,34 +171,33 @@ def rank_program(g, core, T, topo):
     def cp(o, a):
         return add("v", lambda: g.vector.tensor_copy(val(o), val(a)), [a], [o])
 
-    def ms(o, c, eng="g"):
-        if eng == "g":
-            iota(o, [[0, o["n"]]], int(c), 0)
-        else:
-            add("v", lambda: g.vector.memset(val(o), c), [], [o])
+    def ms(o, c):
+        return iota(o, [[0, o["n"]]], int(c), 0)
 
     def scan(o, d0, d1, init, op0, op1):
         return add("v", lambda: g.vector.tensor_tensor_scan(val(o), val(d0), val(d1), init, op0, op1), [d0, d1], [o],
-                   hold=max(64, o["n"]) * CY)
+                   hold=FIX + max(64, o["n"]) * CY)
 
     def act(o, a, f=AF.Identity, bias=0.0, scale=1.0):
         return add("a", lambda: g.scalar.activation(val(o), val(a), f, bias=val(bias), scale=val(scale)), [a, bias, scale], [o])
 
+    def lin(o, a, bias=0.0, scale=1.0):
+        return act(o, a, AF.Identity, bias, scale)
+
     def mm(o, l, r_, st, sp):
         return add("t", lambda: g.tensor.matmul(val(o), val(l), val(r_), st, sp), [l, r_], [o],
-                   hold=max(64, r_["n"]) * PE * (4 if r_["sz"] == 4 else 1), lat=0.1)
+                   hold=max(64, r_["n"]) * PE * (4 if r_["sz"] == 4 else 1), lat=0.08)
 
     def iota(o, pat, base, cm, fl=True):
         if fl:
-            add("g", lambda: g.iota(val(o), pat, base, cm, allow_small_or_imprecise_dtypes=True), [], [o], hold=0.13 + 2 * o["n"] * CY)
-        else:
-            add("g", lambda: g.iota(val(o), pat, base, cm), [], [o], hold=0.13 + 2 * o["n"] * CY)
+            return add("g", lambda: g.iota(val(o), pat, base, cm, allow_small_or_imprecise_dtypes=True), [], [o], hold=0.13 + 2 * o["n"] * CY)
+        return add("g", lambda: g.iota(val(o), pat, base, cm), [], [o], hold=0.13 + 2 * o["n"] * CY)
 
     def pick(o, a, pat, op, fill, base, cm):
         add("g", lambda: g.affine_select(val(o), val(a), pat, op, fill, base, cm), [a], [o], hold=0.17 + 2 * o["n"] * CY)
 
     def dma(e, o, a, lat=2.4):
-        add(e, lambda: Q[e].dma_start(val(o), val(a)), [a], [o], "d", hold=0.1, lat=lat)
+        return add(e, lambda: Q[e].dma_start(val(o), val(a)), [a], [o], "d", hold=0.1, lat=lat)
 
     def X(ap, name):
         return {"ap": ap, "reg": [(name, 0, 1 << 20)], "n": 1, "sz": 4}
@@ -202,7 +206,7 @@ def rank_program(g, core, T, topo):
     coming = [m for c in T.cores if c != core for m in messages(T, topo, c) if m[2] == core]
     sent = {"ls": 0, "lt": 0}
 
-    def send(name, sem="ls", hold=0.5):
+    def send(name, sem="ls", hold=0.6):
         parts = [m for m in mine if m[0] == name]
         trs = []
         for k, (_, via, _, s_, d_) in enumerate(parts):
@@ -231,82 +235,89 @@ def rank_program(g, core, T, topo):
     def D(p):
         return R("DG", 128 * p, 128 * p + 128)
 
-    cK, cR, cG16, cM0, cM1, c128b, cN128, cBO, cBD, cBN, cBM, cXB, cGS = [R("KC", k, k + 1) for k in range(13)]
+    cR, cG16, cM1, cK, cM0, c128b, cN128, cBE, cBD, cBN, cBM, cSX, cGS, cNR, cR1, cR2 = [R("KC", k, k + 1) for k in range(16)]
     kK, kR, kG, kH = [R("KI", k, k + 1) for k in range(4)]
     c32, c128, c256 = [R("R32", k, k + 1) for k in (1, 4, 8)]
     cLD, cMM = [cR, R("R16", 1, 2)], R("R16", 8, 9)
-    cHD = [R("FL", 97, 98), R("FL", 146, 147)]
-    cR0, cE2, cE3, cBE, cB4 = R("RMK", 0, 1), R("RMK", 2, 3), R("RMK", 3, 4), R("RLT", 2, 3), R("RLT", 4, 5)
+    cHD = [R("RH", 0, 1), R("RH", 1, 2)]
+    cR0, cE3, cE4 = R("RMK", 0, 1), R("RMK", 3, 4), R("RMK", 4, 5)
     add_, sub, mul, mx, mn = AL.add, AL.subtract, AL.mult, AL.max, AL.min
     ne, gt, ge, eq = AL.not_equal, AL.is_gt, AL.is_ge, AL.is_equal
     N128 = R("NR", 0, 128)
 
-    dma("s", R("CD"), X(T.cd[:], "cd"))
-    dma("a", R("WI"), X(T.wit[:], "wit"))
+    dma("s", R("CD"), X(T.cd[:], "cd"), 2.0)
+    dma("a", R("WI"), X(T.wit[:], "wit"), 2.0)
     dma("s", R("TX0", TL, TH), X(T.txt[:], "txt"), 4.0)
     dma("a", R("P0"), X(T.pat[:], "pat"), 4.0)
     dma("s", R("OI"), X(T.prb[:], "prb"))
     hints.extend([[0, 2, 4], [1, 3]])
 
     diag = [[1, 128]]
-    iota(kK, [[0, 1]], 0, 1, False)
-    iota(R("NR"), [[1, 264]], 0, 0)
+    k1 = iota(kK, [[0, 1]], 0, 1, False)
+    k2 = iota(R("NR"), [[1, 264]], 0, 0)
+    k3 = iota(cK, [[0, 1]], 0, 1)
+    k4 = ms(R("BLK"), 1.0)
+    hints.append([k1, k3, k2, k4])
     ms(R("WP", 128, 136), 0.0)
     ts(kR, kK, 15, AL.bitwise_and)
-    ts(kG, kK, 4, AL.arith_shift_right)
+    ts(kG, kK, 112, AL.bitwise_and)
     ts(kH, kK, 4, AL.arith_shift_right, 1, AL.bitwise_and)
-    cp(cK, kK)
-    cp(cR, kR)
-    ts(cG16, kG, 16.0, mul)
-    cp(cM1, kH)
-    ts(cM0, kH, -1.0, mul, 1.0, add_)
+    cp(R("KC", 0, 3), R("KI", 1, 4))
+    lin(cM0, cM1, 1.0, -1.0)
     ts(R("ID"), N128, cK, eq)
     ts(R("RMK"), R("NR", 0, 16), cR, eq)
-    for p in range(7):
-        act(D(p), R("ID"), AF.Identity, 0.0, R("RMK", p, p + 1))
-    for p in range(7, 16):
+    for p in range(8):
+        lin(D(p), R("ID"), 0.0, R("RMK", p, p + 1))
+    for p in range(8, 16):
         ts(D(p), R("ID"), R("RMK", p, p + 1), mul)
-    ts(R("R16", 0, 9), R("NR", 0, 144, 16), cR, add_)
-    ts(R("R32", 0, 9), R("NR", 0, 264, 32), cR, mul)
-    ts(R("RLT"), R("NR", 0, 8), cR, gt)
+    lin(R("R16", 0, 9), R("NR", 0, 144, 16), cR)
+    lin(R("R32", 0, 9), R("NR", 0, 264, 32), 0.0, cR)
     ts(R("Z"), R("NR", 0, 144), cG16, sub, 15.0, eq)
-    ts(R("DUMP"), R("NR", 0, 32), c32, add_, 6201.0, add_)
     ts(R("LV"), R("NR", 0, 32), c32, add_)
     ms(R("KJ", 0, 1), 0.0)
     ms(R("LF", 0, 1), -2048.0)
-    ms(R("BLK"), 1.0)
-    pick(R("BLK"), R("BLK"), [[-16, 8], [0, 16]], ge, 0.0, 0, 1)
-    pick(R("BLK"), R("BLK"), [[16, 8], [0, 16]], ge, 0.0, 15, -1)
-    pick(R("TRI"), R("BLK"), diag, gt, 0.0, 0, -1)
-    pick(R("TRI2"), R("BLK"), diag, ge, 0.0, 0, -1)
-    pick(R("X4"), R("BLK"), diag, eq, 0.0, -1, -1)
-    for nm, of, sc in (("ID32", "ID", 1.0), ("IDB", "ID", 262144.0), ("NID", "ID", -1.0), ("ID4", "ID", 4096.0), ("HE", "ID", cBE),
-                       ("IDN4", "ID", -4096.0), ("ZQ", "Z", -16384.0), ("ZH", "Z", -64.0), ("ZN", "Z", -1.0), ("Z2", "Z", cE2),
-                       ("ZE", "Z", cBE), ("BLM8", "BLK", -8.0), ("BL8", "BLK", 8192.0), ("M2", "BLK", -256.0), ("BE", "BLK", cBE),
-                       ("BP", "BLK", cE2), ("X3", "TRI", -32.0), ("NX4", "X4", -1.0), ("HX", "X4", cR0)):
-        act(R(nm), R(of), AF.Identity, 0.0, sc)
-    for o, a, bias, sc in ((c128b, c128, 128.0, 1.0), (cN128, c128, 0.0, -1.0), (cBO, cBE, cB4, -1.0), (cBD, cE2, cBE, 4096.0),
-                           (cBN, cBD, 0.0, -1.0), (cBM, cE3, cBD, -128.0), (cXB, cR0, -1024.0, 512.0), (cGS, cR0, 0.5, -0.5),
-                           (R("NDU"), R("DUMP"), 1.0, -1.0), (R("C128"), R("NR", 0, 16), 0.0, 128.0),
-                           (R("IX"), R("NR", 0, 256), 0.5, -1.0 / 512),
-                           (R("BO"), R("BLK"), 0.0, cBO), (R("BD"), R("BLK"), 0.0, cBM), (R("NBD"), R("BLK"), 0.0, cBN)):
-        act(o, a, AF.Identity, bias, sc)
-    pick(R("HO"), R("BO"), diag, eq, 0.0, 2, -1)
-    pick(R("M1"), R("M2"), diag, gt, 0.0, 0, -1)
-    pick(R("M1"), R("M1"), diag, ne, 128.0, 0, -1)
+    up, down = [[-16, 8], [0, 16]], [[16, 8], [0, 16]]
+    wide = [[1, 144]]
+    for nm, c in (("BL8", 8192.0), ("C256", 256.0), ("HALF", 17.0)):
+        ms(R(nm), c)
+    iota(R("C128"), [[128, 16]], 0, 0)
+    iota(R("IX"), [[-1, 256]], 256, 0)
+    ts(R("DUMP"), R("NR", 0, 32), c32, add_, 6201.0, add_)
+    for o, a, bias, sc in ((c128b, c128, 128.0, 1.0), (cN128, c128, 0.0, -1.0), (cBE, cR0, R("RMK", 1, 2), 1.0), (cBD, cE3, cBE, 4096.0),
+                           (cBN, cBD, 0.0, -1.0), (cBM, cE4, cBD, -128.0), (cSX, cR0, 1024.0, -256.0), (cGS, cR0, -0.5, 0.5),
+                           (cNR, cR, 0.0, -1.0), (R("KC", 14, 16), R("NR", 1, 3), cR, 1.0), (R("RH"), R("R16", 0, 2), float(TH), 1.0),
+                           (R("NDU"), R("DUMP"), 1.0, -1.0)):
+        lin(o, a, bias, sc)
+    pick(R("BLK"), R("BLK"), up, ge, 0.0, 0, 1)
+    pick(R("BLK"), R("BLK"), down, ge, 0.0, 15, -1)
+    for nm, of, sc in (("ID32", "ID", 1.0), ("IDB", "ID", 8192.0), ("NID", "ID", -1.0), ("ID4", "ID", 4096.0),
+                       ("IDB2", "ID", 8192.0 * 256), ("ZQ2", "Z", -16384.0 * 256), ("ZQ", "Z", -16384.0), ("ZH", "Z", -64.0),
+                       ("M2", "BLK", -256.0), ("BD", "BLK", cBM), ("NBD", "BLK", cBN)):
+        lin(R(nm), R(of), 0.0, sc)
+    for nm, of, pat, op, fill, base, cm in (
+            ("TRI", "BLK", diag, gt, 0.0, 0, -1), ("TRI2", "BLK", diag, ge, 0.0, 0, -1), ("X4", "BLK", diag, eq, 0.0, -1, -1),
+            ("BE", "BLK", down, ge, 0.0, 1, -1), ("BX", "BLK", down, ge, 0.0, 2, -1), ("BP", "BLK", up, eq, 0.0, -3, 1),
+            ("BO", "BLK", up, ge, 0.0, -2, 1), ("BO", "BO", down, ge, 0.0, 3, -1), ("HO", "BO", diag, eq, 0.0, 2, -1),
+            ("HE", "BE", diag, eq, 0.0, 0, -1), ("ZE", "Z", wide, ge, 0.0, -13, -1), ("Z0", "Z", wide, eq, 0.0, -15, -1),
+            ("BL8", "BL8", up, ge, 0.0, 0, 1), ("BL8", "BL8", down, ge, 0.0, 15, -1), ("ID5", "C256", diag, eq, 0.0, 0, -1),
+            ("BR0", "C256", up, eq, 0.0, 0, 1), ("NX5", "M2", diag, eq, 0.0, -1, -1), ("X3", "M2", diag, gt, 0.0, 0, -1),
+            ("M1", "X3", diag, ne, 128.0, 0, -1)):
+        pick(R(nm), R(of), pat, op, fill, base, cm)
+    for h, c in enumerate((cR1, cR2)):
+        ts(R("LBD", 8 * h, 8 * h + 8), R("NR", 0, 128, 16), cG16, eq, c, mul)
     cp(R("NIH"), R("NID"))
     for t in range(2):
-        ms(R("O%d" % t, 16, 32), 200.0)
+        ms(R("OB%d" % t), 0.0)
         ms(R("PO%d" % t, 256, 272), 999.0)
     ms(R("PAD"), 8192.0)
+    ms(R("T2", 1, 64, 2), 0.0)
     iota(R("ALT"), [[0, 128], [1, 2]], 0, 0)
-    iota(R("RS"), [[0, 8], [1, 49]], -16, 0)
-    act(R("RS"), R("RS"), AF.Sign, cR)
-    act(R("FL"), R("RS"), AF.Abs)
-    ts(R("FL", 48, 392, 49), R("NR", 0, 128, 16), cR, add_, TH - 16.0, add_)
+    iota(R("RS"), [[0, 8], [-1, 49]], 16, 0)
+    ts(R("FL"), R("RS"), cR, eq, BIG, mul)
+    lin(R("FL", 48, 392, 49), R("NR", 0, 128, 16), cR)
     iota(R("MP"), [[0, 24], [1, 17]], 0, 0)
     pick(R("MP"), R("MP"), [[0, 8], [1, 3], [0, 17]], gt, -100.0, 0, 0)
-    act(R("SG"), R("MP"), AF.Sign, cR, -1.0)
+    act(R("SG"), R("MP"), AF.Sign, cNR)
     ms(R("RX"), 0.0)
     ms(R("RX", 0, 408, 51), BIG)
     ms(R("RX", 34, 408, 51), BIG)
@@ -322,194 +333,206 @@ def rank_program(g, core, T, topo):
         for q in range(4):
             o, a = R(ZT, 32 * q, 32 * q + 32), R(BT, q, 128, 4)
             add("v", lambda o=o, a=a: g.vector.transpose(val(o), val(a)), [a], [o])
-        for q in range(4):
-            tt(R(A, 16 * q, 16 * q + 16), R(ZT, 32 * q, 32 * q + 16), R(ZT, 32 * q + 16, 32 * q + 32), add_)
-        ms(R(ND, 63, 64), -200.0)
         ms(R(NA, 64, 72), -4000.0)
-        tt(R(ND, 0, 63), R(A, 0, 63), R(A, 1, 64), sub)
         if t == 0:
+            for q in range(4):
+                tt(R(A, 16 * q, 16 * q + 16), R(ZT, 32 * q, 32 * q + 16), R(ZT, 32 * q + 16, 32 * q + 32), add_)
+            ms(R(ND, 63, 64), -200.0)
+            tt(R(ND, 0, 63), R(A, 0, 63), R(A, 1, 64), sub)
             ts(R(OW), R(ND), -1.0, mul, 128.0, mn)
-            act(R(NA, 0, 64), R(A), AF.Identity, 0.0, -1.0)
+            lin(R(NA, 0, 64), R(A), 0.0, -1.0)
         else:
-            ts(R("DT"), R(ND), -1.0, mul, 128.0, mn)
-            act(R(NA, 0, 64), R(A), AF.Identity, cN128, -1.0)
-            act(R(OW), R("DT"), AF.Identity, c128)
+            for q in range(8):
+                mm(R("B6", 16 * (q // 2), 16 * (q // 2) + 16), R("ID32"), R(ZT, 16 * q, 16 * q + 16), q == 0, q == 7)
+            lin(R(A), R("B6", 0, 64))
+            lin(R(NA, 0, 64), R(A), cN128, -1.0)
+            mm(R("B6", 0, 64), R("ID32"), R(A), True, False)
+            mm(R("B6", 0, 64), R("ID32"), R(NA, 1, 65), False, True)
+            ts(R(OW), R("B6", 0, 64), -1.0, mul, c128b, mn)
         for h in range(2):
-            act(R(HL, 64 * h, 64 * h + 32), R(A, h, 64, 2))
-            tt(R(HL, 64 * h + 32, 64 * h + 64), R(A, h, 64, 2), R(HL, 64 * h, 64 * h + 32), sub)
+            lin(R(HL, 64 * h, 64 * h + 32), R(A, h, 64, 2))
+            mm(R("B7", 32 * h, 32 * h + 32), R("ID32"), R(A, h, 64, 2), h == 0, False)
+        for h in range(2):
+            mm(R("B7", 32 * h, 32 * h + 32), R("NID"), R(HL, 64 * h, 64 * h + 32), False, h == 1)
+        for h in range(2):
+            lin(R(HL, 64 * h + 32, 64 * h + 64), R("B7", 32 * h, 32 * h + 32))
         for v in range(4):
-            dma("s", {"ap": T.AR[v:128:16, :], "reg": [("AR", v, 512, 4)], "n": 1, "sz": 2}, R(HL, 32 * v, 32 * v + 32))
+            dma("s", {"ap": T.AR[v:128:16, :], "reg": [("AR", v, 512, 4)], "n": 1, "sz": 2}, R(HL, 32 * v, 32 * v + 32), 3.0)
         return act(R(V), IND(R("AR"), R("LV")))
 
-    def wlook(t, off, k, base, h):
-        win = R("WP", 0, 136) if t == 0 else R("WR", 0, 2056)
+    def duel(t, off, k, h, base, nd, cj):
+        win = R("WP", 0, 136) if t == 0 else R("WR", WL, WL + 2056)
         act(R("GW", 0, 16 * h), IND(win, R(off, 0, h)))
         cp(R("GW", 16 * h, 16 * k), IND(win, R(off, h, k)))
         mm(R("B0", 0, k), R("ID32"), base, True, False)
-        for p in range(16):
-            mm(R("B0", 0, k), D(p) if t == 0 else S(p), R("GW", p, 16 * k, 16), False, p == 15)
-
-    def duel(t, k, base, nd, cj, midj):
-        w = R("B0", 0, k)
-        cp(R("OY", 0, k), w)
-        tt(R("TP", 0, k), w, nd, add_)
-        tt(R("TQ", 0, k), w, base, sub)
+        last = []
+        for bk in ("B0", "B4"):
+            for p in range(16):
+                j = mm(R(bk, 0, k), D(p) if t == 0 else S(p), R("GW", p, 16 * k, 16), bk == "B4" and p == 0, p == 15)
+            last += [j - 15, j]
+        hints.append(last[1:3])
+        cp(R("OY", 0, k), R("B0", 0, k))
+        tt(R("TP", 0, k), R("B0", 0, k), nd, add_)
         ts(R("OJ", 0, k), R("TP", 0, k), cj, add_)
-        ts(R("OP", 0, k), R("TQ", 0, k), c128, add_)
-        ts(R("C0", 0, k), R("TQ", 0, k), 0.0, eq, 0.53125, add_)
-        cuts = [0, 10, 32, 64] if k == 64 else [0, 10, 32]
+        ts(R("OP", 0, k), R("B4", 0, k), c128, add_)
+        cuts = [0, 10, 32, 64] if k == 64 else [0, 6, 18, 32]
         for a, b in zip(cuts, cuts[1:]):
-            act(R("Y", 16 * a, 16 * b), IND(R("TX%d" % t, TL, TH), R("OY", a, b)))
-        mm(R("B1", 0, k), R("IDB"), R("C0", 0, k), True, False)
-        mm(R("B2", 0, k), R("IDB"), R("C0", 0, k), True, False)
+            ky = act(R("Y", 16 * a, 16 * b), IND(R("TX%d" % t, TL, TH), R("OY", a, b)))
+        kc = act(R("C0", 0, k), R("B4", 0, k), AF.Relu, 32.0, -32.0)
+        z = k - ZI[k]
+        lasta[0] = act(R("QI", 16 * z, 16 * k), IND(R("P0"), R("OP", z, k)))
+        hints.append([ky, lasta[0], kc])
+        big = "" if k == 64 else "2"
+        mm(R("B1", 0, k), R("IDB" + big), R("HALF", 0, k), True, False)
+        mm(R("B2", 0, k + 1), R("IDB"), R("HALF", 0, k + 1), True, False)
         for a, b in zip(cuts, cuts[1:]):
             tt(R("NJ", 16 * a, 16 * b), IND(R("P0"), R("OJ", a, b)), R("Y", 16 * a, 16 * b), ne)
-            if b <= 32 and k == 64:
-                tt(R("NI", 16 * a, 16 * b), IND(R("P0"), R("OP", a, b)), R("Y", 16 * a, 16 * b), ne)
+            if a < z:
+                e = min(b, z)
+                tt(R("NI", 16 * a, 16 * e), IND(R("P0"), R("OP", a, e)), R("Y", 16 * a, 16 * e), ne)
+        tt(R("NI", 16 * z, 16 * k), R("QI", 16 * z, 16 * k), R("Y", 16 * z, 16 * k), ne)
+        mm(R("B1", 0, k), R("IDB" + big), R("C0", 0, k), False, False)
+        mm(R("B2", 0, k), R("IDB"), R("C0", 0, k), False, False)
         for p in range(16):
-            mm(R("B1", 0, k), S(p, "ZQ"), R("NJ", p, 16 * k, 16), False, p == 15)
-        a = 32 if k == 64 else 0
-        tt(R("NI", 16 * a, 16 * k), IND(R("P0"), R("OP", a, k)), R("Y", 16 * a, 16 * k), ne)
+            mm(R("B1", 0, k), S(p, "ZQ" + big), R("NJ", p, 16 * k, 16), False, p == 15)
         for p in range(16):
             mm(R("B2", 0, k), S(p, "ZQ"), R("NI", p, 16 * k, 16), False, p == 15 and k == 32)
-        midj()
 
-    def flip(tx, off, new):
+    def flip(tx, may, off, new):
+        k = act(R(new), IND(R(tx, TL, TH), R(may)), AF.Identity, 255.0, -1.0)
         for q in range(8):
             c = 2 * q if 32 * q < SA else 16 + 2 * q - SA // 16
-            cp(IND(R(tx), R(off, c, c + 2)), R(new, 32 * q, 32 * q + 32))
+            calls.append(cp(IND(R(tx), R(off, c, c + 2)), R(new, 32 * q, 32 * q + 32)))
+        return k
+
+    calls, named = [], []
 
     def round_(t):
-        A, O, OB, PO, G2, TX, OA, FV = [x + str(t) for x in ("A", "O", "OB", "PO", "G", "TX", "OA", "FV")]
-        text = R(TX, TL, TH)
-        tt(R("TO"), R(O, 0, 16), R("C128"), add_)
-        act(R(OB), R(O, 0, 16))
-        cp(R("OPT"), R("TO"))
+        A, OB, PO, G2, TX, OA, OX, LT, CO = [x + str(t) for x in ("A", "OB", "PO", "G", "TX", "OA", "OX", "LT", "CO")]
+        text, places = R(TX, TL, TH), R(OB, 1, 17)
+        mm(R("B5", 0, 16), R("ID"), places, True, False)
+        mm(R("B5", 0, 16), R("ID"), R("C128"), False, True)
+        cp(R("OPT"), R("B5", 0, 16))
         kpo = act(R(PO, 0, 256), IND(R("P0"), R("OPT")))
-        ops[kpo]["lat"] = 4.0
-        mm(R("B5", 0, 16), R("X4"), R(OB), True, False)
-        mm(R("B5", 0, 16), R("NID"), R(OB), False, True)
-        act(R(G2), R("B5", 0, 16), AF.Identity, 0.0, cGS)
-        iota(R("WN", 0, 528), [[0, 528]], 0, 0)
-        iota(R("WN", 4096, 4624), [[0, 528]], 0, 0)
+        mm(R("B5", 0, 16), R("X4"), places, True, False)
+        mm(R("B5", 0, 16), R("NID"), places, False, True)
+        lin(R(G2), R("B5", 0, 16), 0.0, cGS)
+        act(R("BDO"), IND(R(OB), R("LBD")))
+        mm(R("B5", 0, 128), R("BDO", 0, 128), R("ID"), True, False)
+        mm(R("B5", 0, 128), R("BDO", 128, 256), R("NID"), False, True)
+        lin(R(LT), R("B5", 0, 128), 0.0, 0.5)
+        lin(R(CO), R(OB, 1, 2), 0.0, 0.5)
+        for a in (0, 4096):
+            dma("s", R("WN", a, a + 528), R("ZB"), 4.0)
 
-        wlook(t, "OW%d" % t, 64, R(A), 32 if t == 0 else WSPLIT)
-
-        def j1():
-            act(R("KJ", 1, 64), R("B1", 0, 63), AF.Relu, 0.0, -64.0)
-            mm(R("B2", 0, 64), R("NID"), R("KJ", 0, 64), False, True)
-        duel(t, 64, R(A), R("NA%d" % t, 1, 65), c128 if t == 0 else c256, j1)
+        duel(t, "OW%d" % t, 64, 32 if t == 0 else WSPLIT, R(A), R("NA%d" % t, 1, 65), c128 if t == 0 else c256)
+        act(R("KJ", 1, 64), R("B1", 0, 63), AF.Relu, 0.0, -64.0)
+        mm(R("B2", 0, 64), R("NID"), R("KJ", 0, 64), False, True)
         scan(R("LF", 1, 65), R("B2", 0, 64), R(A), -2048.0, mx, mn)
         scan(R("NN", 0, 64, -1), R("B2", 0, 64, -1), R("NA%d" % t, 0, 64, -1), -8000.0, mx, mn)
-        ts(R("AL1"), R("B2", 0, 64), 0.0, gt)
+        act(R("AL1"), R("B2", 0, 64), AF.Sign)
         tt(R("ND2"), R("LF", 0, 64, 2), R("NN", 0, 64, 2), add_)
         ts(R("OW2"), R("ND2"), -1.0, mul, 128.0 if t == 0 else c128b, mn)
 
-        ts(R("T1"), R("AL1"), -2 * BIG, mul, 2 * BIG, add_)
-        ts(R("T2"), R("AL1"), -BIG, mul)
-        tt(R("T1", 1, 64, 2), R("T1", 1, 64, 2), R("T2", 0, 64, 2), add_)
-        wlook(t, "OW2", 32, R("LF", 0, 64, 2), 16)
-
-        def j2():
-            tt(R("KL", 0, 64, 2), R("B1", 0, 32), R("T1", 0, 64, 2), AL.is_le)
-            tt(R("KL", 1, 64, 2), R("B1", 0, 32), R("T1", 1, 64, 2), AL.is_le)
-            ts(R("TH"), R("KL"), 2 * BIG, mul)
-            ts(R("AL2", 62, 64), R("KL", 62, 64), 0.5, AL.is_lt)
-            tt(R("TH", 0, 64, 2), R("TH", 0, 64, 2), R("T2", 1, 64, 2), add_)
-            tt(R("ANY", 31, 32), R("AL2", 62, 63), R("AL2", 63, 64), mx)
-            tt(R("TM"), R("TH", 0, 64, 2), R("TH", 1, 64, 2), mn)
-        duel(t, 32, R("LF", 0, 64, 2), R("NN", 0, 64, 2), c128 if t == 0 else c256, j2)
+        lin(R("T1"), R("AL1"), HUGE / 2, -HUGE / 2)
+        lin(R("T2", 0, 64, 2), R("AL1", 1, 64, 2), -BIG / 2, -BIG / 2)
+        lin(R("T3"), R("AL1", 0, 64, 2), -HUGE / 4, -HUGE / 4)
+        tt(R("T1", 1, 64, 2), R("T1", 1, 64, 2), R("T3"), add_)
+        duel(t, "OW2", 32, 16, R("LF", 0, 64, 2), R("NN", 0, 64, 2), c128 if t == 0 else c256)
+        for e in range(2):
+            tt(R("KL", e, 64, 2), R("T1", e, 64, 2), R("B1", 0, 32), sub)
+        tt(R("TH"), R("KL"), R("T2"), mx)
+        tt(R("TM"), R("TH", 0, 64, 2), R("TH", 1, 64, 2), mn)
         mm(R("B0", 0, 32), R("ID32"), R("DUMP"), True, False)
-        tt(R("AL2", 0, 62, 2), R("B2", 1, 32), R("TH", 0, 62, 2), gt)
-        tt(R("AL2", 1, 62, 2), R("B2", 1, 32), R("TH", 1, 62, 2), gt)
-        tt(R("ANY", 0, 31), R("B2", 1, 32), R("TM", 0, 31), gt)
+        for e in range(2):
+            tt(R("AL2", e, 64, 2), R("B2", 1, 33), R("TH", e, 64, 2), gt)
+        tt(R("ANY"), R("B2", 1, 33), R("TM"), gt)
 
         scan(R("CUM"), R("AL2"), R("AL2"), 0.0, add_, mx)
         tt(R("XD"), R("ANY"), R("NDU"), mul)
         mm(R("B0", 0, 32), R("NID"), R("AL2", 0, 64, 2), False, False)
         mm(R("B0", 0, 32), R("ID4"), R("AL2", 1, 64, 2), False, False)
+        mm(R("B4", 0, 1), R("TRI2"), R("CUM", 63, 64), True, True)
         mm(R("B3", 0, 1), R("TRI"), R("CUM", 63, 64), True, True)
-        mm(R("B3", 1, 2), R("TRI2"), R("CUM", 63, 64), True, True)
         mm(R("B0", 0, 32), R("ID"), R("CUM", 1, 64, 2), False, False)
         mm(R("B0", 0, 32), R("ID"), R("CUM", 1, 64, 2), False, False)
         mm(R("B0", 0, 32), R("ID32"), R("XD"), False, True)
-        ts(R("SE", 1, 2), R("B3", 1, 2), -0.5, add_)
+        lin(R("SE", 0, 1), R("B4", 0, 1), -0.5)
         ts(R("OS"), R("B0", 0, 32), R("B3", 0, 1), add_, R("B3", 0, 1), add_)
-        act(R("SGE"), R("NR", 0, 256), AF.Sign, R("SE", 1, 2), -1.0)
-        mm(R("B3", 0, 256), R("BLM8"), R("SGE"), True, True)
+        act(R("SGE"), R("NR", 0, 256), AF.Sign, R("SE", 0, 1), -1.0)
+        mm(R("B3", 0, 256), R("M2"), R("SGE"), True, True)
+        mm(R("B1", 0, 256), R(LT), R("SGE"), True, True)
+        kog = lin(R("OG"), R("B1", 0, 256), R(CO))
+        h1 = cp(IND(R("WN"), R("OS", 0, 12)), R("V%d" % t, 0, 192))
+        h2 = ts(R("OPO", 0, 64), R("B3", 0, 64), 1.0 / 32, mul, cMM, add_)
+        h3 = cp(IND(R("WN"), R("OS", 12, 32)), R("V%d" % t, 192, 512))
+        h4 = ts(R("OPO", 64, 256), R("B3", 64, 256), 1.0 / 32, mul, cMM, add_)
+        hints.append([h1, h2, h3, h4])
         for r in range(16):
-            mm(R("B1", 0, 16), S(r), R("SGE", r, 256, 16), r == 0, r == 15)
-        h1 = cp(IND(R("WN"), R("OS", 0, 10)), R("V%d" % t, 0, 160))
-        h2 = ts(R("OPO"), R("B3", 0, 256), cMM, add_)
-        h3 = cp(IND(R("WN"), R("OS", 10, 16)), R("V%d" % t, 160, 256))
-        h4 = ts(R("PL"), R("B1", 0, 16), -0.5, mul, 8.0, add_)
-        h5 = cp(IND(R("WN"), R("OS", 16, 32)), R("V%d" % t, 256, 512))
-        hints.append([h1, h2, h3, h4, h5])
-        kog = act(R("OG"), IND(R(O, 0, 24), R("PL")))
-        for bk, a, b in (("B6", 0, 32), ("B7", 32, 256)):
-            o = R(bk, 0, b - a)
-            mm(o, R("ID"), R("OG", a, b), True, False)
-            mm(o, R("BE"), R("WN", 2 + 2 * a, 2 + 2 * b, 2), False, False)
-            mm(o, R("BO"), R("WN", 4098 + 2 * a, 4098 + 2 * b, 2), False, False)
-            mm(o, R("BO"), R("WN", 4099 + 2 * a, 4099 + 2 * b, 2), False, False)
-            mm(o, R("BE"), R("WN", 4100 + 2 * a, 4100 + 2 * b, 2), False, True)
-            hints.append([len(ops) - 1, len(ops) + 1 + (6 if a == 0 else 1)])
-            if a == 0:
-                hints.append([len(ops) - 1, len(ops) + 1])
-            cp(R("OTU", a, b), o)
-        o = R("B2", 0, 256)
-        mm(o, S(2, "ZH"), R("SGE"), True, False)
-        mm(o, R("HX"), R("OG"), False, False)
-        mm(o, R("HE"), R("WN", 2, 514, 2), False, False)
-        mm(o, R("HO"), R("WN", 4098, 4610, 2), False, False)
-        mm(o, R("HO"), R("WN", 4099, 4611, 2), False, False)
-        mm(o, R("HE"), R("WN", 4100, 4612, 2), False, True)
-        kxs = act(R("XS", 1, 257), o, AF.Identity, cE3)
+            mm(R("B4", 0, 8), S(r), R("SGE", 2 * r, 256, 32), r == 0, r == 15)
+        kpw = lin(R("PW"), R("B4", 0, 8), 0.0, -64.0)
+
+        def unpack(o, even, odd, b):
+            for l, c in ((even, 2), (odd, 4098), (odd, 4099), (even, 4100)):
+                k = mm(o, R(l), R("WN", c, c + 2 * b, 2), False, c == 4100)
+            return k
+        mm(R("B6", 0, SF), R("ID"), R("OG", 0, SF), True, False)
+        mm(R("B2", 0, 256), S(3, "ZH"), R("SGE"), True, False)
+        mm(R("B2", 0, 256), S(2, "Z0"), R("OG"), False, False)
+        k = unpack(R("B6", 0, SF), "BE", "BO", SF)
+        hints.append([k, k + 2])
+        cp(R("OTU", 0, SF), R("B6", 0, SF))
+        unpack(R("B2", 0, 256), "HE", "HO", 256)
+        kxs = lin(R("XS", 1, 257), R("B2", 0, 256), cE4)
+        mm(R("B7", SF, 256), R("ID"), R("OG", SF, 256), True, False)
+        k = mm(R("B7", SF, 256), R("BE"), R("XS", 1 + SF, 257), False, True)
+        hints.append([k, k + 2])
+        ko = cp(R("OTU", SF, 256), R("B7", SF, 256))
 
         for r in range(16):
             mm(R("B0", 0, 16), S(r, "ZE"), R("XS", 1 + r, 257, 16), r == 0, r == 15)
-        kx = [cp(R("LH"), R("B0", 0, 16)), cp(R("OX"), R("B0", 0, 16))]
-        krx = [act(R("RX", 50 - 17 * e, 408, 51), R("B0", e, 16, 2), AF.Identity, float(TL)) for e in range(2)]
-        kfv = act(R(FV), IND(text, R("OX")), AF.Identity, 255.0, -1.0)
-        kf = send("f%d" % t)
+        kx = [cp(R("LH"), R("B0", 0, 16)), cp(R(OX), R("B0", 0, 16))]
+        krx = [lin(R("RX", 50 - 17 * e, 408, 51), R("B0", e, 16, 2), float(TL)) for e in range(2)]
+        kf = send("x%d" % t)
         for q in range(8):
-            mm(R("B1", 51 * q, 51 * q + 34), R("BE"), R("XS", 32 * q, 32 * q + 34), q == 0, False)
-            mm(R("B1", 51 * q + 34, 51 * q + 51), R("BE"), R("XS", 32 * q + 1, 32 * q + 18), False, False)
+            mm(R("B1", 51 * q, 51 * q + 34), R("BX"), R("XS", 32 * q, 32 * q + 34), q == 0, False)
+            mm(R("B1", 51 * q + 34, 51 * q + 51), R("BX"), R("XS", 32 * q + 1, 32 * q + 18), False, False)
         for i in list(range(33)) + list(range(34, 50)):
             mm(R("B1", i, 408, 51), R("NIH"), R("LH", 1 if i < 34 else 0, 16, 2), False, i == 49)
         kmp = act(R("MP"), R("B1", 0, 408), AF.Abs, 0.0, 8192.0)
         for bk, a, b in (("B3", 0, 51 * SA // 32), ("B7", 51 * SA // 32, 408)):
-            mm(R(bk, a, b), R("IDN4"), R("SG", a, b), True, False)
+            mm(R(bk, a, b), R("ID4"), R("SG", a, b), True, False)
             mm(R(bk, a, b), R("ID"), R("MP", a, b), False, False)
-        for bk in ("B2", "B6", "B0"):
-            mm(R(bk, 0, 256), R("BD"), R("XS", 1, 257), True, False)
-            mm(R(bk, 0, 256), R("NBD"), R("XS", 0, 256), False, False)
-            if bk != "B0":
-                mm(R(bk, 0, 256), R("ID"), R("OG"), False, bk == "B2")
-            if bk == "B2":
-                kpen = act(R("PEN"), R("B2", 0, 256), AF.Relu, 512.0, 1024.0)
-            else:
-                mm(R(bk, 0, 256), R("NID"), R("PEN"), False, False)
-        mm(R("B2", 0, 32), R("ID"), R("PAD"), True, False)
-        mm(R("B2", 32, 160), R("BP"), R("XS", 1, 257, 2), False, False)
-        for r in range(16):
-            mm(R("B2", 192, 200), S(r, "Z2"), R("XS", 1 + 2 * r, 257, 32), False, False)
 
-        cuts = [0, 32, 96, 144, SA, SA + 28, 244, 256]
-        kp, kq, ks = {}, {}, [kf]
+        def dist(o, place, pen):
+            mm(o, R("BD"), R("XS", 1, 257), True, False)
+            mm(o, R("NBD"), R("XS", 0, 256), False, False)
+            if place:
+                mm(o, R("ID"), R("OG"), False, not pen)
+            if pen:
+                mm(o, R("NID"), R("PEN"), False, False)
+        dist(R("B2", 0, 256), True, False)
+        kpen = act(R("PEN"), R("B2", 0, 256), AF.Relu, 512.0, 1024.0)
+        dist(R("B0", 0, 256), False, True)
+        dist(R("B6", 0, 256), True, True)
+        mm(R("B2", 192, 200), R("ID"), R("PW"), True, False)
+        for bk in ("B2", "B1"):
+            mm(R(bk, 0, 32), R("ID"), R("PAD"), bk == "B1", False)
+            mm(R(bk, 32, 160), R("BP"), R("XS", 1, 257, 2), False, False)
+
+        cuts = [0, 64, SF, 144, SA, SA + 28, 244, 256]
+        pcut = [0, 32, 64, 80, 112, 152, SA, SA + 28, 244, 256]
+        kp = [act(R("PX", 16 * a, 16 * b), IND(R(PO), R("OPO", a, b))) for a, b in zip(pcut, pcut[1:])]
+        kq, ks = {}, [kf]
         for a, b in zip(cuts, cuts[1:]):
-            if a < 244:
-                e = b if a <= SA else 256
-                kp[a] = act(R("PX", 16 * a, 16 * e), IND(R(PO), R("OPO", a, e)))
             kq[a] = tt(R("NQ", 16 * a, 16 * b), IND(text, R("OTU", a, b)), R("PX", 16 * a, 16 * b), ne)
         kv = []
-        for a, b, bk, nm, parts in ((0, SA, "B4", "a", [0, 96, 144, SA]), (SA, 256, "B5", "b", [SA, 256])):
-            for u, w in zip(parts, parts[1:]):
+        for a, b, bk, fb, cut in ((0, SA, "B4", "B3", [0, 64, 144, SA]), (SA, 256, "B5", "B7", [SA, 256])):
+            for u, w in zip(cut, cut[1:]):
                 for m in range(16):
                     mm(R(bk, u - a, w - a), S(m, "ZQ"), R("NQ", 16 * u + m, 16 * w, 16), m == 0, m == 15)
             kv.append(ts(R("BAD", 1 + a, 1 + b), R(bk, 0, b - a), -16384.0 * 8.5, AL.is_lt))
             qa, qb = a // 32, b // 32
-            fb = "B3" if a == 0 else "B7"
             for q in range(qa, qb):
                 mm(R(fb, 51 * q, 51 * q + 33), R("BL8"), R("BAD", 32 * q, 32 * q + 33), False, False)
                 mm(R(fb, 51 * q + 34, 51 * q + 50), R("BL8"), R("BAD", 32 * q + 1, 32 * q + 17), False, q == qb - 1)
@@ -517,85 +540,86 @@ def rank_program(g, core, T, topo):
             c = 0 if a == 0 else 16
             for e in range(2):
                 kv.append(ts(R(OA, c + e, c + 2 * (qb - qa), 2), R("SF", 51 * qa + 50 - 17 * e, 51 * qb, 51), cHD[e], mn, cLD[e], mx))
-            ks.append(send("%s%d" % (nm, t)))
+            ks.append(send("%s%d" % ("a" if a == 0 else "b", t)))
             for bk in ("B0", "B6"):
                 mm(R(bk, a, b), R("M1"), R("BAD", 1 + a, 1 + b), False, False)
                 mm(R(bk, a, b), R("M2"), R("BAD", a, b), False, b == 256)
-        hints.append([kp[0], kog, kp[32], kxs, kp[96], kp[144], kp[SA], kfv, kp[SA + 28], kmp] + krx + [kpen])
-        hints.append([kq[32]] + kx + [kq[96], kq[144], kq[SA], kv[0], kq[SA + 28]] + kv[1:4] + [kq[244]] + late[t])
+        hints.append([kog, kp[0], kp[1], kp[2], kxs, kp[3], kpw, kp[4], kp[5], kpen, kp[6], kmp, kp[7]] + krx + [kp[8]])
+        hints.append([kq[0]] + kx + [ko, kq[64], kq[SF], kq[144], kq[SA], kv[0], kq[SA + 28]] + kv[1:4] + [kq[244]])
 
         scan(R("UD"), R("ALT"), R("B0", 0, 256), 0.0, mul, mx)
         act(R("UU"), R("B6", 0, 256), AF.Relu)
-        mm(R("B2", 32, 160), R("BLK"), R("UD", 1, 256, 2), False, False)
+        for bk in ("B1", "B2"):
+            mm(R(bk, 32, 160), R("BLK"), R("UD", 1, 256, 2), False, bk == "B1")
         for r in range(16):
             mm(R("B2", 192, 200), S(r), R("UD", 1 + 2 * r, 256, 32), False, r == 15)
         mm(R("B4", 0, 128), S(0), R("UU", 0, 256, 2), True, False)
         mm(R("B4", 0, 128), S(0), R("UU", 1, 256, 2), False, True)
-        act(R("MV"), R("B4", 0, 128))
+        kmv = lin(R("MV"), R("B4", 0, 128))
+        kn = ts(R("NL"), R("B2", 192, 200), -64.0, mul)
         for c in range(8):
-            ts(R("EQ", 49 * c, 49 * c + 48), R("B2", 16 * c, 16 * c + 48, -1), R("B2", 192 + c, 193 + c), eq)
-        ts(R("EQ", 48, 392, 49), R("B2", 192, 200), 1024.0, add_)
-        scan(R("SC"), R("FL"), R("EQ"), 0.0, mul, mx)
-        cp(R("OF"), R("SC", 48, 392, 49))
-        cp(IND(R("WR"), R("OF")), R("MV"))
+            if c < EA:
+                kmv = act(R("EQ", 49 * c, 49 * c + 48), R("B1", 16 * c, 16 * c + 48, -1), AF.Square, R("NL", c, c + 1), 64.0)
+            else:
+                hints.append([kn, ts(R("EQ", 49 * c, 49 * c + 48), R("B2", 16 * c, 16 * c + 48, -1), R("B2", 192 + c, 193 + c), ne, 4096.0, mul)])
+        ts(R("EQ", 48, 392, 49), R("B2", 192, 200), 1024.0 + WL, add_)
+        scan(R("SC"), R("FL"), R("EQ"), 0.0, add_, mn)
+        named.append([cp(R("OF"), R("SC", 48, 392, 49)), cp(IND(R("WR"), R("OF")), R("MV"))])
 
-        mm(R("B7", 0, 256), R("ID"), R("SGE"), True, False)
-        mm(R("B7", 0, 256), R("NX4"), R("SGE"), False, False)
-        mm(R("B7", 0, 256), R("ID"), R("IX"), False, True)
-        act(R("XX"), R("B7", 0, 256), AF.Relu, cXB, 512.0)
-        mm(R("B7", 0, 256), R("BL8"), R("BAD", 1, 257), True, True)
         mm(R("B5", 0, 256), R("BLK"), R("BAD", 1, 257), True, False)
         mm(R("B5", 0, 256), R("X3"), R("BAD", 1, 257), False, True)
         act(R("LE", 0, 256), R("B5", 0, 256), AF.Sign, -0.5)
-        tt(R("YY"), R("B7", 0, 256), R("XX"), mn)
-        mm(R("B6", 0, 16), R("ID"), R(OB), True, False)
-        mm(R("B6", 0, 16), R("ID"), R(G2), False, False)
-        mm(R("B6", 0, 16), S(0, "ZN"), R(G2), False, False)
-        o, a = R("RM", 0, 1), R("YY")
-        add("v", lambda: g.vector.tensor_reduce(val(o), val(a), AxisListType.X, mx), [a], [o], hold=256 * CY)
-        ts(R("SX", 0, 1), R("RM", 0, 1), -1.0, mul, 256.0, add_)
+        for k, (l, r_) in enumerate((("ID5", "SGE"), ("NX5", "SGE"), ("ID", "IX"), ("BR0", "LE"))):
+            mm(R("B7", 0, 256), R(l), R(r_, 0, 256), k == 0, k == 3)
+        mm(R("B6", 0, 16), R("ID"), places, True, False)
+        mm(R("B6", 0, 16), R("NID"), R(G2), False, False)
+        mm(R("B6", 0, 16), S(0), R(G2), False, False)
+        o, a = R("RM", 0, 1), R("B7", 0, 256)
+        add("v", lambda: g.vector.tensor_reduce(val(o), val(a), AxisListType.X, mx, negate=True), [a], [o])
+        ts(R("SX", 0, 1), R("RM", 0, 1), cSX, add_, 256.0, mn)
         tt(R("HH"), IND(R("LE"), R("SX", 0, 1)), R(G2), mul)
-        mm(R("B6", 0, 16), R("ID"), R("HH"), False, False)
-        mm(R("B6", 0, 16), S(0, "ZN"), R("HH"), False, True)
-        act(R("O%d" % (t + 1), 0, 16), R("B6", 0, 16))
+        mm(R("B6", 0, 16), R("NID"), R("HH"), False, False)
+        mm(R("B6", 0, 16), S(0), R("HH"), False, True)
+        lin(R("OB1", 1, 17) if t == 0 else R("O2"), R("B6", 0, 16))
         return ks
 
     def rows(name):
-        return {"ap": T[name][0:128:16, 0:2048], "reg": [(name, 0, 2048)], "n": 1, "sz": 4}
+        return {"ap": T[name][0:128:16, WL:WL + 2048], "reg": [(name, WL, WL + 2048)], "n": 1, "sz": 4}
 
     def take(t, ks):
-        for nm, k in zip("fab", ks):
-            arrive("%s%d" % (nm, t), k, HOP)
-        flip("TX%d" % (1 - t), "ON%d" % t, "FN%d" % t)
+        for nm, k in zip("xab", ks):
+            arrive("%s%d" % (nm, t), k, HOP + (1.5 if nm == "x" else 0.0))
+        flip("TX%d" % (1 - t), "XN%d" % t, "ON%d" % t, "FN")
 
+    first = R("WR", WL, WL + 2048, 128)
     cp(R("WP", 0, 128), R("WI"))
-    cp(R("O0", 0, 16), R("OI"))
+    cp(R("OB0", 1, 17), R("OI"))
     ms(R("AR"), 0.0)
+    ms(R("ZB"), 0.0)
     starts(0)
     kp_ = send("p", "lt", 1.5)
     starts(1)
-    arrive("s", send("s"), 15.0)
-    arrive("v", send("v"), 30.0)
-    late = [[cp(R("OW1"), R("OWN"))], []]
+    for nm in "vsw":
+        arrive(nm, send(nm), 9.0)
     ms(R("WR", 0, 548), 0.0)
     for a in range(548, 2192, 548):
         dma("s", R("WR", a, a + 548), R("WR", 0, 548), 4.0)
-    dma("s", rows("WR"), R("WP", 0, 128), 8.0)
-    cp(R("W0"), R("WR", 0, 2048, 128))
-    ms(R("WR", 0, 2048, 128), 0.0, "v")
-    arrive("p", kp_, 20.0)
+    dma("s", rows("WR"), R("WP", 0, 128), 6.0)
+    lin(R("W0"), first)
+    lin(first, R("W0"), 0.0, 0.0)
+    arrive("p", kp_, 16.0)
     ks = round_(0)
     take(0, ks)
+    hints.append([named[0][0], calls[0], named[0][1]])
     add("x", None, [], [R("TX0")], "x", ("lt", sent["lt"]), hold=0.0, lat=10.0, after=kp_)
-    flip("TX0", "OA0", "FV0")
+    flip("TX0", "OX0", "OA0", "FV")
     ks = round_(1)
     take(1, ks)
     for h, e in enumerate("sa"):
-        dma(e, X(T.yt[64 * h:64 * h + 64, :], "yt%d" % h), {"ap": T.TX0[64 * h:64 * h + 64, TL:TH], "reg": [("TX0", TL, TH)], "n": 1, "sz": 2}, 3.2)
-        ops[-1]["tail"] = 3.2
-    cp(R("WR", 0, 2048, 128), R("W0"))
-    dma("a", X(T.yo[:], "yo"), R("O2"))
-    dma("s", X(T.yw[:], "yw"), rows("WR"))
+        dma(e, X(T.yt[64 * h:64 * h + 64, :], "yt%d" % h), {"ap": T.TX0[64 * h:64 * h + 64, TL:TH], "reg": [("TX0", TL, TH)], "n": 1, "sz": 2}, 2.8)
+    lin(first, R("W0"))
+    dma("a", X(T.yo[:], "yo"), R("O2"), 2.0)
+    dma("s", X(T.yw[:], "yw"), rows("WR"), 2.0)
 
     def meet(a, b):
         for x in a:
@@ -603,9 +627,14 @@ def rank_program(g, core, T, topo):
                 if x[0] == y[0] and x[1] < y[2] and y[1] < x[2]:
                     if len(x) == 4 and len(y) == 4 and x[3] == y[3] and (x[1] - y[1]) % x[3]:
                         continue
+                    if len(x) + len(y) == 7:
+                        u, w = (x, y) if len(x) == 4 else (y, x)
+                        if u[1] + max(0, -((u[1] - w[1]) // u[3])) * u[3] >= min(w[2], u[2]):
+                            continue
                     return True
         return False
 
+    n = len(ops)
     last = {}
     for i, o in enumerate(ops):
         dep, soft = set(), set()
@@ -628,46 +657,53 @@ def rank_program(g, core, T, topo):
     for h in hints:
         for a, b in zip(h, h[1:]):
             ops[b]["soft"].add(a)
-    topo_, mark = [], set()
+    pre = [[(j, ops[j]["lat"] + WAKE) for j in o["dep"]] + [(j, 0.0) for j in o["soft"] - o["dep"]] for o in ops]
+    post = [[] for _ in ops]
+    for i in range(n):
+        for j, w in pre[i]:
+            post[j].append((i, w))
+    rank_, todo = [], [len(p) for p in pre]
+    ready = [i for i in range(n) if not todo[i]]
+    while ready:
+        i = ready.pop()
+        rank_.append(i)
+        for j, _ in post[i]:
+            todo[j] -= 1
+            if not todo[j]:
+                ready.append(j)
+    at = {i: q for q, i in enumerate(rank_)}
 
-    def visit(i):
-        stack = [(i, False)]
-        while stack:
-            x, done = stack.pop()
-            if done:
-                topo_.append(x)
-            elif x not in mark:
-                mark.add(x)
-                stack.append((x, True))
-                stack.extend((j, False) for j in ops[x]["dep"] | ops[x]["soft"] if j not in mark)
-    for i in range(len(ops)):
-        visit(i)
-    level = [o.get("tail", 0.0) for o in ops]
-    for i in reversed(topo_):
-        o = ops[i]
-        level[i] += o["hold"]
-        for j in o["dep"]:
-            level[j] = max(level[j], level[i] + ops[j]["lat"] + WAKE)
-        for j in o["soft"]:
-            level[j] = max(level[j], level[i] + 1e-6)
-    busy = {}
-    for i in sorted(range(len(ops)), key=lambda x: (-level[x], x)):
-        o = ops[i]
-        t0 = 0.5
-        for j in o["dep"]:
-            t0 = max(t0, ops[j]["end"] + ops[j]["lat"] + WAKE)
-        for j in o["soft"]:
-            t0 = max(t0, ops[j]["end"])
-        line = busy.setdefault(o["e"], [])
-        pos = len(line)
-        for q, (a, b) in enumerate(line):
-            if t0 + o["hold"] <= a + 1e-9:
-                pos = q
-                break
-            t0 = max(t0, b)
-        line.insert(pos, (t0, t0 + o["hold"]))
-        o["t"], o["end"] = t0, t0 + o["hold"]
-    order = sorted(range(len(ops)), key=lambda x: (ops[x]["t"], ops[x]["end"], x))
+    def lay(order, edges, t_first):
+        end, busy = {}, {}
+        for i in order:
+            h = ops[i]["hold"]
+            t0 = max([t_first[i]] + [end[j] + w for j, w in edges[i]])
+            line = busy.setdefault(ops[i]["e"], [])
+            pos = len(line)
+            for q, (a, b) in enumerate(line):
+                if b <= t0:
+                    continue
+                if t0 + h <= a + 1e-9:
+                    pos = q
+                    break
+                t0 = b
+            line.insert(pos, (t0, t0 + h))
+            end[i] = t0 + h
+        return end
+
+    level = [0.0] * n
+    for i in reversed(rank_):
+        level[i] = ops[i]["hold"] + max([ops[i]["lat"]] + [level[j] + w for j, w in post[i]])
+    end = lay(sorted(range(n), key=lambda x: (-level[x], at[x])), pre, [0.5] * n)
+    best = None
+    for _ in range(PASSES):
+        span = max(end[i] + ops[i]["lat"] for i in range(n))
+        if best is None or span < best[0] - 1e-9:
+            best = (span, end)
+        back = lay(sorted(range(n), key=lambda x: (-end[x], -at[x])), post, [o["lat"] for o in ops])
+        end = lay(sorted(range(n), key=lambda x: (-back[x], at[x])), pre, [0.5] * n)
+    end = best[1]
+    order = sorted(range(n), key=lambda x: (end[x] - ops[x]["hold"], end[x], at[x]))
     place = {}
     for q, i in enumerate(order):
         place[i] = q

from concourse.bass import DstId, RemoteDMATransfer
from concourse.mybir import AluOpType as AL, AxisListType, ActivationFunctionType as AF

F, B, U, I, H = "float32", "bfloat16", "uint16", "int32", "float16"
SIZE = {F: 4, B: 2, U: 2, I: 4, H: 2}

OWN = {"TX0": (2112, B), "TX1": (2112, B), "P0": (2048, B), "WP": (136, F), "WR": (2192, F),
       "DG": (2048, B), "GW": (1024, B), "Y": (1024, B), "NJ": (1024, B), "NI": (1024, B), "QI": (1024, B), "WN": (8800, B),
       "PX": (4096, B), "NQ": (4096, B), "CD": (128, I), "WI": (128, I), "OI": (16, I), "AR": (512, B), "ZB": (528, B),
       "SO": (136, F), "SN": (136, F), "VO": (512, B), "V1": (512, B), "OWO": (64, U), "OW1": (64, U),
       "HL0": (128, B), "HL1": (128, B), "O2": (16, F), "OA0": (24, U), "OA1": (24, U), "ON0": (24, U), "ON1": (24, U),
       "OX0": (16, U), "OX1": (16, U), "XN0": (16, U), "XN1": (16, U)}
SMALL = {
    F: {"W0": 16, "KC": 24, "NR": 264, "ID32": 128, "R16": 16, "R32": 16, "RH": 2, "TP": 64,
        "DUMP": 32, "NDU": 32, "RMK": 16, "BT0": 128, "ZT0": 128, "BT1": 128, "ZT1": 128, "A0": 64,
        "ND0": 64, "ND1": 64, "NA0": 72, "LF": 72, "NN": 64, "ND2": 32, "AL1": 64, "T1": 64,
        "T2": 64, "T3": 32, "KL": 64, "TH": 64, "TM": 32, "ANY": 32, "XD": 32, "SE": 8, "SC": 392, "FL": 392,
        "EQ": 392, "NL": 8, "RM": 8, "SF": 408, "RX": 408, "CO0": 1, "CO1": 1},
    B: {"OB0": 32, "OB1": 32, "ID": 128, "NID": 128, "IDB": 128, "ID4": 128, "C256": 128, "ID5": 128, "BLK": 128,
        "BL8": 128, "M2": 128, "TRI": 128, "TRI2": 128, "M1": 128, "HE": 128, "HO": 128, "BX": 128, "BR0": 128, "PW": 8,
        "FV": 256, "FN": 256, "BD": 128, "NBD": 128, "BP": 128, "Z0": 144, "ZE": 144, "ZH": 144, "XS": 264,
        "BE": 128, "BO": 128, "IDB2": 128, "ZQ2": 144, "X3": 128, "X4": 128, "NX5": 128, "Z": 144, "ZQ": 144, "SG": 408,
        "RS": 392, "ALT": 256, "PAD": 32, "IX": 256, "C0": 64, "HALF": 72, "C128": 16, "KJ": 72, "AL2": 64, "CUM": 64,
        "V0": 512, "PO0": 272, "PO1": 272, "BDO": 256, "LT0": 128, "LT1": 128, "SGE": 256, "OG": 256, "PEN": 256,
        "BAD": 264, "UU": 256, "UD": 256, "LE": 264, "G0": 16, "G1": 16, "HH": 16, "MP": 408, "MV": 128},
    U: {"LV": 32, "LBD": 16, "OW0": 64, "OY": 64, "OJ": 64, "OP": 64, "OW2": 32, "OS": 32, "OTU": 256, "OPO": 256,
        "OPT": 16, "SX": 2, "OF": 8},
    I: {"KI": 8},
    H: {"NIH": 128, "LH": 16},
}
SCRATCH = {}
PLACE = {}
for _k, (_n, _d) in OWN.items():
    SCRATCH[_k] = ("sbuf", [128, _n], _d)
    PLACE[_k] = (_k, 0, _n, SIZE[_d])
for _d, _t in SMALL.items():
    _o = 0
    for _k, _n in _t.items():
        PLACE[_k] = ("pool_" + _d, _o, _n, SIZE[_d])
        _o += (_n + 15) // 16 * 16
    SCRATCH["pool_" + _d] = ("sbuf", [128, _o], _d)
for _k in range(8):
    SCRATCH["B%d" % _k] = ("psum", [128, 512], F)
    PLACE["B%d" % _k] = ("B%d" % _k, 0, 512, 4)

for _k, _b, _o, _n in (("AO", "SO", 0, 64), ("NAO", "SO", 64, 72), ("A1", "SN", 0, 64), ("NA1", "SN", 64, 72)):
    PLACE[_k] = (_b, _o, _n, 4)

NDMA = 28
MSG = ["p", "v", "s", "w", "x0", "a0", "b0", "x1", "a1", "b1"]
SEMAPHORES = (["sv", "sa", "st", "sg", "ls", "lt"] + ["r" + m for m in MSG] + ["a" + m for m in MSG]
              + ["d%d" % k for k in range(NDMA)])
BIG, HUGE = 1.0e6, 1.0e9
SA = 192
SF = 96
TL, TH = 32, 2080
WL = 128
WSPLIT = 48
ZI = {64: 32, 32: 8}
EA = 5
PASSES = 4
CY, PE, FIX, WAKE, HOP = 1.0e-3, 0.5e-3, 0.07, 0.11, 3.6


def relays(topo, src, dst):
    c = [x for x in topo.cores_of(src) if x != src and topo.may_write(x, dst)]
    return [x for x in c if topo.die(x) == topo.die(src)] + [x for x in c if topo.die(x) != topo.die(src)]


def messages(T, topo, src):
    n = len(T.cores)
    r = T.rank_of(src)
    prv, nxt = T.cores[(r - 1) % n], T.cores[(r + 1) % n]
    rl = relays(topo, src, nxt)
    wd = (TH - TL) // len(rl)
    out = [("p", c, nxt, ("TX0", TL + k * wd, TL + (k + 1) * wd), ("TX1", TL + k * wd, TL + (k + 1) * wd)) for k, c in enumerate(rl)]
    out += [("v", rl[3], nxt, ("VO", 0, 512), ("V1", 0, 512)), ("s", rl[1], nxt, ("SO", 0, 136), ("SN", 0, 136)),
            ("w", rl[0], nxt, ("OWO", 0, 64), ("OW1", 0, 64))]
    for t, dst in enumerate((nxt, prv)):
        rl = relays(topo, src, dst)
        out += [("x%d" % t, rl[2], dst, ("OX%d" % t, 0, 16), ("XN%d" % t, 0, 16)),
                ("a%d" % t, rl[1], dst, ("OA%d" % t, 0, SA // 16), ("ON%d" % t, 0, SA // 16)),
                ("b%d" % t, rl[0], dst, ("OA%d" % t, 16, 32 - SA // 16), ("ON%d" % t, 16, 32 - SA // 16))]
    return out


def relay_program(g, core, T, topo):
    own = [c for c in topo.cores_of(core) if T.rank_of(c) is not None]
    if not own:
        return
    msgs = messages(T, topo, own[0])
    tot = 0
    for name, via, dst, _, (buf, a, b) in msgs:
        if via != core:
            continue
        share = sum(1 for m in msgs if m[0] == name)
        g.wait_ge(T.sem["r" + name], len(topo.engines(own[0], core)) // share)
        rid, pid = topo.addr(dst, core)
        g.remote_dma(T[buf][:, a:b], T[buf][:, a:b], T.sem["a" + name], T.sem.ls, pid, rid, topo.mask(core, dst))
        tot += len(topo.engines(core, dst))
    if tot:
        g.wait_ge(T.sem.ls, tot)


def rank_program(g, core, T, topo):
    rank = T.rank_of(core)
    if rank is None:
        relay_program(g, core, T, topo)
        return
    ops = []
    Q = {"v": g.vector, "a": g.scalar, "t": g.tensor, "g": g, "s": g.sync}

    def R(name, a=None, b=None, s=1):
        name, o, w, sz = PLACE[name]
        a = o if a is None else a + o
        b = o + w if b is None else b + o
        if s == -1:
            ap = T[name][:, b - 1::-1] if a == 0 else T[name][:, b - 1:a - 1:-1]
        elif s == 1:
            ap = T[name][:, a:b]
        else:
            return {"ap": T[name][:, a:b:s], "reg": [(name, a, b, s)], "n": (b - a + s - 1) // s, "sz": sz}
        return {"ap": ap, "reg": [(name, a, b)], "n": b - a, "sz": sz}

    def IND(win, off):
        return {"ap": win["ap"].indirect(off["ap"]), "reg": win["reg"], "off": off["reg"], "n": 16 * off["n"], "sz": win["sz"]}

    def val(x):
        return x["ap"] if isinstance(x, dict) else x

    def add(e, fn, rd, wr, kind="c", ext=None, hold=None, lat=0.0, after=None):
        r_, w_ = [], []
        rd = [x for x in rd if isinstance(x, dict)]
        for x in rd:
            r_ += x["reg"] + x.get("off", [])
        for x in wr:
            w_ += x["reg"]
            r_ += x.get("off", [])
        if hold is None:
            m = max(x["n"] for x in rd + wr)
            if "off" in wr[0]:
                hold = 0.05 + 3.8 * m * CY
            elif any("off" in x for x in rd):
                hold = 0.06 + 1.56 * m * CY
            elif e == "a":
                hold = FIX + max(64, m) * CY
            else:
                hold = FIX + max(64, m * (0.5 if all(x["sz"] == 2 for x in rd + wr if x["n"] > 1) else 1)) * CY
        ops.append({"e": e, "fn": fn, "r": r_, "w": w_, "k": kind, "ext": ext, "hold": hold, "lat": lat, "after": after})
        return len(ops) - 1

    chain, lasta = [None], [None]

    def tt(o, a, b, op):
        two = "off" not in a and a["reg"][0][0][0] != "B" and b["reg"][0][0][0] != "B"
        k = add("v", lambda: g.vector.tensor_tensor(val(o), val(a), val(b), op), [a, b], [o])
        if two:
            ops[k]["hold"] = FIX + max(64, o["n"] * (1 if o["sz"] == a["sz"] == b["sz"] == 2 else 2)) * CY
        if op == AL.not_equal:
            ops[k]["after"] = chain[0]
            chain[0] = k
        return k

    def ts(o, a, s1, op0, s2=None, op1=None):
        if op1 is None:
            return add("v", lambda: g.vector.tensor_scalar(val(o), val(a), val(s1), None, op0), [a, s1], [o])
        return add("v", lambda: g.vector.tensor_scalar(val(o), val(a), val(s1), val(s2), op0, op1), [a, s1, s2], [o])

    hints = []

    def cp(o, a):
        return add("v", lambda: g.vector.tensor_copy(val(o), val(a)), [a], [o])

    def ms(o, c):
        return iota(o, [[0, o["n"]]], int(c), 0)

    def scan(o, d0, d1, init, op0, op1):
        return add("v", lambda: g.vector.tensor_tensor_scan(val(o), val(d0), val(d1), init, op0, op1), [d0, d1], [o],
                   hold=FIX + max(64, o["n"]) * CY)

    def act(o, a, f=AF.Identity, bias=0.0, scale=1.0):
        return add("a", lambda: g.scalar.activation(val(o), val(a), f, bias=val(bias), scale=val(scale)), [a, bias, scale], [o])

    def lin(o, a, bias=0.0, scale=1.0):
        return act(o, a, AF.Identity, bias, scale)

    def mm(o, l, r_, st, sp):
        return add("t", lambda: g.tensor.matmul(val(o), val(l), val(r_), st, sp), [l, r_], [o],
                   hold=max(64, r_["n"]) * PE * (4 if r_["sz"] == 4 else 1), lat=0.08)

    def iota(o, pat, base, cm, fl=True):
        if fl:
            return add("g", lambda: g.iota(val(o), pat, base, cm, allow_small_or_imprecise_dtypes=True), [], [o], hold=0.13 + 2 * o["n"] * CY)
        return add("g", lambda: g.iota(val(o), pat, base, cm), [], [o], hold=0.13 + 2 * o["n"] * CY)

    def pick(o, a, pat, op, fill, base, cm):
        add("g", lambda: g.affine_select(val(o), val(a), pat, op, fill, base, cm), [a], [o], hold=0.17 + 2 * o["n"] * CY)

    def dma(e, o, a, lat=2.4):
        return add(e, lambda: Q[e].dma_start(val(o), val(a)), [a], [o], "d", hold=0.1, lat=lat)

    def X(ap, name):
        return {"ap": ap, "reg": [(name, 0, 1 << 20)], "n": 1, "sz": 4}

    mine = messages(T, topo, core)
    coming = [m for c in T.cores if c != core for m in messages(T, topo, c) if m[2] == core]
    sent = {"ls": 0, "lt": 0}

    def send(name, sem="ls", hold=0.6):
        parts = [m for m in mine if m[0] == name]
        trs = []
        for k, (_, via, _, s_, d_) in enumerate(parts):
            en = topo.engines(core, via)
            h = len(en) // len(parts)
            rid, pid = topo.addr(via, core)
            trs.append((R(*d_)["ap"], R(*s_)["ap"], pid, rid, sum(1 << e for e in en[k * h:(k + 1) * h])))
            sent[sem] += h
        if len(trs) == 1:
            o, a, pid, rid, m = trs[0]
            fn = lambda: g.remote_dma(o, a, T.sem["r" + name], T.sem[sem], pid, rid, m)
        else:
            tl = [RemoteDMATransfer(dst_ids=[DstId(rid=rid, pnc=pid)], dma_engine_mask=m, remote_sem=T.sem["r" + name], src=a, dst=o)
                  for o, a, pid, rid, m in trs]
            fn = lambda: g.remote_dma_fused(tl, local_sem=T.sem[sem])
        return add("g", fn, [R(*m[3]) for m in parts], [], "r", hold=hold)

    def arrive(name, after, lat):
        parts = [m for m in coming if m[0] == name]
        cnt = sum(len(topo.engines(m[1], core)) for m in parts)
        add("x", None, [], [R(*m[4]) for m in parts], "x", ("a" + name, cnt), hold=0.0, lat=lat, after=after)

    def S(p, z="Z"):
        return R(z, 15 - p, 143 - p)

    def D(p):
        return R("DG", 128 * p, 128 * p + 128)

    cR, cG16, cM1, cK, cM0, c128b, cN128, cBE, cBD, cBN, cBM, cSX, cGS, cNR, cR1, cR2 = [R("KC", k, k + 1) for k in range(16)]
    kK, kR, kG, kH = [R("KI", k, k + 1) for k in range(4)]
    c32, c128, c256 = [R("R32", k, k + 1) for k in (1, 4, 8)]
    cLD, cMM = [cR, R("R16", 1, 2)], R("R16", 8, 9)
    cHD = [R("RH", 0, 1), R("RH", 1, 2)]
    cR0, cE3, cE4 = R("RMK", 0, 1), R("RMK", 3, 4), R("RMK", 4, 5)
    add_, sub, mul, mx, mn = AL.add, AL.subtract, AL.mult, AL.max, AL.min
    ne, gt, ge, eq = AL.not_equal, AL.is_gt, AL.is_ge, AL.is_equal
    N128 = R("NR", 0, 128)

    dma("s", R("CD"), X(T.cd[:], "cd"), 2.0)
    dma("a", R("WI"), X(T.wit[:], "wit"), 2.0)
    dma("s", R("TX0", TL, TH), X(T.txt[:], "txt"), 4.0)
    dma("a", R("P0"), X(T.pat[:], "pat"), 4.0)
    dma("s", R("OI"), X(T.prb[:], "prb"))
    hints.extend([[0, 2, 4], [1, 3]])

    diag = [[1, 128]]
    k1 = iota(kK, [[0, 1]], 0, 1, False)
    k2 = iota(R("NR"), [[1, 264]], 0, 0)
    k3 = iota(cK, [[0, 1]], 0, 1)
    k4 = ms(R("BLK"), 1.0)
    hints.append([k1, k3, k2, k4])
    ms(R("WP", 128, 136), 0.0)
    ts(kR, kK, 15, AL.bitwise_and)
    ts(kG, kK, 112, AL.bitwise_and)
    ts(kH, kK, 4, AL.arith_shift_right, 1, AL.bitwise_and)
    cp(R("KC", 0, 3), R("KI", 1, 4))
    lin(cM0, cM1, 1.0, -1.0)
    ts(R("ID"), N128, cK, eq)
    ts(R("RMK"), R("NR", 0, 16), cR, eq)
    for p in range(8):
        lin(D(p), R("ID"), 0.0, R("RMK", p, p + 1))
    for p in range(8, 16):
        ts(D(p), R("ID"), R("RMK", p, p + 1), mul)
    lin(R("R16", 0, 9), R("NR", 0, 144, 16), cR)
    lin(R("R32", 0, 9), R("NR", 0, 264, 32), 0.0, cR)
    ts(R("Z"), R("NR", 0, 144), cG16, sub, 15.0, eq)
    ts(R("LV"), R("NR", 0, 32), c32, add_)
    ms(R("KJ", 0, 1), 0.0)
    ms(R("LF", 0, 1), -2048.0)
    up, down = [[-16, 8], [0, 16]], [[16, 8], [0, 16]]
    wide = [[1, 144]]
    for nm, c in (("BL8", 8192.0), ("C256", 256.0), ("HALF", 17.0)):
        ms(R(nm), c)
    iota(R("C128"), [[128, 16]], 0, 0)
    iota(R("IX"), [[-1, 256]], 256, 0)
    ts(R("DUMP"), R("NR", 0, 32), c32, add_, 6201.0, add_)
    for o, a, bias, sc in ((c128b, c128, 128.0, 1.0), (cN128, c128, 0.0, -1.0), (cBE, cR0, R("RMK", 1, 2), 1.0), (cBD, cE3, cBE, 4096.0),
                           (cBN, cBD, 0.0, -1.0), (cBM, cE4, cBD, -128.0), (cSX, cR0, 1024.0, -256.0), (cGS, cR0, -0.5, 0.5),
                           (cNR, cR, 0.0, -1.0), (R("KC", 14, 16), R("NR", 1, 3), cR, 1.0), (R("RH"), R("R16", 0, 2), float(TH), 1.0),
                           (R("NDU"), R("DUMP"), 1.0, -1.0)):
        lin(o, a, bias, sc)
    pick(R("BLK"), R("BLK"), up, ge, 0.0, 0, 1)
    pick(R("BLK"), R("BLK"), down, ge, 0.0, 15, -1)
    for nm, of, sc in (("ID32", "ID", 1.0), ("IDB", "ID", 8192.0), ("NID", "ID", -1.0), ("ID4", "ID", 4096.0),
                       ("IDB2", "ID", 8192.0 * 256), ("ZQ2", "Z", -16384.0 * 256), ("ZQ", "Z", -16384.0), ("ZH", "Z", -64.0),
                       ("M2", "BLK", -256.0), ("BD", "BLK", cBM), ("NBD", "BLK", cBN)):
        lin(R(nm), R(of), 0.0, sc)
    for nm, of, pat, op, fill, base, cm in (
            ("TRI", "BLK", diag, gt, 0.0, 0, -1), ("TRI2", "BLK", diag, ge, 0.0, 0, -1), ("X4", "BLK", diag, eq, 0.0, -1, -1),
            ("BE", "BLK", down, ge, 0.0, 1, -1), ("BX", "BLK", down, ge, 0.0, 2, -1), ("BP", "BLK", up, eq, 0.0, -3, 1),
            ("BO", "BLK", up, ge, 0.0, -2, 1), ("BO", "BO", down, ge, 0.0, 3, -1), ("HO", "BO", diag, eq, 0.0, 2, -1),
            ("HE", "BE", diag, eq, 0.0, 0, -1), ("ZE", "Z", wide, ge, 0.0, -13, -1), ("Z0", "Z", wide, eq, 0.0, -15, -1),
            ("BL8", "BL8", up, ge, 0.0, 0, 1), ("BL8", "BL8", down, ge, 0.0, 15, -1), ("ID5", "C256", diag, eq, 0.0, 0, -1),
            ("BR0", "C256", up, eq, 0.0, 0, 1), ("NX5", "M2", diag, eq, 0.0, -1, -1), ("X3", "M2", diag, gt, 0.0, 0, -1),
            ("M1", "X3", diag, ne, 128.0, 0, -1)):
        pick(R(nm), R(of), pat, op, fill, base, cm)
    for h, c in enumerate((cR1, cR2)):
        ts(R("LBD", 8 * h, 8 * h + 8), R("NR", 0, 128, 16), cG16, eq, c, mul)
    cp(R("NIH"), R("NID"))
    for t in range(2):
        ms(R("OB%d" % t), 0.0)
        ms(R("PO%d" % t, 256, 272), 999.0)
    ms(R("PAD"), 8192.0)
    ms(R("T2", 1, 64, 2), 0.0)
    iota(R("ALT"), [[0, 128], [1, 2]], 0, 0)
    iota(R("RS"), [[0, 8], [-1, 49]], 16, 0)
    ts(R("FL"), R("RS"), cR, eq, BIG, mul)
    lin(R("FL", 48, 392, 49), R("NR", 0, 128, 16), cR)
    iota(R("MP"), [[0, 24], [1, 17]], 0, 0)
    pick(R("MP"), R("MP"), [[0, 8], [1, 3], [0, 17]], gt, -100.0, 0, 0)
    act(R("SG"), R("MP"), AF.Sign, cNR)
    ms(R("RX"), 0.0)
    ms(R("RX", 0, 408, 51), BIG)
    ms(R("RX", 34, 408, 51), BIG)
    ms(R("XS", 0, 264, 257), 0.0)
    ms(R("BAD", 0, 1), 1.0)
    ms(R("LE", 256, 264), -1.0)

    def starts(t):
        ND, BT, ZT, HL = [x + str(t) for x in ("ND", "BT", "ZT", "HL")]
        A, NA, OW, V = [x + "0O"[t] for x in ("A", "NA", "OW", "V")]
        ts(R(BT, 0, 64), R("CD", 64 * t, 64 * t + 64), cM0, mul)
        ts(R(BT, 64, 128), R("CD", 64 * t, 64 * t + 64), cM1, mul)
        for q in range(4):
            o, a = R(ZT, 32 * q, 32 * q + 32), R(BT, q, 128, 4)
            add("v", lambda o=o, a=a: g.vector.transpose(val(o), val(a)), [a], [o])
        ms(R(NA, 64, 72), -4000.0)
        if t == 0:
            for q in range(4):
                tt(R(A, 16 * q, 16 * q + 16), R(ZT, 32 * q, 32 * q + 16), R(ZT, 32 * q + 16, 32 * q + 32), add_)
            ms(R(ND, 63, 64), -200.0)
            tt(R(ND, 0, 63), R(A, 0, 63), R(A, 1, 64), sub)
            ts(R(OW), R(ND), -1.0, mul, 128.0, mn)
            lin(R(NA, 0, 64), R(A), 0.0, -1.0)
        else:
            for q in range(8):
                mm(R("B6", 16 * (q // 2), 16 * (q // 2) + 16), R("ID32"), R(ZT, 16 * q, 16 * q + 16), q == 0, q == 7)
            lin(R(A), R("B6", 0, 64))
            lin(R(NA, 0, 64), R(A), cN128, -1.0)
            mm(R("B6", 0, 64), R("ID32"), R(A), True, False)
            mm(R("B6", 0, 64), R("ID32"), R(NA, 1, 65), False, True)
            ts(R(OW), R("B6", 0, 64), -1.0, mul, c128b, mn)
        for h in range(2):
            lin(R(HL, 64 * h, 64 * h + 32), R(A, h, 64, 2))
            mm(R("B7", 32 * h, 32 * h + 32), R("ID32"), R(A, h, 64, 2), h == 0, False)
        for h in range(2):
            mm(R("B7", 32 * h, 32 * h + 32), R("NID"), R(HL, 64 * h, 64 * h + 32), False, h == 1)
        for h in range(2):
            lin(R(HL, 64 * h + 32, 64 * h + 64), R("B7", 32 * h, 32 * h + 32))
        for v in range(4):
            dma("s", {"ap": T.AR[v:128:16, :], "reg": [("AR", v, 512, 4)], "n": 1, "sz": 2}, R(HL, 32 * v, 32 * v + 32), 3.0)
        return act(R(V), IND(R("AR"), R("LV")))

    def duel(t, off, k, h, base, nd, cj):
        win = R("WP", 0, 136) if t == 0 else R("WR", WL, WL + 2056)
        act(R("GW", 0, 16 * h), IND(win, R(off, 0, h)))
        cp(R("GW", 16 * h, 16 * k), IND(win, R(off, h, k)))
        mm(R("B0", 0, k), R("ID32"), base, True, False)
        last = []
        for bk in ("B0", "B4"):
            for p in range(16):
                j = mm(R(bk, 0, k), D(p) if t == 0 else S(p), R("GW", p, 16 * k, 16), bk == "B4" and p == 0, p == 15)
            last += [j - 15, j]
        hints.append(last[1:3])
        cp(R("OY", 0, k), R("B0", 0, k))
        tt(R("TP", 0, k), R("B0", 0, k), nd, add_)
        ts(R("OJ", 0, k), R("TP", 0, k), cj, add_)
        ts(R("OP", 0, k), R("B4", 0, k), c128, add_)
        cuts = [0, 10, 32, 64] if k == 64 else [0, 6, 18, 32]
        for a, b in zip(cuts, cuts[1:]):
            ky = act(R("Y", 16 * a, 16 * b), IND(R("TX%d" % t, TL, TH), R("OY", a, b)))
        kc = act(R("C0", 0, k), R("B4", 0, k), AF.Relu, 32.0, -32.0)
        z = k - ZI[k]
        lasta[0] = act(R("QI", 16 * z, 16 * k), IND(R("P0"), R("OP", z, k)))
        hints.append([ky, lasta[0], kc])
        big = "" if k == 64 else "2"
        mm(R("B1", 0, k), R("IDB" + big), R("HALF", 0, k), True, False)
        mm(R("B2", 0, k + 1), R("IDB"), R("HALF", 0, k + 1), True, False)
        for a, b in zip(cuts, cuts[1:]):
            tt(R("NJ", 16 * a, 16 * b), IND(R("P0"), R("OJ", a, b)), R("Y", 16 * a, 16 * b), ne)
            if a < z:
                e = min(b, z)
                tt(R("NI", 16 * a, 16 * e), IND(R("P0"), R("OP", a, e)), R("Y", 16 * a, 16 * e), ne)
        tt(R("NI", 16 * z, 16 * k), R("QI", 16 * z, 16 * k), R("Y", 16 * z, 16 * k), ne)
        mm(R("B1", 0, k), R("IDB" + big), R("C0", 0, k), False, False)
        mm(R("B2", 0, k), R("IDB"), R("C0", 0, k), False, False)
        for p in range(16):
            mm(R("B1", 0, k), S(p, "ZQ" + big), R("NJ", p, 16 * k, 16), False, p == 15)
        for p in range(16):
            mm(R("B2", 0, k), S(p, "ZQ"), R("NI", p, 16 * k, 16), False, p == 15 and k == 32)

    def flip(tx, may, off, new):
        k = act(R(new), IND(R(tx, TL, TH), R(may)), AF.Identity, 255.0, -1.0)
        for q in range(8):
            c = 2 * q if 32 * q < SA else 16 + 2 * q - SA // 16
            calls.append(cp(IND(R(tx), R(off, c, c + 2)), R(new, 32 * q, 32 * q + 32)))
        return k

    calls, named = [], []

    def round_(t):
        A, OB, PO, G2, TX, OA, OX, LT, CO = [x + str(t) for x in ("A", "OB", "PO", "G", "TX", "OA", "OX", "LT", "CO")]
        text, places = R(TX, TL, TH), R(OB, 1, 17)
        mm(R("B5", 0, 16), R("ID"), places, True, False)
        mm(R("B5", 0, 16), R("ID"), R("C128"), False, True)
        cp(R("OPT"), R("B5", 0, 16))
        kpo = act(R(PO, 0, 256), IND(R("P0"), R("OPT")))
        mm(R("B5", 0, 16), R("X4"), places, True, False)
        mm(R("B5", 0, 16), R("NID"), places, False, True)
        lin(R(G2), R("B5", 0, 16), 0.0, cGS)
        act(R("BDO"), IND(R(OB), R("LBD")))
        mm(R("B5", 0, 128), R("BDO", 0, 128), R("ID"), True, False)
        mm(R("B5", 0, 128), R("BDO", 128, 256), R("NID"), False, True)
        lin(R(LT), R("B5", 0, 128), 0.0, 0.5)
        lin(R(CO), R(OB, 1, 2), 0.0, 0.5)
        for a in (0, 4096):
            dma("s", R("WN", a, a + 528), R("ZB"), 4.0)

        duel(t, "OW%d" % t, 64, 32 if t == 0 else WSPLIT, R(A), R("NA%d" % t, 1, 65), c128 if t == 0 else c256)
        act(R("KJ", 1, 64), R("B1", 0, 63), AF.Relu, 0.0, -64.0)
        mm(R("B2", 0, 64), R("NID"), R("KJ", 0, 64), False, True)
        scan(R("LF", 1, 65), R("B2", 0, 64), R(A), -2048.0, mx, mn)
        scan(R("NN", 0, 64, -1), R("B2", 0, 64, -1), R("NA%d" % t, 0, 64, -1), -8000.0, mx, mn)
        act(R("AL1"), R("B2", 0, 64), AF.Sign)
        tt(R("ND2"), R("LF", 0, 64, 2), R("NN", 0, 64, 2), add_)
        ts(R("OW2"), R("ND2"), -1.0, mul, 128.0 if t == 0 else c128b, mn)

        lin(R("T1"), R("AL1"), HUGE / 2, -HUGE / 2)
        lin(R("T2", 0, 64, 2), R("AL1", 1, 64, 2), -BIG / 2, -BIG / 2)
        lin(R("T3"), R("AL1", 0, 64, 2), -HUGE / 4, -HUGE / 4)
        tt(R("T1", 1, 64, 2), R("T1", 1, 64, 2), R("T3"), add_)
        duel(t, "OW2", 32, 16, R("LF", 0, 64, 2), R("NN", 0, 64, 2), c128 if t == 0 else c256)
        for e in range(2):
            tt(R("KL", e, 64, 2), R("T1", e, 64, 2), R("B1", 0, 32), sub)
        tt(R("TH"), R("KL"), R("T2"), mx)
        tt(R("TM"), R("TH", 0, 64, 2), R("TH", 1, 64, 2), mn)
        mm(R("B0", 0, 32), R("ID32"), R("DUMP"), True, False)
        for e in range(2):
            tt(R("AL2", e, 64, 2), R("B2", 1, 33), R("TH", e, 64, 2), gt)
        tt(R("ANY"), R("B2", 1, 33), R("TM"), gt)

        scan(R("CUM"), R("AL2"), R("AL2"), 0.0, add_, mx)
        tt(R("XD"), R("ANY"), R("NDU"), mul)
        mm(R("B0", 0, 32), R("NID"), R("AL2", 0, 64, 2), False, False)
        mm(R("B0", 0, 32), R("ID4"), R("AL2", 1, 64, 2), False, False)
        mm(R("B4", 0, 1), R("TRI2"), R("CUM", 63, 64), True, True)
        mm(R("B3", 0, 1), R("TRI"), R("CUM", 63, 64), True, True)
        mm(R("B0", 0, 32), R("ID"), R("CUM", 1, 64, 2), False, False)
        mm(R("B0", 0, 32), R("ID"), R("CUM", 1, 64, 2), False, False)
        mm(R("B0", 0, 32), R("ID32"), R("XD"), False, True)
        lin(R("SE", 0, 1), R("B4", 0, 1), -0.5)
        ts(R("OS"), R("B0", 0, 32), R("B3", 0, 1), add_, R("B3", 0, 1), add_)
        act(R("SGE"), R("NR", 0, 256), AF.Sign, R("SE", 0, 1), -1.0)
        mm(R("B3", 0, 256), R("M2"), R("SGE"), True, True)
        mm(R("B1", 0, 256), R(LT), R("SGE"), True, True)
        kog = lin(R("OG"), R("B1", 0, 256), R(CO))
        h1 = cp(IND(R("WN"), R("OS", 0, 12)), R("V%d" % t, 0, 192))
        h2 = ts(R("OPO", 0, 64), R("B3", 0, 64), 1.0 / 32, mul, cMM, add_)
        h3 = cp(IND(R("WN"), R("OS", 12, 32)), R("V%d" % t, 192, 512))
        h4 = ts(R("OPO", 64, 256), R("B3", 64, 256), 1.0 / 32, mul, cMM, add_)
        hints.append([h1, h2, h3, h4])
        for r in range(16):
            mm(R("B4", 0, 8), S(r), R("SGE", 2 * r, 256, 32), r == 0, r == 15)
        kpw = lin(R("PW"), R("B4", 0, 8), 0.0, -64.0)

        def unpack(o, even, odd, b):
            for l, c in ((even, 2), (odd, 4098), (odd, 4099), (even, 4100)):
                k = mm(o, R(l), R("WN", c, c + 2 * b, 2), False, c == 4100)
            return k
        mm(R("B6", 0, SF), R("ID"), R("OG", 0, SF), True, False)
        mm(R("B2", 0, 256), S(3, "ZH"), R("SGE"), True, False)
        mm(R("B2", 0, 256), S(2, "Z0"), R("OG"), False, False)
        k = unpack(R("B6", 0, SF), "BE", "BO", SF)
        hints.append([k, k + 2])
        cp(R("OTU", 0, SF), R("B6", 0, SF))
        unpack(R("B2", 0, 256), "HE", "HO", 256)
        kxs = lin(R("XS", 1, 257), R("B2", 0, 256), cE4)
        mm(R("B7", SF, 256), R("ID"), R("OG", SF, 256), True, False)
        k = mm(R("B7", SF, 256), R("BE"), R("XS", 1 + SF, 257), False, True)
        hints.append([k, k + 2])
        ko = cp(R("OTU", SF, 256), R("B7", SF, 256))

        for r in range(16):
            mm(R("B0", 0, 16), S(r, "ZE"), R("XS", 1 + r, 257, 16), r == 0, r == 15)
        kx = [cp(R("LH"), R("B0", 0, 16)), cp(R(OX), R("B0", 0, 16))]
        krx = [lin(R("RX", 50 - 17 * e, 408, 51), R("B0", e, 16, 2), float(TL)) for e in range(2)]
        kf = send("x%d" % t)
        for q in range(8):
            mm(R("B1", 51 * q, 51 * q + 34), R("BX"), R("XS", 32 * q, 32 * q + 34), q == 0, False)
            mm(R("B1", 51 * q + 34, 51 * q + 51), R("BX"), R("XS", 32 * q + 1, 32 * q + 18), False, False)
        for i in list(range(33)) + list(range(34, 50)):
            mm(R("B1", i, 408, 51), R("NIH"), R("LH", 1 if i < 34 else 0, 16, 2), False, i == 49)
        kmp = act(R("MP"), R("B1", 0, 408), AF.Abs, 0.0, 8192.0)
        for bk, a, b in (("B3", 0, 51 * SA // 32), ("B7", 51 * SA // 32, 408)):
            mm(R(bk, a, b), R("ID4"), R("SG", a, b), True, False)
            mm(R(bk, a, b), R("ID"), R("MP", a, b), False, False)

        def dist(o, place, pen):
            mm(o, R("BD"), R("XS", 1, 257), True, False)
            mm(o, R("NBD"), R("XS", 0, 256), False, False)
            if place:
                mm(o, R("ID"), R("OG"), False, not pen)
            if pen:
                mm(o, R("NID"), R("PEN"), False, False)
        dist(R("B2", 0, 256), True, False)
        kpen = act(R("PEN"), R("B2", 0, 256), AF.Relu, 512.0, 1024.0)
        dist(R("B0", 0, 256), False, True)
        dist(R("B6", 0, 256), True, True)
        mm(R("B2", 192, 200), R("ID"), R("PW"), True, False)
        for bk in ("B2", "B1"):
            mm(R(bk, 0, 32), R("ID"), R("PAD"), bk == "B1", False)
            mm(R(bk, 32, 160), R("BP"), R("XS", 1, 257, 2), False, False)

        cuts = [0, 64, SF, 144, SA, SA + 28, 244, 256]
        pcut = [0, 32, 64, 80, 112, 152, SA, SA + 28, 244, 256]
        kp = [act(R("PX", 16 * a, 16 * b), IND(R(PO), R("OPO", a, b))) for a, b in zip(pcut, pcut[1:])]
        kq, ks = {}, [kf]
        for a, b in zip(cuts, cuts[1:]):
            kq[a] = tt(R("NQ", 16 * a, 16 * b), IND(text, R("OTU", a, b)), R("PX", 16 * a, 16 * b), ne)
        kv = []
        for a, b, bk, fb, cut in ((0, SA, "B4", "B3", [0, 64, 144, SA]), (SA, 256, "B5", "B7", [SA, 256])):
            for u, w in zip(cut, cut[1:]):
                for m in range(16):
                    mm(R(bk, u - a, w - a), S(m, "ZQ"), R("NQ", 16 * u + m, 16 * w, 16), m == 0, m == 15)
            kv.append(ts(R("BAD", 1 + a, 1 + b), R(bk, 0, b - a), -16384.0 * 8.5, AL.is_lt))
            qa, qb = a // 32, b // 32
            for q in range(qa, qb):
                mm(R(fb, 51 * q, 51 * q + 33), R("BL8"), R("BAD", 32 * q, 32 * q + 33), False, False)
                mm(R(fb, 51 * q + 34, 51 * q + 50), R("BL8"), R("BAD", 32 * q + 1, 32 * q + 17), False, q == qb - 1)
            kv.append(scan(R("SF", 51 * qa, 51 * qb), R("RX", 51 * qa, 51 * qb), R(fb, 51 * qa, 51 * qb), 0.0, add_, mn))
            c = 0 if a == 0 else 16
            for e in range(2):
                kv.append(ts(R(OA, c + e, c + 2 * (qb - qa), 2), R("SF", 51 * qa + 50 - 17 * e, 51 * qb, 51), cHD[e], mn, cLD[e], mx))
            ks.append(send("%s%d" % ("a" if a == 0 else "b", t)))
            for bk in ("B0", "B6"):
                mm(R(bk, a, b), R("M1"), R("BAD", 1 + a, 1 + b), False, False)
                mm(R(bk, a, b), R("M2"), R("BAD", a, b), False, b == 256)
        hints.append([kog, kp[0], kp[1], kp[2], kxs, kp[3], kpw, kp[4], kp[5], kpen, kp[6], kmp, kp[7]] + krx + [kp[8]])
        hints.append([kq[0]] + kx + [ko, kq[64], kq[SF], kq[144], kq[SA], kv[0], kq[SA + 28]] + kv[1:4] + [kq[244]])

        scan(R("UD"), R("ALT"), R("B0", 0, 256), 0.0, mul, mx)
        act(R("UU"), R("B6", 0, 256), AF.Relu)
        for bk in ("B1", "B2"):
            mm(R(bk, 32, 160), R("BLK"), R("UD", 1, 256, 2), False, bk == "B1")
        for r in range(16):
            mm(R("B2", 192, 200), S(r), R("UD", 1 + 2 * r, 256, 32), False, r == 15)
        mm(R("B4", 0, 128), S(0), R("UU", 0, 256, 2), True, False)
        mm(R("B4", 0, 128), S(0), R("UU", 1, 256, 2), False, True)
        kmv = lin(R("MV"), R("B4", 0, 128))
        kn = ts(R("NL"), R("B2", 192, 200), -64.0, mul)
        for c in range(8):
            if c < EA:
                kmv = act(R("EQ", 49 * c, 49 * c + 48), R("B1", 16 * c, 16 * c + 48, -1), AF.Square, R("NL", c, c + 1), 64.0)
            else:
                hints.append([kn, ts(R("EQ", 49 * c, 49 * c + 48), R("B2", 16 * c, 16 * c + 48, -1), R("B2", 192 + c, 193 + c), ne, 4096.0, mul)])
        ts(R("EQ", 48, 392, 49), R("B2", 192, 200), 1024.0 + WL, add_)
        scan(R("SC"), R("FL"), R("EQ"), 0.0, add_, mn)
        named.append([cp(R("OF"), R("SC", 48, 392, 49)), cp(IND(R("WR"), R("OF")), R("MV"))])

        mm(R("B5", 0, 256), R("BLK"), R("BAD", 1, 257), True, False)
        mm(R("B5", 0, 256), R("X3"), R("BAD", 1, 257), False, True)
        act(R("LE", 0, 256), R("B5", 0, 256), AF.Sign, -0.5)
        for k, (l, r_) in enumerate((("ID5", "SGE"), ("NX5", "SGE"), ("ID", "IX"), ("BR0", "LE"))):
            mm(R("B7", 0, 256), R(l), R(r_, 0, 256), k == 0, k == 3)
        mm(R("B6", 0, 16), R("ID"), places, True, False)
        mm(R("B6", 0, 16), R("NID"), R(G2), False, False)
        mm(R("B6", 0, 16), S(0), R(G2), False, False)
        o, a = R("RM", 0, 1), R("B7", 0, 256)
        add("v", lambda: g.vector.tensor_reduce(val(o), val(a), AxisListType.X, mx, negate=True), [a], [o])
        ts(R("SX", 0, 1), R("RM", 0, 1), cSX, add_, 256.0, mn)
        tt(R("HH"), IND(R("LE"), R("SX", 0, 1)), R(G2), mul)
        mm(R("B6", 0, 16), R("NID"), R("HH"), False, False)
        mm(R("B6", 0, 16), S(0), R("HH"), False, True)
        lin(R("OB1", 1, 17) if t == 0 else R("O2"), R("B6", 0, 16))
        return ks

    def rows(name):
        return {"ap": T[name][0:128:16, WL:WL + 2048], "reg": [(name, WL, WL + 2048)], "n": 1, "sz": 4}

    def take(t, ks):
        for nm, k in zip("xab", ks):
            arrive("%s%d" % (nm, t), k, HOP + (1.5 if nm == "x" else 0.0))
        flip("TX%d" % (1 - t), "XN%d" % t, "ON%d" % t, "FN")

    first = R("WR", WL, WL + 2048, 128)
    cp(R("WP", 0, 128), R("WI"))
    cp(R("OB0", 1, 17), R("OI"))
    ms(R("AR"), 0.0)
    ms(R("ZB"), 0.0)
    starts(0)
    kp_ = send("p", "lt", 1.5)
    starts(1)
    for nm in "vsw":
        arrive(nm, send(nm), 9.0)
    ms(R("WR", 0, 548), 0.0)
    for a in range(548, 2192, 548):
        dma("s", R("WR", a, a + 548), R("WR", 0, 548), 4.0)
    dma("s", rows("WR"), R("WP", 0, 128), 6.0)
    lin(R("W0"), first)
    lin(first, R("W0"), 0.0, 0.0)
    arrive("p", kp_, 16.0)
    ks = round_(0)
    take(0, ks)
    hints.append([named[0][0], calls[0], named[0][1]])
    add("x", None, [], [R("TX0")], "x", ("lt", sent["lt"]), hold=0.0, lat=10.0, after=kp_)
    flip("TX0", "OX0", "OA0", "FV")
    ks = round_(1)
    take(1, ks)
    for h, e in enumerate("sa"):
        dma(e, X(T.yt[64 * h:64 * h + 64, :], "yt%d" % h), {"ap": T.TX0[64 * h:64 * h + 64, TL:TH], "reg": [("TX0", TL, TH)], "n": 1, "sz": 2}, 2.8)
    lin(first, R("W0"))
    dma("a", X(T.yo[:], "yo"), R("O2"), 2.0)
    dma("s", X(T.yw[:], "yw"), rows("WR"), 2.0)

    def meet(a, b):
        for x in a:
            for y in b:
                if x[0] == y[0] and x[1] < y[2] and y[1] < x[2]:
                    if len(x) == 4 and len(y) == 4 and x[3] == y[3] and (x[1] - y[1]) % x[3]:
                        continue
                    if len(x) + len(y) == 7:
                        u, w = (x, y) if len(x) == 4 else (y, x)
                        if u[1] + max(0, -((u[1] - w[1]) // u[3])) * u[3] >= min(w[2], u[2]):
                            continue
                    return True
        return False

    n = len(ops)
    last = {}
    for i, o in enumerate(ops):
        dep, soft = set(), set()
        for nm in set(x[0] for x in o["r"] + o["w"]):
            bank = nm[0] == "B"
            prev = last.setdefault(nm, [])
            for j in prev:
                p = ops[j]
                if p["e"] == o["e"] == "t":
                    if bank:
                        soft.add(j)
                elif p["k"] == "r":
                    continue
                elif (bank and p["e"] != o["e"]) or meet(p["w"], o["r"]) or meet(p["w"], o["w"]) or meet(p["r"], o["w"]):
                    dep.add(j)
            prev.append(i)
        if o["after"] is not None:
            soft.add(o["after"])
        o["dep"], o["soft"] = dep, soft
    for h in hints:
        for a, b in zip(h, h[1:]):
            ops[b]["soft"].add(a)
    pre = [[(j, ops[j]["lat"] + WAKE) for j in o["dep"]] + [(j, 0.0) for j in o["soft"] - o["dep"]] for o in ops]
    post = [[] for _ in ops]
    for i in range(n):
        for j, w in pre[i]:
            post[j].append((i, w))
    rank_, todo = [], [len(p) for p in pre]
    ready = [i for i in range(n) if not todo[i]]
    while ready:
        i = ready.pop()
        rank_.append(i)
        for j, _ in post[i]:
            todo[j] -= 1
            if not todo[j]:
                ready.append(j)
    at = {i: q for q, i in enumerate(rank_)}

    def lay(order, edges, t_first):
        end, busy = {}, {}
        for i in order:
            h = ops[i]["hold"]
            t0 = max([t_first[i]] + [end[j] + w for j, w in edges[i]])
            line = busy.setdefault(ops[i]["e"], [])
            pos = len(line)
            for q, (a, b) in enumerate(line):
                if b <= t0:
                    continue
                if t0 + h <= a + 1e-9:
                    pos = q
                    break
                t0 = b
            line.insert(pos, (t0, t0 + h))
            end[i] = t0 + h
        return end

    level = [0.0] * n
    for i in reversed(rank_):
        level[i] = ops[i]["hold"] + max([ops[i]["lat"]] + [level[j] + w for j, w in post[i]])
    end = lay(sorted(range(n), key=lambda x: (-level[x], at[x])), pre, [0.5] * n)
    best = None
    for _ in range(PASSES):
        span = max(end[i] + ops[i]["lat"] for i in range(n))
        if best is None or span < best[0] - 1e-9:
            best = (span, end)
        back = lay(sorted(range(n), key=lambda x: (-end[x], -at[x])), post, [o["lat"] for o in ops])
        end = lay(sorted(range(n), key=lambda x: (-back[x], at[x])), pre, [0.5] * n)
    end = best[1]
    order = sorted(range(n), key=lambda x: (end[x] - ops[x]["hold"], end[x], at[x]))
    place = {}
    for q, i in enumerate(order):
        place[i] = q
    seen = {}
    for i in order:
        o = ops[i]
        best = {}
        for j in o["dep"]:
            key = (o["e"], ops[j]["e"] if ops[j]["k"] == "c" else j)
            if key not in best or place[best[key]] < place[j]:
                best[key] = j
        o["wait"] = []
        for key, j in best.items():
            if o["k"] != "x" and seen.get(key, -1) < place[j]:
                seen[key] = place[j]
                o["wait"].append(j)
                ops[j]["sig"] = True
    cnt = {"v": 0, "a": 0, "t": 0, "g": 0}
    nd = 0
    for i in order:
        o = ops[i]
        if o["k"] == "x":
            o["tok"] = (T.sem[o["ext"][0]], o["ext"][1])
            continue
        for j in sorted(o["wait"], key=lambda x: place[x]):
            Q[o["e"]].wait_ge(ops[j]["tok"][0], ops[j]["tok"][1])
        ins = o["fn"]()
        if o["k"] == "d":
            o["tok"] = (T.sem["d%d" % nd], 16)
            nd += 1
            ins.then_inc(o["tok"][0], 16)
        elif o["k"] == "c" and o.get("sig"):
            cnt[o["e"]] += 1
            o["tok"] = (T.sem["s" + o["e"]], cnt[o["e"]])
            ins.then_inc(o["tok"][0], 1)
    g.wait_ge(T.sem.ls, sent["ls"])
    for o in ops:
        if o["k"] == "d" and not o.get("sig"):
            g.wait_ge(o["tok"][0], 16)
